import numpy as np
import ml_dtypes


def mxq(x, axis, fmt="e4m3"):
    dtype, down = {"e4m3": (ml_dtypes.float8_e4m3fn, 7), "e5m2": (ml_dtypes.float8_e5m2, 14)}[fmt]
    v = np.moveaxis(np.asarray(x, np.float32).astype(ml_dtypes.bfloat16).astype(np.float64), axis, -1)
    blocks = v.reshape(v.shape[:-1] + (-1, 32))
    amax = np.abs(blocks).max(-1, keepdims=True)
    byte = np.maximum(np.where(amax > 0, np.frexp(amax)[1] - 1 + 127, 0) - down, 1)
    scale = np.exp2(byte - 127.0)
    codes = (blocks / scale).astype(np.float32).astype(dtype).astype(np.float64)
    return np.moveaxis((codes * scale).reshape(v.shape), -1, axis)


WIDE = False


def mx_kscale(k):
    if not WIDE:
        return np.ones(k)
    levels = np.array([18, -18])
    if k % 512:
        return np.exp2(np.random.permutation(np.resize(levels, k // 32))).repeat(32)
    a = np.empty((k // 512, 16))
    for p in range(k // 512):
        a[p, :8] = np.random.permutation(np.resize(levels, 8))
        for g in range(8):
            far = levels[np.abs(levels - a[p, g]) >= 10]
            a[p, g + 8] = far[np.random.randint(len(far))]
    return np.exp2(a.ravel()).repeat(32)


def f64(x):
    return np.asarray(x).astype(np.float64)


def striped(idx):
    return np.tile(np.asarray(idx).reshape(-1, 16).T, (8, 1)).astype(np.uint16)


def unstriped(offs):
    return offs[:16].T.reshape(-1).astype(np.int64)


B, N, T, D, R = 1, 512, 2048, 512, 512


def setup_inputs():
    n = np.random.standard_normal
    idx = np.random.permutation(T)[:B * N]
    s = mx_kscale(D)[:, None]
    z = mx_kscale(R)[:, None]
    x = n((B, D, R))
    return {
        "xT": (x * s).astype(np.float32),
        "wT": (n((D, T)) * (1.00 / np.sqrt(D)) / s).astype(np.float32),
        "y": n((B, R, N)).astype(np.float32),
        "wt": (np.random.uniform(0.5, 1.5, (B, R, 1)) * 1.0 / np.sqrt(R) * z).astype(np.float32),
        "xm": (x.transpose(0, 2, 1) / z).astype(np.float32),
        "offs": striped(idx),
    }


def reference(xT, wT, y, wt, xm, offs):
    idx = unstriped(offs)
    pick = lambda x: x[:, idx].reshape(x.shape[0], B, N).transpose(1, 0, 2)
    a = mxq(f64(xT), 1, "e4m3").transpose(0, 2, 1) @ mxq(pick(f64(wT)), 1, "e4m3")
    q = a - f64(y)
    g = f64(wt) * q / (1.0 + q * q)
    dw = mxq(f64(xm), 1, "e4m3").transpose(0, 2, 1) @ mxq(g, 1, "e5m2")
    gw = np.zeros((D, T))
    gw[:, idx] = dw.transpose(1, 0, 2).reshape(D, B * N)
    return gw

@@ -1,0 +1,186 @@
+from contextlib import ExitStack
+
+import concourse.mybir as mybir
+
+N, T, D, R = 512, 2048, 512, 512
+FLOPS = 2 * R * D * N * 2
+
+F32 = mybir.dt.float32
+BF16 = mybir.dt.bfloat16
+U32 = mybir.dt.uint32
+U16 = mybir.dt.uint16
+U8 = mybir.dt.uint8
+E4M3 = mybir.dt.float8_e4m3fn_x4
+E5M2 = mybir.dt.float8_e5m2_x4
+ACT = mybir.ActivationFunctionType
+ALU = mybir.AluOpType
+
+P = 128
+PACK = 4
+HALVES = 2
+NH = N // HALVES
+RH = R // HALVES
+
+
+def tile_attend_gcau_w_kernel(tc, xT, wT, y, wt, xm, offs, out):
+    nc = tc.nc
+    with ExitStack() as ctx:
+        keep = ctx.enter_context(tc.tile_pool(name="keep", bufs=1))
+        psum = ctx.enter_context(tc.psum_pool(name="psum", bufs=1))
+
+        offsets = keep.tile([P, N // 16], U16, name="offsets")
+        w_view = wT.rearrange("(p t) c -> p t c", t=PACK)
+        planes = [keep.tile([P, T], F32, name=f"plane{t}") for t in range(PACK)]
+        nc.sync.dma_start(out=planes[0][:], in_=w_view[:, 0, :])
+        nc.sync.dma_start(offsets[:], offs)
+        for t in range(1, PACK):
+            nc.sync.dma_start(out=planes[t][:], in_=w_view[:, t, :])
+        x_view = xT[0].rearrange("(p t) r -> p t r", t=PACK)
+        x_raw = [keep.tile([P, PACK, RH], F32, name=f"x_raw{h}") for h in range(HALVES)]
+        for h in range(HALVES):
+            nc.sync.dma_start(out=x_raw[h][:], in_=x_view[:, :, h * RH:(h + 1) * RH])
+        y_view = y[0].rearrange("(p j) n -> p j n", j=PACK)
+        y_sb = [keep.tile([P, PACK, NH], F32, name=f"y_sb{h}") for h in range(HALVES)]
+        wt_sb = keep.tile([P, PACK], F32, name="wt_sb")
+        nc.sync.dma_start(out=y_sb[0][:], in_=y_view[:, :, 0:NH])
+        nc.sync.dma_start(out=wt_sb[:], in_=wt[0].rearrange("(p j) o -> p (j o)", j=PACK))
+        nc.sync.dma_start(out=y_sb[1][:], in_=y_view[:, :, NH:N])
+        xm_view = xm[0].rearrange("(p j) d -> p j d", j=PACK)
+        xm_raw = [keep.tile([P, PACK, D // HALVES], F32, name=f"xm_raw{h}") for h in range(HALVES)]
+        for h in range(HALVES):
+            nc.sync.dma_start(out=xm_raw[h][:], in_=xm_view[:, :, h * (D // HALVES):(h + 1) * (D // HALVES)])
+
+        warm_in = keep.tile([P, 1], F32, name="warm_in")
+        warm_out = keep.tile([P, 1], F32, name="warm_out")
+        nc.gpsimd.memset(warm_in[:], 1.0)
+        nc.scalar.activation(out=warm_out[:], in_=warm_in[:], func=ACT.Abs_reciprocal_sqrt)
+
+        windows = [keep.tile([P, T], F32, name=f"window{m}") for m in range(D // P)]
+        for win in windows:
+            nc.vector.memset(win[:].bitcast(mybir.dt.int32), 0)
+
+        w_grouped = keep.tile([P, N, PACK], BF16, name="w_grouped", align_bytes=64)
+        for t in range(PACK):
+            nc.vector.tensor_copy(out=w_grouped[:, :, t], in_=planes[t][:].indirect(offsets[:]))
+        w_codes = keep.tile([P, N], U32, name="w_codes", align_bytes=64)
+        w_scales = keep.tile([P, N], U8, name="w_scales", align_bytes=64)
+
+        def quantize_w(h):
+            cols = slice(h * NH, (h + 1) * NH)
+            nc.vector.quantize_mx(out=w_codes[:, cols].bitcast(E4M3), scales=w_scales[:, cols],
+                                  in_=w_grouped[:, cols, :].rearrange("p n t -> p (n t)"))
+
+        quantize_w(0)
+
+        x_grouped = keep.tile([P, PACK, P, PACK], BF16, name="x_grouped", align_bytes=64)
+        for h in range(HALVES):
+            dst = x_grouped[:, :, h * 64:(h + 1) * 64, :].rearrange("p j (c i) t -> p c t i j", i=2)
+            src = x_raw[h][:].rearrange("p t (c i j) -> p c t i j", i=2, j=PACK)
+            if h == 0:
+                nc.scalar.copy(out=dst, in_=src)
+            else:
+                nc.vector.tensor_copy(out=dst, in_=src)
+        x_codes = keep.tile([P, R], U32, name="x_codes", align_bytes=64)
+        x_scales = keep.tile([P, R], U8, name="x_scales", align_bytes=64)
+        nc.vector.quantize_mx(out=x_codes[:].bitcast(E4M3), scales=x_scales[:],
+                              in_=x_grouped[:].rearrange("p j s t -> p (j s t)"))
+        quantize_w(1)
+
+        q = [keep.tile([P, PACK, NH], F32, name=f"q{h}") for h in range(HALVES)]
+        sq = [keep.tile([P, PACK, NH], F32, name=f"sq{h}") for h in range(HALVES)]
+        rs = [keep.tile([P, PACK, NH], F32, name=f"rs{h}") for h in range(HALVES)]
+        u = [keep.tile([P, PACK, NH], F32, name=f"u{h}", tag=f"u{h}") for h in range(HALVES)]
+        for h in range(HALVES):
+            for b in range(2):
+                bank = psum.tile([P, 2, NH], F32, name=f"score{h}{b}")
+                for jj in range(2):
+                    j = 2 * b + jj
+                    nc.tensor.matmul_mx(
+                        out=bank[:, jj, :],
+                        lhsT=x_codes[:, j * P:(j + 1) * P].bitcast(E4M3), lhsT_scale=x_scales[:, j * P:(j + 1) * P],
+                        rhs=w_codes[:, h * NH:(h + 1) * NH].bitcast(E4M3), rhs_scale=w_scales[:, h * NH:(h + 1) * NH],
+                        start=True, stop=True)
+                js = slice(2 * b, 2 * b + 2)
+                nc.vector.tensor_tensor(out=q[h][:, js, :], in0=bank[:], in1=y_sb[h][:, js, :], op=ALU.subtract)
+                nc.scalar.activation(out=sq[h][:, js, :], in_=q[h][:, js, :], func=ACT.Square)
+                nc.scalar.activation(out=rs[h][:, js, :], in_=sq[h][:, js, :], func=ACT.Abs_reciprocal_sqrt, bias=1.0)
+
+        xm_grouped = keep.tile([P, D, PACK], BF16, name="xm_grouped", align_bytes=64)
+        xm_codes = keep.tile([P, D], U32, name="xm_codes", align_bytes=64)
+        xm_scales = keep.tile([P, D], U8, name="xm_scales", align_bytes=64)
+
+        def weave_xm(m):
+            h, off = divmod(m * P, D // HALVES)
+            nc.scalar.copy(
+                out=xm_grouped[:, m * P:(m + 1) * P, :].rearrange("p (c i) t -> p c t i", i=4),
+                in_=xm_raw[h][:, :, off:off + P].rearrange("p t (c i) -> p c t i", i=4))
+
+        def quantize_xm(m):
+            cols = slice(m * P, (m + 1) * P)
+            nc.vector.quantize_mx(out=xm_codes[:, cols].bitcast(E4M3), scales=xm_scales[:, cols],
+                                  in_=xm_grouped[:, cols, :].rearrange("p d t -> p (d t)"))
+
+        g_grouped = keep.tile([P, N, PACK], BF16, name="g_grouped", align_bytes=64)
+        g_codes = keep.tile([P, NH + N], U32, name="g_codes", align_bytes=64)
+        g_scales = keep.tile([P, NH + N], U8, name="g_scales", align_bytes=64)
+        nc.gpsimd.memset(g_codes[:, 0:NH], 0)
+        nc.gpsimd.memset(g_scales[:, 0:NH], 0)
+
+        def weigh(h, j):
+            nc.vector.scalar_tensor_tensor(out=u[h][:, j, :], in0=rs[h][:, j, :], scalar=wt_sb[:, j:j + 1],
+                                           in1=rs[h][:, j, :], op0=ALU.mult, op1=ALU.mult)
+
+        def gradient(h):
+            nc.vector.tensor_tensor(
+                out=g_grouped[:, h * NH:(h + 1) * NH, :].rearrange("p (c i) j -> p c j i", i=4),
+                in0=q[h][:].rearrange("p j (c i) -> p c j i", i=4),
+                in1=u[h][:].rearrange("p j (c i) -> p c j i", i=4), op=ALU.mult)
+
+        def quantize_g(h):
+            cols = slice(h * NH, (h + 1) * NH)
+            dst = slice((h + 1) * NH, (h + 2) * NH)
+            nc.vector.quantize_mx(out=g_codes[:, dst].bitcast(E5M2), scales=g_scales[:, dst],
+                                  in_=g_grouped[:, cols, :].rearrange("p n j -> p (n j)"))
+
+        def product(m, first, tag):
+            cols = slice(m * P, (m + 1) * P)
+            moving = slice(first, first + N)
+            acc = psum.tile([P, N], F32, name=tag)
+            nc.tensor.matmul_mx(out=acc[:], lhsT=xm_codes[:, cols].bitcast(E4M3), lhsT_scale=xm_scales[:, cols],
+                                rhs=g_codes[:, moving].bitcast(E5M2), rhs_scale=g_scales[:, moving],
+                                start=True, stop=True)
+            return acc
+
+        def leave(acc, cols, name):
+            dw = keep.tile([P, cols.stop - cols.start], F32, name=name, tag=name)
+            nc.scalar.copy(out=dw[:], in_=acc[:, cols])
+            return dw
+
+        weave_xm(0)
+        for j in range(PACK):
+            weigh(0, j)
+        gradient(0)
+        quantize_xm(0)
+        quantize_g(0)
+        early_acc = product(0, 0, "acc0")
+        for j in range(PACK):
+            weigh(1, j)
+        gradient(1)
+        quantize_g(1)
+        early = leave(early_acc, slice(NH, N), "u1")
+        nc.vector.tensor_copy(out=windows[0][:].indirect(offsets[:, 0:NH // 16]), in_=early[:])
+        for m in range(1, D // P):
+            weave_xm(m)
+            quantize_xm(m)
+
+        def whole(m):
+            dw = leave(product(m, NH, f"acc{m}"), slice(0, N), f"dw{m}")
+            nc.vector.tensor_copy(out=windows[m][:].indirect(offsets[:]), in_=dw[:])
+            nc.sync.dma_start(out=out[m * P:(m + 1) * P, :], in_=windows[m][:])
+
+        whole(1)
+        late = leave(product(0, NH, "acc0"), slice(NH, N), "dw_late")
+        nc.vector.tensor_copy(out=windows[0][:].indirect(offsets[:, NH // 16:N // 16]), in_=late[:])
+        nc.sync.dma_start(out=out[0:P, :], in_=windows[0][:])
+        whole(2)
+        whole(3)

@@ -7,6 +7,7 @@ FLOPS = 2 * R * D * N * 2
 
 F32 = mybir.dt.float32
 BF16 = mybir.dt.bfloat16
+I32 = mybir.dt.int32
 U32 = mybir.dt.uint32
 U16 = mybir.dt.uint16
 U8 = mybir.dt.uint8
@@ -19,7 +20,9 @@ P = 128
 PACK = 4
 HALVES = 2
 NH = N // HALVES
-RH = R // HALVES
+CH = 128
+CHUNKS = N // CH
+DH = D // HALVES
 
 
 def tile_attend_gcau_w_kernel(tc, xT, wT, y, wt, xm, offs, out):
@@ -29,16 +32,13 @@ def tile_attend_gcau_w_kernel(tc, xT, wT, y, wt, xm, offs, out):
         psum = ctx.enter_context(tc.psum_pool(name="psum", bufs=1))
 
         offsets = keep.tile([P, N // 16], U16, name="offsets")
+        x_raw = keep.tile([P, PACK, R], F32, name="x_raw")
+        nc.sync.dma_start(out=x_raw[:], in_=xT[0].rearrange("(p t) r -> p t r", t=PACK))
+        nc.sync.dma_start(offsets[:], offs)
         w_view = wT.rearrange("(p t) c -> p t c", t=PACK)
         planes = [keep.tile([P, T], F32, name=f"plane{t}") for t in range(PACK)]
-        nc.sync.dma_start(out=planes[0][:], in_=w_view[:, 0, :])
-        nc.sync.dma_start(offsets[:], offs)
-        for t in range(1, PACK):
+        for t in range(PACK):
             nc.sync.dma_start(out=planes[t][:], in_=w_view[:, t, :])
-        x_view = xT[0].rearrange("(p t) r -> p t r", t=PACK)
-        x_raw = [keep.tile([P, PACK, RH], F32, name=f"x_raw{h}") for h in range(HALVES)]
-        for h in range(HALVES):
-            nc.sync.dma_start(out=x_raw[h][:], in_=x_view[:, :, h * RH:(h + 1) * RH])
         y_view = y[0].rearrange("(p j) n -> p j n", j=PACK)
         y_sb = [keep.tile([P, PACK, NH], F32, name=f"y_sb{h}") for h in range(HALVES)]
         wt_sb = keep.tile([P, PACK], F32, name="wt_sb")
@@ -46,9 +46,9 @@ def tile_attend_gcau_w_kernel(tc, xT, wT, y, wt, xm, offs, out):
         nc.sync.dma_start(out=wt_sb[:], in_=wt[0].rearrange("(p j) o -> p (j o)", j=PACK))
         nc.sync.dma_start(out=y_sb[1][:], in_=y_view[:, :, NH:N])
         xm_view = xm[0].rearrange("(p j) d -> p j d", j=PACK)
-        xm_raw = [keep.tile([P, PACK, D // HALVES], F32, name=f"xm_raw{h}") for h in range(HALVES)]
+        xm_raw = [keep.tile([P, PACK, DH], F32, name=f"xm_raw{h}") for h in range(HALVES)]
         for h in range(HALVES):
-            nc.sync.dma_start(out=xm_raw[h][:], in_=xm_view[:, :, h * (D // HALVES):(h + 1) * (D // HALVES)])
+            nc.sync.dma_start(out=xm_raw[h][:], in_=xm_view[:, :, h * DH:(h + 1) * DH])
 
         warm_in = keep.tile([P, 1], F32, name="warm_in")
         warm_out = keep.tile([P, 1], F32, name="warm_out")
@@ -57,84 +57,76 @@ def tile_attend_gcau_w_kernel(tc, xT, wT, y, wt, xm, offs, out):
 
         windows = [keep.tile([P, T], F32, name=f"window{m}") for m in range(D // P)]
         for win in windows:
-            nc.vector.memset(win[:].bitcast(mybir.dt.int32), 0)
+            nc.vector.memset(win[:].bitcast(I32), 0)
+
+        g_codes = keep.tile([P, NH + N], U32, name="g_codes", align_bytes=64)
+        g_scales = keep.tile([P, NH + N], U8, name="g_scales", align_bytes=64)
+        nc.gpsimd.memset(g_codes[:, 0:NH], 0)
+        nc.gpsimd.memset(g_scales[:, 0:NH], 0)
+
+        x_grouped = keep.tile([P, PACK, P, PACK], BF16, name="x_grouped", align_bytes=64)
+        nc.scalar.copy(out=x_grouped[:].rearrange("p j (c i) t -> p c t i j", i=2),
+                       in_=x_raw[:].rearrange("p t (c i j) -> p c t i j", i=2, j=PACK))
+        x_codes = keep.tile([P, R], U32, name="x_codes", align_bytes=64)
+        x_scales = keep.tile([P, R], U8, name="x_scales", align_bytes=64)
+        nc.vector.quantize_mx(out=x_codes[:].bitcast(E4M3), scales=x_scales[:],
+                              in_=x_grouped[:].rearrange("p j s t -> p (j s t)"))
 
         w_grouped = keep.tile([P, N, PACK], BF16, name="w_grouped", align_bytes=64)
-        for t in range(PACK):
-            nc.vector.tensor_copy(out=w_grouped[:, :, t], in_=planes[t][:].indirect(offsets[:]))
         w_codes = keep.tile([P, N], U32, name="w_codes", align_bytes=64)
         w_scales = keep.tile([P, N], U8, name="w_scales", align_bytes=64)
+        for t in range(PACK - 1):
+            nc.vector.tensor_copy(out=w_grouped[:, :, t], in_=planes[t][:].indirect(offsets[:]))
+
+        def half_offsets(h):
+            return offsets[:, h * NH // 16:(h + 1) * NH // 16]
+
+        def gather_last(h):
+            nc.vector.tensor_copy(out=w_grouped[:, h * NH:(h + 1) * NH, PACK - 1],
+                                  in_=planes[PACK - 1][:].indirect(half_offsets(h)))
 
         def quantize_w(h):
             cols = slice(h * NH, (h + 1) * NH)
             nc.vector.quantize_mx(out=w_codes[:, cols].bitcast(E4M3), scales=w_scales[:, cols],
                                   in_=w_grouped[:, cols, :].rearrange("p n t -> p (n t)"))
 
-        quantize_w(0)
-
-        x_grouped = keep.tile([P, PACK, P, PACK], BF16, name="x_grouped", align_bytes=64)
-        for h in range(HALVES):
-            dst = x_grouped[:, :, h * 64:(h + 1) * 64, :].rearrange("p j (c i) t -> p c t i j", i=2)
-            src = x_raw[h][:].rearrange("p t (c i j) -> p c t i j", i=2, j=PACK)
-            if h == 0:
-                nc.scalar.copy(out=dst, in_=src)
-            else:
-                nc.vector.tensor_copy(out=dst, in_=src)
-        x_codes = keep.tile([P, R], U32, name="x_codes", align_bytes=64)
-        x_scales = keep.tile([P, R], U8, name="x_scales", align_bytes=64)
-        nc.vector.quantize_mx(out=x_codes[:].bitcast(E4M3), scales=x_scales[:],
-                              in_=x_grouped[:].rearrange("p j s t -> p (j s t)"))
-        quantize_w(1)
-
         q = [keep.tile([P, PACK, NH], F32, name=f"q{h}") for h in range(HALVES)]
-        sq = [keep.tile([P, PACK, NH], F32, name=f"sq{h}") for h in range(HALVES)]
-        rs = [keep.tile([P, PACK, NH], F32, name=f"rs{h}") for h in range(HALVES)]
-        u = [keep.tile([P, PACK, NH], F32, name=f"u{h}", tag=f"u{h}") for h in range(HALVES)]
-        for h in range(HALVES):
-            for b in range(2):
-                bank = psum.tile([P, 2, NH], F32, name=f"score{h}{b}")
-                for jj in range(2):
-                    j = 2 * b + jj
-                    nc.tensor.matmul_mx(
-                        out=bank[:, jj, :],
-                        lhsT=x_codes[:, j * P:(j + 1) * P].bitcast(E4M3), lhsT_scale=x_scales[:, j * P:(j + 1) * P],
-                        rhs=w_codes[:, h * NH:(h + 1) * NH].bitcast(E4M3), rhs_scale=w_scales[:, h * NH:(h + 1) * NH],
-                        start=True, stop=True)
-                js = slice(2 * b, 2 * b + 2)
-                nc.vector.tensor_tensor(out=q[h][:, js, :], in0=bank[:], in1=y_sb[h][:, js, :], op=ALU.subtract)
-                nc.scalar.activation(out=sq[h][:, js, :], in_=q[h][:, js, :], func=ACT.Square)
-                nc.scalar.activation(out=rs[h][:, js, :], in_=sq[h][:, js, :], func=ACT.Abs_reciprocal_sqrt, bias=1.0)
+        qw = [keep.tile([P, PACK, NH], F32, name=f"qw{h}") for h in range(HALVES)]
+        damp = [keep.tile([P, PACK, CH], F32, name=f"damp{k}", tag=f"damp{k}") for k in range(CHUNKS)]
 
-        xm_grouped = keep.tile([P, D, PACK], BF16, name="xm_grouped", align_bytes=64)
-        xm_codes = keep.tile([P, D], U32, name="xm_codes", align_bytes=64)
-        xm_scales = keep.tile([P, D], U8, name="xm_scales", align_bytes=64)
+        def part(tiles, k):
+            h, c = divmod(k, NH // CH)
+            return tiles[h][:, :, c * CH:(c + 1) * CH]
 
-        def weave_xm(m):
-            h, off = divmod(m * P, D // HALVES)
-            nc.scalar.copy(
-                out=xm_grouped[:, m * P:(m + 1) * P, :].rearrange("p (c i) t -> p c t i", i=4),
-                in_=xm_raw[h][:, :, off:off + P].rearrange("p t (c i) -> p c t i", i=4))
+        def residual(k):
+            cols = slice(k * CH, (k + 1) * CH)
+            bank = psum.tile([P, PACK, CH], F32, name=f"bank{k}", tag=f"bank{k}")
+            for j in range(PACK):
+                nc.tensor.matmul_mx(
+                    out=bank[:, j, :],
+                    lhsT=x_codes[:, j * P:(j + 1) * P].bitcast(E4M3), lhsT_scale=x_scales[:, j * P:(j + 1) * P],
+                    rhs=w_codes[:, cols].bitcast(E4M3), rhs_scale=w_scales[:, cols], start=True, stop=True)
+            nc.vector.tensor_tensor(out=part(q, k), in0=bank[:], in1=part(y_sb, k), op=ALU.subtract)
 
-        def quantize_xm(m):
-            cols = slice(m * P, (m + 1) * P)
-            nc.vector.quantize_mx(out=xm_codes[:, cols].bitcast(E4M3), scales=xm_scales[:, cols],
-                                  in_=xm_grouped[:, cols, :].rearrange("p d t -> p (d t)"))
+        def damping(k):
+            sq = keep.tile([P, PACK, CH], F32, name=f"sq{k}")
+            rs = keep.tile([P, PACK, CH], F32, name=f"rs{k}")
+            nc.scalar.activation(out=sq[:], in_=part(q, k), func=ACT.Square)
+            nc.scalar.activation(out=rs[:], in_=sq[:], func=ACT.Abs_reciprocal_sqrt, bias=1.0)
+            nc.scalar.activation(out=damp[k][:], in_=rs[:], func=ACT.Square)
+
+        def weigh(h):
+            for j in range(PACK):
+                nc.vector.tensor_scalar(out=qw[h][:, j, :], in0=q[h][:, j, :], scalar1=wt_sb[:, j:j + 1],
+                                        scalar2=None, op0=ALU.mult)
 
         g_grouped = keep.tile([P, N, PACK], BF16, name="g_grouped", align_bytes=64)
-        g_codes = keep.tile([P, NH + N], U32, name="g_codes", align_bytes=64)
-        g_scales = keep.tile([P, NH + N], U8, name="g_scales", align_bytes=64)
-        nc.gpsimd.memset(g_codes[:, 0:NH], 0)
-        nc.gpsimd.memset(g_scales[:, 0:NH], 0)
 
-        def weigh(h, j):
-            nc.vector.scalar_tensor_tensor(out=u[h][:, j, :], in0=rs[h][:, j, :], scalar=wt_sb[:, j:j + 1],
-                                           in1=rs[h][:, j, :], op0=ALU.mult, op1=ALU.mult)
-
-        def gradient(h):
+        def gradient(k):
             nc.vector.tensor_tensor(
-                out=g_grouped[:, h * NH:(h + 1) * NH, :].rearrange("p (c i) j -> p c j i", i=4),
-                in0=q[h][:].rearrange("p j (c i) -> p c j i", i=4),
-                in1=u[h][:].rearrange("p j (c i) -> p c j i", i=4), op=ALU.mult)
+                out=g_grouped[:, k * CH:(k + 1) * CH, :].rearrange("p (c i) j -> p c j i", i=4),
+                in0=part(qw, k).rearrange("p j (c i) -> p c j i", i=4),
+                in1=damp[k][:].rearrange("p j (c i) -> p c j i", i=4), op=ALU.mult)
 
         def quantize_g(h):
             cols = slice(h * NH, (h + 1) * NH)
@@ -142,45 +134,68 @@ def tile_attend_gcau_w_kernel(tc, xT, wT, y, wt, xm, offs, out):
             nc.vector.quantize_mx(out=g_codes[:, dst].bitcast(E5M2), scales=g_scales[:, dst],
                                   in_=g_grouped[:, cols, :].rearrange("p n j -> p (n j)"))
 
+        xm_grouped = keep.tile([P, D, PACK], BF16, name="xm_grouped", align_bytes=64)
+        xm_codes = keep.tile([P, D], U32, name="xm_codes", align_bytes=64)
+        xm_scales = keep.tile([P, D], U8, name="xm_scales", align_bytes=64)
+
+        def weave_xm(copy, first, width):
+            h, off = divmod(first, DH)
+            copy(out=xm_grouped[:, first:first + width, :].rearrange("p (c i) t -> p c t i", i=4),
+                 in_=xm_raw[h][:, :, off:off + width].rearrange("p t (c i) -> p c t i", i=4))
+
+        def quantize_xm(h):
+            cols = slice(h * DH, (h + 1) * DH)
+            nc.vector.quantize_mx(out=xm_codes[:, cols].bitcast(E4M3), scales=xm_scales[:, cols],
+                                  in_=xm_grouped[:, cols, :].rearrange("p d t -> p (d t)"))
+
         def product(m, first, tag):
             cols = slice(m * P, (m + 1) * P)
             moving = slice(first, first + N)
-            acc = psum.tile([P, N], F32, name=tag)
+            acc = psum.tile([P, N], F32, name=f"acc_{tag}", tag=tag)
             nc.tensor.matmul_mx(out=acc[:], lhsT=xm_codes[:, cols].bitcast(E4M3), lhsT_scale=xm_scales[:, cols],
                                 rhs=g_codes[:, moving].bitcast(E5M2), rhs_scale=g_scales[:, moving],
                                 start=True, stop=True)
             return acc
 
-        def leave(acc, cols, name):
-            dw = keep.tile([P, cols.stop - cols.start], F32, name=name, tag=name)
+        def place(acc, m, cols, where, tag):
+            dw = keep.tile([P, cols.stop - cols.start], F32, name=f"dw_{tag}", tag=tag)
             nc.scalar.copy(out=dw[:], in_=acc[:, cols])
-            return dw
+            nc.vector.tensor_copy(out=windows[m][:].indirect(where), in_=dw[:])
 
-        weave_xm(0)
-        for j in range(PACK):
-            weigh(0, j)
-        gradient(0)
-        quantize_xm(0)
-        quantize_g(0)
-        early_acc = product(0, 0, "acc0")
-        for j in range(PACK):
-            weigh(1, j)
-        gradient(1)
-        quantize_g(1)
-        early = leave(early_acc, slice(NH, N), "u1")
-        nc.vector.tensor_copy(out=windows[0][:].indirect(offsets[:, 0:NH // 16]), in_=early[:])
-        for m in range(1, D // P):
-            weave_xm(m)
-            quantize_xm(m)
-
-        def whole(m):
-            dw = leave(product(m, NH, f"acc{m}"), slice(0, N), f"dw{m}")
-            nc.vector.tensor_copy(out=windows[m][:].indirect(offsets[:]), in_=dw[:])
+        def store(m):
             nc.sync.dma_start(out=out[m * P:(m + 1) * P, :], in_=windows[m][:])
 
-        whole(1)
-        late = leave(product(0, NH, "acc0"), slice(NH, N), "dw_late")
-        nc.vector.tensor_copy(out=windows[0][:].indirect(offsets[:, NH // 16:N // 16]), in_=late[:])
-        nc.sync.dma_start(out=out[0:P, :], in_=windows[0][:])
-        whole(2)
-        whole(3)
+        gather_last(0)
+        quantize_w(0)
+        gather_last(1)
+        residual(0)
+        damping(0)
+        quantize_w(1)
+        residual(1)
+        damping(1)
+        weigh(0)
+        residual(2)
+        gradient(0)
+        residual(3)
+        weave_xm(nc.vector.tensor_copy, 0, DH)
+        weigh(1)
+        quantize_xm(0)
+        gradient(1)
+        quantize_g(0)
+        early = [product(m, 0, f"early{m}") for m in range(2)]
+        damping(2)
+        place(early[0], 0, slice(NH, N), half_offsets(0), "dw_a")
+        damping(3)
+        gradient(2)
+        gradient(3)
+        quantize_g(1)
+        place(early[1], 1, slice(NH, N), half_offsets(0), "damp3")
+        weave_xm(nc.scalar.copy, DH, DH)
+        for m in range(2):
+            place(product(m, NH, f"bank{m}"), m, slice(NH, N), half_offsets(1), f"dw_late{m}")
+            store(m)
+            if m == 0:
+                quantize_xm(1)
+        for m in range(2, D // P):
+            place(product(m, NH, f"bank{m}"), m, slice(0, N), offsets[:], f"dw{m}")
+            store(m)

@@ -23,6 +23,9 @@ NH = N // HALVES
 CH = 128
 CHUNKS = N // CH
 DH = D // HALVES
+RH = R // HALVES
+SH = RH // PACK
+X_VECTOR = 40
 
 
 def tile_attend_gcau_w_kernel(tc, xT, wT, y, wt, xm, offs, out):
@@ -32,13 +35,16 @@ def tile_attend_gcau_w_kernel(tc, xT, wT, y, wt, xm, offs, out):
         psum = ctx.enter_context(tc.psum_pool(name="psum", bufs=1))
 
         offsets = keep.tile([P, N // 16], U16, name="offsets")
-        x_raw = keep.tile([P, PACK, R], F32, name="x_raw")
-        nc.sync.dma_start(out=x_raw[:], in_=xT[0].rearrange("(p t) r -> p t r", t=PACK))
-        nc.sync.dma_start(offsets[:], offs)
         w_view = wT.rearrange("(p t) c -> p t c", t=PACK)
         planes = [keep.tile([P, T], F32, name=f"plane{t}") for t in range(PACK)]
-        for t in range(PACK):
+        nc.sync.dma_start(out=planes[0][:], in_=w_view[:, 0, :])
+        nc.sync.dma_start(offsets[:], offs)
+        for t in range(1, PACK):
             nc.sync.dma_start(out=planes[t][:], in_=w_view[:, t, :])
+        x_view = xT[0].rearrange("(p t) r -> p t r", t=PACK)
+        x_raw = [keep.tile([P, PACK, RH], F32, name=f"x_raw{h}") for h in range(HALVES)]
+        for h in range(HALVES):
+            nc.sync.dma_start(out=x_raw[h][:], in_=x_view[:, :, h * RH:(h + 1) * RH])
         y_view = y[0].rearrange("(p j) n -> p j n", j=PACK)
         y_sb = [keep.tile([P, PACK, NH], F32, name=f"y_sb{h}") for h in range(HALVES)]
         wt_sb = keep.tile([P, PACK], F32, name="wt_sb")
@@ -56,66 +62,80 @@ def tile_attend_gcau_w_kernel(tc, xT, wT, y, wt, xm, offs, out):
         nc.scalar.activation(out=warm_out[:], in_=warm_in[:], func=ACT.Abs_reciprocal_sqrt)
 
         windows = [keep.tile([P, T], F32, name=f"window{m}") for m in range(D // P)]
-        for win in windows:
-            nc.vector.memset(win[:].bitcast(I32), 0)
+        for m, win in enumerate(windows):
+            (nc.vector if m < 3 else nc.gpsimd).memset(win[:].bitcast(I32), 0)
 
         g_codes = keep.tile([P, NH + N], U32, name="g_codes", align_bytes=64)
         g_scales = keep.tile([P, NH + N], U8, name="g_scales", align_bytes=64)
         nc.gpsimd.memset(g_codes[:, 0:NH], 0)
         nc.gpsimd.memset(g_scales[:, 0:NH], 0)
 
-        x_grouped = keep.tile([P, PACK, P, PACK], BF16, name="x_grouped", align_bytes=64)
-        nc.scalar.copy(out=x_grouped[:].rearrange("p j (c i) t -> p c t i j", i=2),
-                       in_=x_raw[:].rearrange("p t (c i j) -> p c t i j", i=2, j=PACK))
-        x_codes = keep.tile([P, R], U32, name="x_codes", align_bytes=64)
-        x_scales = keep.tile([P, R], U8, name="x_scales", align_bytes=64)
-        nc.vector.quantize_mx(out=x_codes[:].bitcast(E4M3), scales=x_scales[:],
-                              in_=x_grouped[:].rearrange("p j s t -> p (j s t)"))
-
         w_grouped = keep.tile([P, N, PACK], BF16, name="w_grouped", align_bytes=64)
         w_codes = keep.tile([P, N], U32, name="w_codes", align_bytes=64)
         w_scales = keep.tile([P, N], U8, name="w_scales", align_bytes=64)
-        for t in range(PACK - 1):
+        for t in range(PACK):
             nc.vector.tensor_copy(out=w_grouped[:, :, t], in_=planes[t][:].indirect(offsets[:]))
 
         def half_offsets(h):
             return offsets[:, h * NH // 16:(h + 1) * NH // 16]
-
-        def gather_last(h):
-            nc.vector.tensor_copy(out=w_grouped[:, h * NH:(h + 1) * NH, PACK - 1],
-                                  in_=planes[PACK - 1][:].indirect(half_offsets(h)))
 
         def quantize_w(h):
             cols = slice(h * NH, (h + 1) * NH)
             nc.vector.quantize_mx(out=w_codes[:, cols].bitcast(E4M3), scales=w_scales[:, cols],
                                   in_=w_grouped[:, cols, :].rearrange("p n t -> p (n t)"))
 
+        x_grouped = keep.tile([P, PACK, P, PACK], BF16, name="x_grouped", align_bytes=64)
+        x_codes = keep.tile([P, R], U32, name="x_codes", align_bytes=64)
+        x_scales = keep.tile([P, R], U8, name="x_scales", align_bytes=64)
+
+        def weave_x(copy, h, first, last):
+            copy(out=x_grouped[:, :, h * SH + first:h * SH + last, :].rearrange("p j (c i) t -> p c t i j", i=2),
+                 in_=x_raw[h][:, :, first * PACK:last * PACK].rearrange("p t (c i j) -> p c t i j", i=2, j=PACK))
+
+        quantize_w(0)
+        weave_x(nc.scalar.copy, 0, 0, SH)
+        weave_x(nc.vector.tensor_copy, 1, 0, X_VECTOR)
+        weave_x(nc.scalar.copy, 1, X_VECTOR, SH)
+        quantize_w(1)
+        nc.vector.quantize_mx(out=x_codes[:].bitcast(E4M3), scales=x_scales[:],
+                              in_=x_grouped[:].rearrange("p j s t -> p (j s t)"))
+
         q = [keep.tile([P, PACK, NH], F32, name=f"q{h}") for h in range(HALVES)]
-        qw = [keep.tile([P, PACK, NH], F32, name=f"qw{h}") for h in range(HALVES)]
-        damp = [keep.tile([P, PACK, CH], F32, name=f"damp{k}", tag=f"damp{k}") for k in range(CHUNKS)]
+        qw = []
+        damp = [keep.tile([P, PACK, CH], F32, name=f"damp{k}", tag=f"damp{k}", align_bytes=64) for k in range(CHUNKS)]
 
         def part(tiles, k):
             h, c = divmod(k, NH // CH)
             return tiles[h][:, :, c * CH:(c + 1) * CH]
 
-        def residual(k):
+        def residual(k, groups):
             cols = slice(k * CH, (k + 1) * CH)
-            bank = psum.tile([P, PACK, CH], F32, name=f"bank{k}", tag=f"bank{k}")
-            for j in range(PACK):
-                nc.tensor.matmul_mx(
-                    out=bank[:, j, :],
-                    lhsT=x_codes[:, j * P:(j + 1) * P].bitcast(E4M3), lhsT_scale=x_scales[:, j * P:(j + 1) * P],
-                    rhs=w_codes[:, cols].bitcast(E4M3), rhs_scale=w_scales[:, cols], start=True, stop=True)
-            nc.vector.tensor_tensor(out=part(q, k), in0=bank[:], in1=part(y_sb, k), op=ALU.subtract)
+            per = PACK // groups
+            for b in range(groups):
+                bank = psum.tile([P, per, CH], F32, name=f"bank{k}{b}", tag=f"bank{k + CHUNKS * b}")
+                for jj in range(per):
+                    j = b * per + jj
+                    nc.tensor.matmul_mx(
+                        out=bank[:, jj, :],
+                        lhsT=x_codes[:, j * P:(j + 1) * P].bitcast(E4M3), lhsT_scale=x_scales[:, j * P:(j + 1) * P],
+                        rhs=w_codes[:, cols].bitcast(E4M3), rhs_scale=w_scales[:, cols], start=True, stop=True)
+                js = slice(b * per, (b + 1) * per)
+                nc.vector.tensor_tensor(out=part(q, k)[:, js, :], in0=bank[:], in1=part(y_sb, k)[:, js, :],
+                                        op=ALU.subtract)
 
         def damping(k):
             sq = keep.tile([P, PACK, CH], F32, name=f"sq{k}")
             rs = keep.tile([P, PACK, CH], F32, name=f"rs{k}")
-            nc.scalar.activation(out=sq[:], in_=part(q, k), func=ACT.Square)
-            nc.scalar.activation(out=rs[:], in_=sq[:], func=ACT.Abs_reciprocal_sqrt, bias=1.0)
-            nc.scalar.activation(out=damp[k][:], in_=rs[:], func=ACT.Square)
+            pairs = [slice(0, 2), slice(2, 4)]
+            for js in pairs:
+                nc.scalar.activation(out=sq[:, js, :], in_=part(q, k)[:, js, :], func=ACT.Square)
+            for js in pairs:
+                nc.scalar.activation(out=rs[:, js, :], in_=sq[:, js, :], func=ACT.Abs_reciprocal_sqrt, bias=1.0)
+            for js in pairs:
+                nc.scalar.activation(out=damp[k][:, js, :], in_=rs[:, js, :], func=ACT.Square)
 
         def weigh(h):
+            qw.append(keep.tile([P, PACK, NH], F32, name=f"qw{h}", tag="qw"))
             for j in range(PACK):
                 nc.vector.tensor_scalar(out=qw[h][:, j, :], in0=q[h][:, j, :], scalar1=wt_sb[:, j:j + 1],
                                         scalar2=None, op0=ALU.mult)
@@ -124,9 +144,9 @@ def tile_attend_gcau_w_kernel(tc, xT, wT, y, wt, xm, offs, out):
 
         def gradient(k):
             nc.vector.tensor_tensor(
-                out=g_grouped[:, k * CH:(k + 1) * CH, :].rearrange("p (c i) j -> p c j i", i=4),
-                in0=part(qw, k).rearrange("p j (c i) -> p c j i", i=4),
-                in1=damp[k][:].rearrange("p j (c i) -> p c j i", i=4), op=ALU.mult)
+                out=g_grouped[:, k * CH:(k + 1) * CH, :].rearrange("p (c i) j -> p c j i", i=2),
+                in0=part(qw, k).rearrange("p j (c i) -> p c j i", i=2),
+                in1=damp[k][:].rearrange("p j (c i) -> p c j i", i=2), op=ALU.mult)
 
         def quantize_g(h):
             cols = slice(h * NH, (h + 1) * NH)
@@ -134,19 +154,20 @@ def tile_attend_gcau_w_kernel(tc, xT, wT, y, wt, xm, offs, out):
             nc.vector.quantize_mx(out=g_codes[:, dst].bitcast(E5M2), scales=g_scales[:, dst],
                                   in_=g_grouped[:, cols, :].rearrange("p n j -> p (n j)"))
 
-        xm_grouped = keep.tile([P, D, PACK], BF16, name="xm_grouped", align_bytes=64)
         xm_codes = keep.tile([P, D], U32, name="xm_codes", align_bytes=64)
         xm_scales = keep.tile([P, D], U8, name="xm_scales", align_bytes=64)
 
-        def weave_xm(copy, first, width):
+        def weave_xm(copy, first, width, tag):
             h, off = divmod(first, DH)
-            copy(out=xm_grouped[:, first:first + width, :].rearrange("p (c i) t -> p c t i", i=4),
+            grouped = keep.tile([P, width, PACK], BF16, name=f"xm_grouped{first}", tag=tag, align_bytes=64)
+            copy(out=grouped[:].rearrange("p (c i) t -> p c t i", i=4),
                  in_=xm_raw[h][:, :, off:off + width].rearrange("p t (c i) -> p c t i", i=4))
+            return grouped
 
-        def quantize_xm(h):
-            cols = slice(h * DH, (h + 1) * DH)
+        def quantize_xm(grouped, first, width):
+            cols = slice(first, first + width)
             nc.vector.quantize_mx(out=xm_codes[:, cols].bitcast(E4M3), scales=xm_scales[:, cols],
-                                  in_=xm_grouped[:, cols, :].rearrange("p d t -> p (d t)"))
+                                  in_=grouped[:].rearrange("p d t -> p (d t)"))
 
         def product(m, first, tag):
             cols = slice(m * P, (m + 1) * P)
@@ -157,45 +178,43 @@ def tile_attend_gcau_w_kernel(tc, xT, wT, y, wt, xm, offs, out):
                                 start=True, stop=True)
             return acc
 
-        def place(acc, m, cols, where, tag):
-            dw = keep.tile([P, cols.stop - cols.start], F32, name=f"dw_{tag}", tag=tag)
-            nc.scalar.copy(out=dw[:], in_=acc[:, cols])
+        def place(acc, m, cols, where, tag, copy=nc.scalar.copy):
+            dw = keep.tile([P, cols.stop - cols.start], F32, name=f"dw_{tag}", tag=tag, align_bytes=64)
+            copy(out=dw[:], in_=acc[:, cols])
             nc.vector.tensor_copy(out=windows[m][:].indirect(where), in_=dw[:])
 
         def store(m):
             nc.sync.dma_start(out=out[m * P:(m + 1) * P, :], in_=windows[m][:])
 
-        gather_last(0)
-        quantize_w(0)
-        gather_last(1)
-        residual(0)
+        residual(0, 2)
         damping(0)
-        quantize_w(1)
-        residual(1)
+        residual(1, 1)
         damping(1)
         weigh(0)
-        residual(2)
+        residual(2, 1)
+        xm_first = weave_xm(nc.vector.tensor_copy, 0, P, "xm_first")
         gradient(0)
-        residual(3)
-        weave_xm(nc.vector.tensor_copy, 0, DH)
-        weigh(1)
-        quantize_xm(0)
+        quantize_xm(xm_first, 0, P)
         gradient(1)
         quantize_g(0)
-        early = [product(m, 0, f"early{m}") for m in range(2)]
+        residual(3, 1)
+        weigh(1)
+        place(product(0, 0, "early0"), 0, slice(NH, N), half_offsets(0), "dw_a")
         damping(2)
-        place(early[0], 0, slice(NH, N), half_offsets(0), "dw_a")
-        damping(3)
         gradient(2)
+        xm_second = weave_xm(nc.scalar.copy, P, P, "xm_second")
+        damping(3)
+        quantize_xm(xm_second, P, P)
+        early = product(1, 0, "early1")
         gradient(3)
         quantize_g(1)
-        place(early[1], 1, slice(NH, N), half_offsets(0), "damp3")
-        weave_xm(nc.scalar.copy, DH, DH)
+        place(early, 1, slice(NH, N), half_offsets(0), "damp3")
+        xm_last = weave_xm(nc.scalar.copy, DH, DH, "xm_last")
         for m in range(2):
             place(product(m, NH, f"bank{m}"), m, slice(NH, N), half_offsets(1), f"dw_late{m}")
             store(m)
             if m == 0:
-                quantize_xm(1)
+                quantize_xm(xm_last, DH, DH)
         for m in range(2, D // P):
             place(product(m, NH, f"bank{m}"), m, slice(0, N), offsets[:], f"dw{m}")
             store(m)

@@ -23,9 +23,6 @@ NH = N // HALVES
 CH = 128
 CHUNKS = N // CH
 DH = D // HALVES
-RH = R // HALVES
-SH = RH // PACK
-X_VECTOR = 40
 
 
 def tile_attend_gcau_w_kernel(tc, xT, wT, y, wt, xm, offs, out):
@@ -41,20 +38,16 @@ def tile_attend_gcau_w_kernel(tc, xT, wT, y, wt, xm, offs, out):
         nc.sync.dma_start(offsets[:], offs)
         for t in range(1, PACK):
             nc.sync.dma_start(out=planes[t][:], in_=w_view[:, t, :])
-        x_view = xT[0].rearrange("(p t) r -> p t r", t=PACK)
-        x_raw = [keep.tile([P, PACK, RH], F32, name=f"x_raw{h}") for h in range(HALVES)]
-        for h in range(HALVES):
-            nc.sync.dma_start(out=x_raw[h][:], in_=x_view[:, :, h * RH:(h + 1) * RH])
+        x_raw = keep.tile([P, PACK, R], F32, name="x_raw")
+        nc.sync.dma_start(out=x_raw[:], in_=xT[0].rearrange("(p t) r -> p t r", t=PACK))
         y_view = y[0].rearrange("(p j) n -> p j n", j=PACK)
-        y_sb = [keep.tile([P, PACK, NH], F32, name=f"y_sb{h}") for h in range(HALVES)]
+        y_sb = [keep.tile([P, 2, N], F32, name=f"y_sb{u}") for u in range(2)]
         wt_sb = keep.tile([P, PACK], F32, name="wt_sb")
-        nc.sync.dma_start(out=y_sb[0][:], in_=y_view[:, :, 0:NH])
+        nc.sync.dma_start(out=y_sb[0][:], in_=y_view[:, 0:2, :])
+        nc.sync.dma_start(out=y_sb[1][:], in_=y_view[:, 2:4, :])
         nc.sync.dma_start(out=wt_sb[:], in_=wt[0].rearrange("(p j) o -> p (j o)", j=PACK))
-        nc.sync.dma_start(out=y_sb[1][:], in_=y_view[:, :, NH:N])
-        xm_view = xm[0].rearrange("(p j) d -> p j d", j=PACK)
-        xm_raw = [keep.tile([P, PACK, DH], F32, name=f"xm_raw{h}") for h in range(HALVES)]
-        for h in range(HALVES):
-            nc.sync.dma_start(out=xm_raw[h][:], in_=xm_view[:, :, h * DH:(h + 1) * DH])
+        xm_raw = keep.tile([P, PACK, D], F32, name="xm_raw")
+        nc.sync.dma_start(out=xm_raw[:], in_=xm[0].rearrange("(p j) d -> p j d", j=PACK))
 
         warm_in = keep.tile([P, 1], F32, name="warm_in")
         warm_out = keep.tile([P, 1], F32, name="warm_out")
@@ -62,8 +55,8 @@ def tile_attend_gcau_w_kernel(tc, xT, wT, y, wt, xm, offs, out):
         nc.scalar.activation(out=warm_out[:], in_=warm_in[:], func=ACT.Abs_reciprocal_sqrt)
 
         windows = [keep.tile([P, T], F32, name=f"window{m}") for m in range(D // P)]
-        for m, win in enumerate(windows):
-            (nc.vector if m < 3 else nc.gpsimd).memset(win[:].bitcast(I32), 0)
+        for win in windows:
+            nc.vector.memset(win[:].bitcast(I32), 0)
 
         g_codes = keep.tile([P, NH + N], U32, name="g_codes", align_bytes=64)
         g_scales = keep.tile([P, NH + N], U8, name="g_scales", align_bytes=64)
@@ -84,21 +77,25 @@ def tile_attend_gcau_w_kernel(tc, xT, wT, y, wt, xm, offs, out):
             nc.vector.quantize_mx(out=w_codes[:, cols].bitcast(E4M3), scales=w_scales[:, cols],
                                   in_=w_grouped[:, cols, :].rearrange("p n t -> p (n t)"))
 
-        x_grouped = keep.tile([P, PACK, P, PACK], BF16, name="x_grouped", align_bytes=64)
         x_codes = keep.tile([P, R], U32, name="x_codes", align_bytes=64)
         x_scales = keep.tile([P, R], U8, name="x_scales", align_bytes=64)
 
-        def weave_x(copy, h, first, last):
-            copy(out=x_grouped[:, :, h * SH + first:h * SH + last, :].rearrange("p j (c i) t -> p c t i j", i=2),
-                 in_=x_raw[h][:, :, first * PACK:last * PACK].rearrange("p t (c i j) -> p c t i j", i=2, j=PACK))
+        def weave_x(copy, u):
+            grouped = keep.tile([P, 2, P, PACK], BF16, name=f"x_grouped{u}", align_bytes=64)
+            copy(out=grouped[:].rearrange("p e (c i) t -> p c t i e", i=2),
+                 in_=x_raw[:].rearrange("p t (c i j) -> p c t i j", i=2, j=PACK)[:, :, :, :, 2 * u:2 * u + 2])
+            return grouped
+
+        def quantize_x(grouped, u):
+            cols = slice(2 * u * P, (2 * u + 2) * P)
+            nc.vector.quantize_mx(out=x_codes[:, cols].bitcast(E4M3), scales=x_scales[:, cols],
+                                  in_=grouped[:].rearrange("p e s t -> p (e s t)"))
 
         quantize_w(0)
-        weave_x(nc.scalar.copy, 0, 0, SH)
-        weave_x(nc.vector.tensor_copy, 1, 0, X_VECTOR)
-        weave_x(nc.scalar.copy, 1, X_VECTOR, SH)
+        x_grouped = [weave_x(nc.vector.tensor_copy, 0), weave_x(nc.scalar.copy, 1)]
+        quantize_x(x_grouped[0], 0)
+        quantize_x(x_grouped[1], 1)
         quantize_w(1)
-        nc.vector.quantize_mx(out=x_codes[:].bitcast(E4M3), scales=x_scales[:],
-                              in_=x_grouped[:].rearrange("p j s t -> p (j s t)"))
 
         q = [keep.tile([P, PACK, NH], F32, name=f"q{h}") for h in range(HALVES)]
         qw = []
@@ -108,20 +105,19 @@ def tile_attend_gcau_w_kernel(tc, xT, wT, y, wt, xm, offs, out):
             h, c = divmod(k, NH // CH)
             return tiles[h][:, :, c * CH:(c + 1) * CH]
 
-        def residual(k, groups):
-            cols = slice(k * CH, (k + 1) * CH)
-            per = PACK // groups
-            for b in range(groups):
-                bank = psum.tile([P, per, CH], F32, name=f"bank{k}{b}", tag=f"bank{k + CHUNKS * b}")
-                for jj in range(per):
-                    j = b * per + jj
-                    nc.tensor.matmul_mx(
-                        out=bank[:, jj, :],
-                        lhsT=x_codes[:, j * P:(j + 1) * P].bitcast(E4M3), lhsT_scale=x_scales[:, j * P:(j + 1) * P],
-                        rhs=w_codes[:, cols].bitcast(E4M3), rhs_scale=w_scales[:, cols], start=True, stop=True)
-                js = slice(b * per, (b + 1) * per)
-                nc.vector.tensor_tensor(out=part(q, k)[:, js, :], in0=bank[:], in1=part(y_sb, k)[:, js, :],
-                                        op=ALU.subtract)
+        def residual(h, u, pieces):
+            cols = slice(h * NH, (h + 1) * NH)
+            bank = psum.tile([P, 2, NH], F32, name=f"bank{h}{u}", tag=f"bank{2 * h + u}")
+            for e in range(2):
+                j = 2 * u + e
+                nc.tensor.matmul_mx(
+                    out=bank[:, e, :],
+                    lhsT=x_codes[:, j * P:(j + 1) * P].bitcast(E4M3), lhsT_scale=x_scales[:, j * P:(j + 1) * P],
+                    rhs=w_codes[:, cols].bitcast(E4M3), rhs_scale=w_scales[:, cols], start=True, stop=True)
+            width = NH // pieces
+            for c in range(0, NH, width):
+                nc.vector.tensor_tensor(out=q[h][:, 2 * u:2 * u + 2, c:c + width], in0=bank[:, :, c:c + width],
+                                        in1=y_sb[u][:, :, h * NH + c:h * NH + c + width], op=ALU.subtract)
 
         def damping(k):
             sq = keep.tile([P, PACK, CH], F32, name=f"sq{k}")
@@ -158,10 +154,9 @@ def tile_attend_gcau_w_kernel(tc, xT, wT, y, wt, xm, offs, out):
         xm_scales = keep.tile([P, D], U8, name="xm_scales", align_bytes=64)
 
         def weave_xm(copy, first, width, tag):
-            h, off = divmod(first, DH)
             grouped = keep.tile([P, width, PACK], BF16, name=f"xm_grouped{first}", tag=tag, align_bytes=64)
             copy(out=grouped[:].rearrange("p (c i) t -> p c t i", i=4),
-                 in_=xm_raw[h][:, :, off:off + width].rearrange("p t (c i) -> p c t i", i=4))
+                 in_=xm_raw[:, :, first:first + width].rearrange("p t (c i) -> p c t i", i=4))
             return grouped
 
         def quantize_xm(grouped, first, width):
@@ -186,18 +181,18 @@ def tile_attend_gcau_w_kernel(tc, xT, wT, y, wt, xm, offs, out):
         def store(m):
             nc.sync.dma_start(out=out[m * P:(m + 1) * P, :], in_=windows[m][:])
 
-        residual(0, 2)
+        residual(0, 0, 2)
+        residual(0, 1, 2)
         damping(0)
-        residual(1, 1)
         damping(1)
         weigh(0)
-        residual(2, 1)
+        residual(1, 0, 1)
         xm_first = weave_xm(nc.vector.tensor_copy, 0, P, "xm_first")
         gradient(0)
         quantize_xm(xm_first, 0, P)
         gradient(1)
         quantize_g(0)
-        residual(3, 1)
+        residual(1, 1, 1)
         weigh(1)
         place(product(0, 0, "early0"), 0, slice(NH, N), half_offsets(0), "dw_a")
         damping(2)

@@ -55,8 +55,8 @@ def tile_attend_gcau_w_kernel(tc, xT, wT, y, wt, xm, offs, out):
         nc.scalar.activation(out=warm_out[:], in_=warm_in[:], func=ACT.Abs_reciprocal_sqrt)
 
         windows = [keep.tile([P, T], F32, name=f"window{m}") for m in range(D // P)]
-        for win in windows:
-            nc.vector.memset(win[:].bitcast(I32), 0)
+        for m, win in enumerate(windows):
+            (nc.vector if m < 2 else nc.gpsimd).memset(win[:].bitcast(I32), 0)
 
         g_codes = keep.tile([P, NH + N], U32, name="g_codes", align_bytes=64)
         g_scales = keep.tile([P, NH + N], U8, name="g_scales", align_bytes=64)
@@ -64,24 +64,31 @@ def tile_attend_gcau_w_kernel(tc, xT, wT, y, wt, xm, offs, out):
         nc.gpsimd.memset(g_scales[:, 0:NH], 0)
 
         w_grouped = keep.tile([P, N, PACK], BF16, name="w_grouped", align_bytes=64)
-        w_codes = keep.tile([P, N], U32, name="w_codes", align_bytes=64)
+        w_codes = []
         w_scales = keep.tile([P, N], U8, name="w_scales", align_bytes=64)
-        for t in range(PACK):
-            nc.vector.tensor_copy(out=w_grouped[:, :, t], in_=planes[t][:].indirect(offsets[:]))
+        w_listed = keep.tile([P, PACK, N], F32, name="w_listed")
+        for t in range(PACK - 1):
+            nc.vector.tensor_copy(out=w_listed[:, t, :], in_=planes[t][:].indirect(offsets[:]))
+
+        def weave_w(copy, h):
+            cols = slice(h * NH, (h + 1) * NH)
+            copy(out=w_grouped[:, cols, :].rearrange("p (c i) t -> p c t i", i=4),
+                 in_=w_listed[:, :, cols].rearrange("p t (c i) -> p c t i", i=4))
 
         def half_offsets(h):
             return offsets[:, h * NH // 16:(h + 1) * NH // 16]
 
-        def quantize_w(h):
+        def quantize_w(h, tag):
             cols = slice(h * NH, (h + 1) * NH)
-            nc.vector.quantize_mx(out=w_codes[:, cols].bitcast(E4M3), scales=w_scales[:, cols],
+            w_codes.append(keep.tile([P, NH], U32, name=f"w_codes{h}", tag=tag, align_bytes=64))
+            nc.vector.quantize_mx(out=w_codes[h][:].bitcast(E4M3), scales=w_scales[:, cols],
                                   in_=w_grouped[:, cols, :].rearrange("p n t -> p (n t)"))
 
         x_codes = keep.tile([P, R], U32, name="x_codes", align_bytes=64)
         x_scales = keep.tile([P, R], U8, name="x_scales", align_bytes=64)
 
         def weave_x(copy, u):
-            grouped = keep.tile([P, 2, P, PACK], BF16, name=f"x_grouped{u}", align_bytes=64)
+            grouped = keep.tile([P, 2, P, PACK], BF16, name=f"x_grouped{u}", tag=f"x_grouped{u}", align_bytes=64)
             copy(out=grouped[:].rearrange("p e (c i) t -> p c t i e", i=2),
                  in_=x_raw[:].rearrange("p t (c i j) -> p c t i j", i=2, j=PACK)[:, :, :, :, 2 * u:2 * u + 2])
             return grouped
@@ -91,11 +98,16 @@ def tile_attend_gcau_w_kernel(tc, xT, wT, y, wt, xm, offs, out):
             nc.vector.quantize_mx(out=x_codes[:, cols].bitcast(E4M3), scales=x_scales[:, cols],
                                   in_=grouped[:].rearrange("p e s t -> p (e s t)"))
 
-        quantize_w(0)
+        for h in range(HALVES):
+            nc.vector.tensor_copy(out=w_listed[:, PACK - 1, h * NH:(h + 1) * NH],
+                                  in_=planes[PACK - 1][:].indirect(half_offsets(h)))
+        weave_w(nc.scalar.copy, 0)
+        weave_w(nc.vector.tensor_copy, 1)
+        quantize_w(0, "w_codes0")
         x_grouped = [weave_x(nc.vector.tensor_copy, 0), weave_x(nc.scalar.copy, 1)]
         quantize_x(x_grouped[0], 0)
         quantize_x(x_grouped[1], 1)
-        quantize_w(1)
+        quantize_w(1, "x_grouped0")
 
         q = [keep.tile([P, PACK, NH], F32, name=f"q{h}") for h in range(HALVES)]
         qw = []
@@ -113,7 +125,7 @@ def tile_attend_gcau_w_kernel(tc, xT, wT, y, wt, xm, offs, out):
                 nc.tensor.matmul_mx(
                     out=bank[:, e, :],
                     lhsT=x_codes[:, j * P:(j + 1) * P].bitcast(E4M3), lhsT_scale=x_scales[:, j * P:(j + 1) * P],
-                    rhs=w_codes[:, cols].bitcast(E4M3), rhs_scale=w_scales[:, cols], start=True, stop=True)
+                    rhs=w_codes[h][:].bitcast(E4M3), rhs_scale=w_scales[:, cols], start=True, stop=True)
             width = NH // pieces
             for c in range(0, NH, width):
                 nc.vector.tensor_tensor(out=q[h][:, 2 * u:2 * u + 2, c:c + width], in0=bank[:, :, c:c + width],

@@ -64,31 +64,24 @@ def tile_attend_gcau_w_kernel(tc, xT, wT, y, wt, xm, offs, out):
         nc.gpsimd.memset(g_scales[:, 0:NH], 0)
 
         w_grouped = keep.tile([P, N, PACK], BF16, name="w_grouped", align_bytes=64)
-        w_codes = []
+        w_codes = keep.tile([P, N], U32, name="w_codes", align_bytes=64)
         w_scales = keep.tile([P, N], U8, name="w_scales", align_bytes=64)
-        w_listed = keep.tile([P, PACK, N], F32, name="w_listed")
         for t in range(PACK - 1):
-            nc.vector.tensor_copy(out=w_listed[:, t, :], in_=planes[t][:].indirect(offsets[:]))
-
-        def weave_w(copy, h):
-            cols = slice(h * NH, (h + 1) * NH)
-            copy(out=w_grouped[:, cols, :].rearrange("p (c i) t -> p c t i", i=4),
-                 in_=w_listed[:, :, cols].rearrange("p t (c i) -> p c t i", i=4))
+            nc.vector.tensor_copy(out=w_grouped[:, :, t], in_=planes[t][:].indirect(offsets[:]))
 
         def half_offsets(h):
             return offsets[:, h * NH // 16:(h + 1) * NH // 16]
 
-        def quantize_w(h, tag):
+        def quantize_w(h):
             cols = slice(h * NH, (h + 1) * NH)
-            w_codes.append(keep.tile([P, NH], U32, name=f"w_codes{h}", tag=tag, align_bytes=64))
-            nc.vector.quantize_mx(out=w_codes[h][:].bitcast(E4M3), scales=w_scales[:, cols],
+            nc.vector.quantize_mx(out=w_codes[:, cols].bitcast(E4M3), scales=w_scales[:, cols],
                                   in_=w_grouped[:, cols, :].rearrange("p n t -> p (n t)"))
 
         x_codes = keep.tile([P, R], U32, name="x_codes", align_bytes=64)
         x_scales = keep.tile([P, R], U8, name="x_scales", align_bytes=64)
 
         def weave_x(copy, u):
-            grouped = keep.tile([P, 2, P, PACK], BF16, name=f"x_grouped{u}", tag=f"x_grouped{u}", align_bytes=64)
+            grouped = keep.tile([P, 2, P, PACK], BF16, name=f"x_grouped{u}", align_bytes=64)
             copy(out=grouped[:].rearrange("p e (c i) t -> p c t i e", i=2),
                  in_=x_raw[:].rearrange("p t (c i j) -> p c t i j", i=2, j=PACK)[:, :, :, :, 2 * u:2 * u + 2])
             return grouped
@@ -98,16 +91,15 @@ def tile_attend_gcau_w_kernel(tc, xT, wT, y, wt, xm, offs, out):
             nc.vector.quantize_mx(out=x_codes[:, cols].bitcast(E4M3), scales=x_scales[:, cols],
                                   in_=grouped[:].rearrange("p e s t -> p (e s t)"))
 
-        for h in range(HALVES):
-            nc.vector.tensor_copy(out=w_listed[:, PACK - 1, h * NH:(h + 1) * NH],
-                                  in_=planes[PACK - 1][:].indirect(half_offsets(h)))
-        weave_w(nc.scalar.copy, 0)
-        weave_w(nc.vector.tensor_copy, 1)
-        quantize_w(0, "w_codes0")
+        last_listed = keep.tile([P, NH], F32, name="last_listed")
+        nc.vector.tensor_copy(out=last_listed[:], in_=planes[PACK - 1][:].indirect(half_offsets(0)))
+        nc.scalar.copy(out=w_grouped[:, 0:NH, PACK - 1], in_=last_listed[:])
+        nc.vector.tensor_copy(out=w_grouped[:, NH:N, PACK - 1], in_=planes[PACK - 1][:].indirect(half_offsets(1)))
+        quantize_w(0)
+        quantize_w(1)
         x_grouped = [weave_x(nc.vector.tensor_copy, 0), weave_x(nc.scalar.copy, 1)]
         quantize_x(x_grouped[0], 0)
         quantize_x(x_grouped[1], 1)
-        quantize_w(1, "x_grouped0")
 
         q = [keep.tile([P, PACK, NH], F32, name=f"q{h}") for h in range(HALVES)]
         qw = []
@@ -117,19 +109,17 @@ def tile_attend_gcau_w_kernel(tc, xT, wT, y, wt, xm, offs, out):
             h, c = divmod(k, NH // CH)
             return tiles[h][:, :, c * CH:(c + 1) * CH]
 
-        def residual(h, u, pieces):
-            cols = slice(h * NH, (h + 1) * NH)
-            bank = psum.tile([P, 2, NH], F32, name=f"bank{h}{u}", tag=f"bank{2 * h + u}")
+        def residual(h, u, first, width, tag):
+            cols = slice(h * NH + first, h * NH + first + width)
+            bank = psum.tile([P, 2, width], F32, name=f"scores_{tag}", tag=tag)
             for e in range(2):
                 j = 2 * u + e
                 nc.tensor.matmul_mx(
                     out=bank[:, e, :],
                     lhsT=x_codes[:, j * P:(j + 1) * P].bitcast(E4M3), lhsT_scale=x_scales[:, j * P:(j + 1) * P],
-                    rhs=w_codes[h][:].bitcast(E4M3), rhs_scale=w_scales[:, cols], start=True, stop=True)
-            width = NH // pieces
-            for c in range(0, NH, width):
-                nc.vector.tensor_tensor(out=q[h][:, 2 * u:2 * u + 2, c:c + width], in0=bank[:, :, c:c + width],
-                                        in1=y_sb[u][:, :, h * NH + c:h * NH + c + width], op=ALU.subtract)
+                    rhs=w_codes[:, cols].bitcast(E4M3), rhs_scale=w_scales[:, cols], start=True, stop=True)
+            nc.vector.tensor_tensor(out=q[h][:, 2 * u:2 * u + 2, first:first + width], in0=bank[:],
+                                    in1=y_sb[u][:, :, cols], op=ALU.subtract)
 
         def damping(k):
             sq = keep.tile([P, PACK, CH], F32, name=f"sq{k}")
@@ -193,18 +183,19 @@ def tile_attend_gcau_w_kernel(tc, xT, wT, y, wt, xm, offs, out):
         def store(m):
             nc.sync.dma_start(out=out[m * P:(m + 1) * P, :], in_=windows[m][:])
 
-        residual(0, 0, 2)
-        residual(0, 1, 2)
+        for u in range(2):
+            for c in range(2):
+                residual(0, u, c * CH, CH, f"bank{2 * u + c}")
         damping(0)
         damping(1)
         weigh(0)
-        residual(1, 0, 1)
+        residual(1, 0, 0, NH, "bank4")
         xm_first = weave_xm(nc.vector.tensor_copy, 0, P, "xm_first")
         gradient(0)
         quantize_xm(xm_first, 0, P)
         gradient(1)
         quantize_g(0)
-        residual(1, 1, 1)
+        residual(1, 1, 0, NH, "bank5")
         weigh(1)
         place(product(0, 0, "early0"), 0, slice(NH, N), half_offsets(0), "dw_a")
         damping(2)

@@ -18,11 +18,12 @@ ALU = mybir.AluOpType
 
 P = 128
 PACK = 4
+PAIRS = PACK // 2
 HALVES = 2
 NH = N // HALVES
 CH = 128
 CHUNKS = N // CH
-DH = D // HALVES
+EARLY = 2
 
 
 def tile_attend_gcau_w_kernel(tc, xT, wT, y, wt, xm, offs, out):
@@ -41,10 +42,10 @@ def tile_attend_gcau_w_kernel(tc, xT, wT, y, wt, xm, offs, out):
         x_raw = keep.tile([P, PACK, R], F32, name="x_raw")
         nc.sync.dma_start(out=x_raw[:], in_=xT[0].rearrange("(p t) r -> p t r", t=PACK))
         y_view = y[0].rearrange("(p j) n -> p j n", j=PACK)
-        y_sb = [keep.tile([P, 2, N], F32, name=f"y_sb{u}") for u in range(2)]
+        y_sb = [keep.tile([P, 2, N], F32, name=f"y_sb{u}") for u in range(PAIRS)]
         wt_sb = keep.tile([P, PACK], F32, name="wt_sb")
-        nc.sync.dma_start(out=y_sb[0][:], in_=y_view[:, 0:2, :])
-        nc.sync.dma_start(out=y_sb[1][:], in_=y_view[:, 2:4, :])
+        for u in range(PAIRS):
+            nc.sync.dma_start(out=y_sb[u][:], in_=y_view[:, 2 * u:2 * u + 2, :])
         nc.sync.dma_start(out=wt_sb[:], in_=wt[0].rearrange("(p j) o -> p (j o)", j=PACK))
         xm_raw = keep.tile([P, PACK, D], F32, name="xm_raw")
         nc.sync.dma_start(out=xm_raw[:], in_=xm[0].rearrange("(p j) d -> p j d", j=PACK))
@@ -55,19 +56,17 @@ def tile_attend_gcau_w_kernel(tc, xT, wT, y, wt, xm, offs, out):
         nc.scalar.activation(out=warm_out[:], in_=warm_in[:], func=ACT.Abs_reciprocal_sqrt)
 
         windows = [keep.tile([P, T], F32, name=f"window{m}") for m in range(D // P)]
-        for m, win in enumerate(windows):
-            (nc.vector if m < 2 else nc.gpsimd).memset(win[:].bitcast(I32), 0)
+        for win in windows:
+            nc.vector.memset(win[:].bitcast(I32), 0)
 
-        g_codes = keep.tile([P, NH + N], U32, name="g_codes", align_bytes=64)
-        g_scales = keep.tile([P, NH + N], U8, name="g_scales", align_bytes=64)
-        nc.gpsimd.memset(g_codes[:, 0:NH], 0)
-        nc.gpsimd.memset(g_scales[:, 0:NH], 0)
+        g_codes = keep.tile([P, N], U32, name="g_codes", align_bytes=64)
+        g_scales = keep.tile([P, N], U8, name="g_scales", align_bytes=64)
+        nc.vector.memset(g_codes[:, NH:N], 0)
+        nc.vector.memset(g_scales[:, NH:N].bitcast(I32), 0)
 
         w_grouped = keep.tile([P, N, PACK], BF16, name="w_grouped", align_bytes=64)
         w_codes = keep.tile([P, N], U32, name="w_codes", align_bytes=64)
         w_scales = keep.tile([P, N], U8, name="w_scales", align_bytes=64)
-        for t in range(PACK - 1):
-            nc.vector.tensor_copy(out=w_grouped[:, :, t], in_=planes[t][:].indirect(offsets[:]))
 
         def half_offsets(h):
             return offsets[:, h * NH // 16:(h + 1) * NH // 16]
@@ -76,6 +75,18 @@ def tile_attend_gcau_w_kernel(tc, xT, wT, y, wt, xm, offs, out):
             cols = slice(h * NH, (h + 1) * NH)
             nc.vector.quantize_mx(out=w_codes[:, cols].bitcast(E4M3), scales=w_scales[:, cols],
                                   in_=w_grouped[:, cols, :].rearrange("p n t -> p (n t)"))
+
+        pair_listed = keep.tile([P, 2, N], F32, name="pair_listed")
+        for t in range(2):
+            nc.vector.tensor_copy(out=pair_listed[:, t, :], in_=planes[t][:].indirect(offsets[:]))
+        nc.scalar.copy(out=w_grouped[:, :, 0:2], in_=pair_listed[:].rearrange("p t n -> p n t"))
+        nc.vector.tensor_copy(out=w_grouped[:, :, 2], in_=planes[2][:].indirect(offsets[:]))
+        last_listed = keep.tile([P, NH], F32, name="last_listed")
+        nc.vector.tensor_copy(out=last_listed[:], in_=planes[3][:].indirect(half_offsets(0)))
+        nc.scalar.copy(out=w_grouped[:, 0:NH, 3], in_=last_listed[:])
+        nc.vector.tensor_copy(out=w_grouped[:, NH:N, 3], in_=planes[3][:].indirect(half_offsets(1)))
+        for h in range(HALVES):
+            quantize_w(h)
 
         x_codes = keep.tile([P, R], U32, name="x_codes", align_bytes=64)
         x_scales = keep.tile([P, R], U8, name="x_scales", align_bytes=64)
@@ -91,27 +102,21 @@ def tile_attend_gcau_w_kernel(tc, xT, wT, y, wt, xm, offs, out):
             nc.vector.quantize_mx(out=x_codes[:, cols].bitcast(E4M3), scales=x_scales[:, cols],
                                   in_=grouped[:].rearrange("p e s t -> p (e s t)"))
 
-        last_listed = keep.tile([P, NH], F32, name="last_listed")
-        nc.vector.tensor_copy(out=last_listed[:], in_=planes[PACK - 1][:].indirect(half_offsets(0)))
-        nc.scalar.copy(out=w_grouped[:, 0:NH, PACK - 1], in_=last_listed[:])
-        nc.vector.tensor_copy(out=w_grouped[:, NH:N, PACK - 1], in_=planes[PACK - 1][:].indirect(half_offsets(1)))
-        quantize_w(0)
-        quantize_w(1)
         x_grouped = [weave_x(nc.vector.tensor_copy, 0), weave_x(nc.scalar.copy, 1)]
-        quantize_x(x_grouped[0], 0)
-        quantize_x(x_grouped[1], 1)
+        for u in range(PAIRS):
+            quantize_x(x_grouped[u], u)
 
         q = [keep.tile([P, PACK, NH], F32, name=f"q{h}") for h in range(HALVES)]
         qw = []
         damp = [keep.tile([P, PACK, CH], F32, name=f"damp{k}", tag=f"damp{k}", align_bytes=64) for k in range(CHUNKS)]
 
-        def part(tiles, k):
+        def chunk_of(halves, k):
             h, c = divmod(k, NH // CH)
-            return tiles[h][:, :, c * CH:(c + 1) * CH]
+            return halves[h][:, :, c * CH:(c + 1) * CH]
 
-        def residual(h, u, first, width, tag):
+        def residual(h, u, first, width, bank_tag):
             cols = slice(h * NH + first, h * NH + first + width)
-            bank = psum.tile([P, 2, width], F32, name=f"scores_{tag}", tag=tag)
+            bank = psum.tile([P, 2, width], F32, name=f"scores_{bank_tag}", tag=bank_tag)
             for e in range(2):
                 j = 2 * u + e
                 nc.tensor.matmul_mx(
@@ -124,9 +129,9 @@ def tile_attend_gcau_w_kernel(tc, xT, wT, y, wt, xm, offs, out):
         def damping(k):
             sq = keep.tile([P, PACK, CH], F32, name=f"sq{k}")
             rs = keep.tile([P, PACK, CH], F32, name=f"rs{k}")
-            pairs = [slice(0, 2), slice(2, 4)]
+            pairs = [slice(2 * u, 2 * u + 2) for u in range(PAIRS)]
             for js in pairs:
-                nc.scalar.activation(out=sq[:, js, :], in_=part(q, k)[:, js, :], func=ACT.Square)
+                nc.scalar.activation(out=sq[:, js, :], in_=chunk_of(q, k)[:, js, :], func=ACT.Square)
             for js in pairs:
                 nc.scalar.activation(out=rs[:, js, :], in_=sq[:, js, :], func=ACT.Abs_reciprocal_sqrt, bias=1.0)
             for js in pairs:
@@ -143,76 +148,77 @@ def tile_attend_gcau_w_kernel(tc, xT, wT, y, wt, xm, offs, out):
         def gradient(k):
             nc.vector.tensor_tensor(
                 out=g_grouped[:, k * CH:(k + 1) * CH, :].rearrange("p (c i) j -> p c j i", i=2),
-                in0=part(qw, k).rearrange("p j (c i) -> p c j i", i=2),
+                in0=chunk_of(qw, k).rearrange("p j (c i) -> p c j i", i=2),
                 in1=damp[k][:].rearrange("p j (c i) -> p c j i", i=2), op=ALU.mult)
 
-        def quantize_g(h):
-            cols = slice(h * NH, (h + 1) * NH)
-            dst = slice((h + 1) * NH, (h + 2) * NH)
-            nc.vector.quantize_mx(out=g_codes[:, dst].bitcast(E5M2), scales=g_scales[:, dst],
+        def quantize_g(k):
+            cols = slice(k * CH, (k + 1) * CH)
+            nc.vector.quantize_mx(out=g_codes[:, cols].bitcast(E5M2), scales=g_scales[:, cols],
                                   in_=g_grouped[:, cols, :].rearrange("p n j -> p (n j)"))
 
-        xm_codes = keep.tile([P, D], U32, name="xm_codes", align_bytes=64)
         xm_scales = keep.tile([P, D], U8, name="xm_scales", align_bytes=64)
+        xm_codes = []
 
-        def weave_xm(copy, first, width, tag):
-            grouped = keep.tile([P, width, PACK], BF16, name=f"xm_grouped{first}", tag=tag, align_bytes=64)
-            copy(out=grouped[:].rearrange("p (c i) t -> p c t i", i=4),
-                 in_=xm_raw[:, :, first:first + width].rearrange("p t (c i) -> p c t i", i=4))
+        def weave_xm(copy, first, width):
+            grouped = keep.tile([P, width, PACK], BF16, name=f"xm_grouped{first}", align_bytes=64)
+            copy(out=grouped[:].rearrange("p (c i) j -> p c j i", i=4),
+                 in_=xm_raw[:, :, first:first + width].rearrange("p j (c i) -> p c j i", i=4))
             return grouped
 
-        def quantize_xm(grouped, first, width):
-            cols = slice(first, first + width)
-            nc.vector.quantize_mx(out=xm_codes[:, cols].bitcast(E4M3), scales=xm_scales[:, cols],
-                                  in_=grouped[:].rearrange("p d t -> p (d t)"))
+        def quantize_xm(grouped, first, width, codes_tag):
+            codes = keep.tile([P, width], U32, name=f"xm_codes{first}", tag=codes_tag, align_bytes=64)
+            nc.vector.quantize_mx(out=codes[:].bitcast(E4M3), scales=xm_scales[:, first:first + width],
+                                  in_=grouped[:].rearrange("p d j -> p (d j)"))
+            xm_codes.extend(codes[:, c:c + P] for c in range(0, width, P))
 
-        def product(m, first, tag):
-            cols = slice(m * P, (m + 1) * P)
-            moving = slice(first, first + N)
-            acc = psum.tile([P, N], F32, name=f"acc_{tag}", tag=tag)
-            nc.tensor.matmul_mx(out=acc[:], lhsT=xm_codes[:, cols].bitcast(E4M3), lhsT_scale=xm_scales[:, cols],
-                                rhs=g_codes[:, moving].bitcast(E5M2), rhs_scale=g_scales[:, moving],
-                                start=True, stop=True)
+        def product(m, bank_tag):
+            acc = psum.tile([P, N], F32, name=f"acc_{bank_tag}", tag=bank_tag)
+            nc.tensor.matmul_mx(out=acc[:], lhsT=xm_codes[m].bitcast(E4M3), lhsT_scale=xm_scales[:, m * P:(m + 1) * P],
+                                rhs=g_codes[:].bitcast(E5M2), rhs_scale=g_scales[:], start=True, stop=True)
             return acc
 
-        def place(acc, m, cols, where, tag, copy=nc.scalar.copy):
-            dw = keep.tile([P, cols.stop - cols.start], F32, name=f"dw_{tag}", tag=tag, align_bytes=64)
-            copy(out=dw[:], in_=acc[:, cols])
+        def place(acc, m, cols, where, dw_tag):
+            dw = keep.tile([P, cols.stop - cols.start], F32, name=f"dw_{dw_tag}", tag=dw_tag, align_bytes=64)
+            nc.scalar.copy(out=dw[:], in_=acc[:, cols])
             nc.vector.tensor_copy(out=windows[m][:].indirect(where), in_=dw[:])
 
         def store(m):
             nc.sync.dma_start(out=out[m * P:(m + 1) * P, :], in_=windows[m][:])
 
-        for u in range(2):
-            for c in range(2):
+        for u in range(PAIRS):
+            for c in range(NH // CH):
                 residual(0, u, c * CH, CH, f"bank{2 * u + c}")
         damping(0)
         damping(1)
         weigh(0)
         residual(1, 0, 0, NH, "bank4")
-        xm_first = weave_xm(nc.vector.tensor_copy, 0, P, "xm_first")
         gradient(0)
-        quantize_xm(xm_first, 0, P)
-        gradient(1)
+        xm_first = weave_xm(nc.vector.tensor_copy, 0, P)
         quantize_g(0)
+        gradient(1)
+        quantize_xm(xm_first, 0, P, "damp1")
+        quantize_g(1)
         residual(1, 1, 0, NH, "bank5")
         weigh(1)
-        place(product(0, 0, "early0"), 0, slice(NH, N), half_offsets(0), "dw_a")
+        place(product(0, "early0"), 0, slice(0, NH), half_offsets(0), "dw_a")
+
         damping(2)
         gradient(2)
-        xm_second = weave_xm(nc.scalar.copy, P, P, "xm_second")
+        xm_second = weave_xm(nc.scalar.copy, P, P)
         damping(3)
-        quantize_xm(xm_second, P, P)
-        early = product(1, 0, "early1")
+        quantize_xm(xm_second, P, P, "xm_codes1")
+        early_second = product(1, "early1")
         gradient(3)
-        quantize_g(1)
-        place(early, 1, slice(NH, N), half_offsets(0), "damp3")
-        xm_last = weave_xm(nc.scalar.copy, DH, DH, "xm_last")
-        for m in range(2):
-            place(product(m, NH, f"bank{m}"), m, slice(NH, N), half_offsets(1), f"dw_late{m}")
-            store(m)
-            if m == 0:
-                quantize_xm(xm_last, DH, DH)
-        for m in range(2, D // P):
-            place(product(m, NH, f"bank{m}"), m, slice(0, N), offsets[:], f"dw{m}")
+        quantize_g(2)
+        quantize_g(3)
+        place(early_second, 1, slice(0, NH), half_offsets(0), "damp3")
+
+        xm_last = weave_xm(nc.scalar.copy, EARLY * P, D - EARLY * P)
+        place(product(0, "bank0"), 0, slice(NH, N), half_offsets(1), "dw_late0")
+        store(0)
+        quantize_xm(xm_last, EARLY * P, D - EARLY * P, "xm_codes2")
+        place(product(1, "bank1"), 1, slice(NH, N), half_offsets(1), "dw_late1")
+        store(1)
+        for m in range(EARLY, D // P):
+            place(product(m, f"bank{m}"), m, slice(0, N), offsets[:], f"dw{m}")
             store(m)

@@ -55,9 +55,10 @@ def tile_attend_gcau_w_kernel(tc, xT, wT, y, wt, xm, offs, out):
         nc.gpsimd.memset(warm_in[:], 1.0)
         nc.scalar.activation(out=warm_out[:], in_=warm_in[:], func=ACT.Abs_reciprocal_sqrt)
 
-        windows = [keep.tile([P, T], F32, name=f"window{m}") for m in range(D // P)]
+        windows = [keep.tile([P, T], F32, name=f"window{m}") for m in range(D // P - 1)]
         for win in windows:
             nc.vector.memset(win[:].bitcast(I32), 0)
+        windows.append(windows[0])
 
         g_codes = keep.tile([P, N], U32, name="g_codes", align_bytes=64)
         g_scales = keep.tile([P, N], U8, name="g_scales", align_bytes=64)

@@ -24,6 +24,7 @@ NH = N // HALVES
 CH = 128
 CHUNKS = N // CH
 EARLY = 2
+TILES = D // P
 
 
 def tile_attend_gcau_w_kernel(tc, xT, wT, y, wt, xm, offs, out):
@@ -50,15 +51,13 @@ def tile_attend_gcau_w_kernel(tc, xT, wT, y, wt, xm, offs, out):
         xm_raw = keep.tile([P, PACK, D], F32, name="xm_raw")
         nc.sync.dma_start(out=xm_raw[:], in_=xm[0].rearrange("(p j) d -> p j d", j=PACK))
 
-        warm_in = keep.tile([P, 1], F32, name="warm_in")
-        warm_out = keep.tile([P, 1], F32, name="warm_out")
-        nc.gpsimd.memset(warm_in[:], 1.0)
-        nc.scalar.activation(out=warm_out[:], in_=warm_in[:], func=ACT.Abs_reciprocal_sqrt)
-
-        windows = [keep.tile([P, T], F32, name=f"window{m}") for m in range(D // P - 1)]
+        windows = [keep.tile([P, T], F32, name=f"window{m}") for m in range(TILES - 1)]
         for win in windows:
             nc.vector.memset(win[:].bitcast(I32), 0)
         windows.append(windows[0])
+
+        warm_out = keep.tile([P, 1], F32, name="warm_out")
+        nc.scalar.activation(out=warm_out[:], in_=windows[0][:, 0:1], func=ACT.Abs_reciprocal_sqrt, bias=1.0)
 
         g_codes = keep.tile([P, N], U32, name="g_codes", align_bytes=64)
         g_scales = keep.tile([P, N], U8, name="g_scales", align_bytes=64)
@@ -220,6 +219,6 @@ def tile_attend_gcau_w_kernel(tc, xT, wT, y, wt, xm, offs, out):
         quantize_xm(xm_last, EARLY * P, D - EARLY * P, "xm_codes2")
         place(product(1, "bank1"), 1, slice(NH, N), half_offsets(1), "dw_late1")
         store(1)
-        for m in range(EARLY, D // P):
+        for m in range(EARLY, TILES):
             place(product(m, f"bank{m}"), m, slice(0, N), offsets[:], f"dw{m}")
             store(m)

@@ -51,18 +51,12 @@ def tile_attend_gcau_w_kernel(tc, xT, wT, y, wt, xm, offs, out):
         xm_raw = keep.tile([P, PACK, D], F32, name="xm_raw")
         nc.sync.dma_start(out=xm_raw[:], in_=xm[0].rearrange("(p j) d -> p j d", j=PACK))
 
-        windows = [keep.tile([P, T], F32, name=f"window{m}") for m in range(TILES - 1)]
+        windows = [keep.tile([P, T], F32, name=f"window{m}") for m in range(TILES)]
         for win in windows:
             nc.vector.memset(win[:].bitcast(I32), 0)
-        windows.append(windows[0])
 
         warm_out = keep.tile([P, 1], F32, name="warm_out")
         nc.scalar.activation(out=warm_out[:], in_=windows[0][:, 0:1], func=ACT.Abs_reciprocal_sqrt, bias=1.0)
-
-        g_codes = keep.tile([P, N], U32, name="g_codes", align_bytes=64)
-        g_scales = keep.tile([P, N], U8, name="g_scales", align_bytes=64)
-        nc.vector.memset(g_codes[:, NH:N], 0)
-        nc.vector.memset(g_scales[:, NH:N].bitcast(I32), 0)
 
         w_grouped = keep.tile([P, N, PACK], BF16, name="w_grouped", align_bytes=64)
         w_codes = keep.tile([P, N], U32, name="w_codes", align_bytes=64)
@@ -78,7 +72,7 @@ def tile_attend_gcau_w_kernel(tc, xT, wT, y, wt, xm, offs, out):
 
         pair_listed = keep.tile([P, 2, N], F32, name="pair_listed")
         for t in range(2):
-            nc.vector.tensor_copy(out=pair_listed[:, t, :], in_=planes[t][:].indirect(offsets[:]))
+            nc.scalar.activation(out=pair_listed[:, t, :], in_=planes[t][:].indirect(offsets[:]), func=ACT.Copy)
         nc.scalar.copy(out=w_grouped[:, :, 0:2], in_=pair_listed[:].rearrange("p t n -> p n t"))
         nc.vector.tensor_copy(out=w_grouped[:, :, 2], in_=planes[2][:].indirect(offsets[:]))
         last_listed = keep.tile([P, NH], F32, name="last_listed")
@@ -107,49 +101,44 @@ def tile_attend_gcau_w_kernel(tc, xT, wT, y, wt, xm, offs, out):
             quantize_x(x_grouped[u], u)
 
         q = [keep.tile([P, PACK, NH], F32, name=f"q{h}") for h in range(HALVES)]
-        qw = []
-        damp = [keep.tile([P, PACK, CH], F32, name=f"damp{k}", tag=f"damp{k}", align_bytes=64) for k in range(CHUNKS)]
+        sq = [keep.tile([P, PACK, NH], F32, name=f"sq{h}", tag=f"sq{h}", align_bytes=64) for h in range(HALVES)]
+        root = [keep.tile([P, PACK, NH], F32, name=f"root{h}") for h in range(HALVES)]
+        part = [keep.tile([P, PACK, NH], F32, name=f"part{h}") for h in range(HALVES)]
 
-        def chunk_of(halves, k):
-            h, c = divmod(k, NH // CH)
-            return halves[h][:, :, c * CH:(c + 1) * CH]
-
-        def residual(h, u, first, width, bank_tag):
-            cols = slice(h * NH + first, h * NH + first + width)
-            bank = psum.tile([P, 2, width], F32, name=f"scores_{bank_tag}", tag=bank_tag)
-            for e in range(2):
-                j = 2 * u + e
+        def residual(h, first, count, bank_tag):
+            cols = slice(h * NH, (h + 1) * NH)
+            bank = psum.tile([P, count, NH], F32, name=f"scores_{bank_tag}", tag=bank_tag)
+            for e in range(count):
+                j = first + e
                 nc.tensor.matmul_mx(
                     out=bank[:, e, :],
                     lhsT=x_codes[:, j * P:(j + 1) * P].bitcast(E4M3), lhsT_scale=x_scales[:, j * P:(j + 1) * P],
                     rhs=w_codes[:, cols].bitcast(E4M3), rhs_scale=w_scales[:, cols], start=True, stop=True)
-            nc.vector.tensor_tensor(out=q[h][:, 2 * u:2 * u + 2, first:first + width], in0=bank[:],
-                                    in1=y_sb[u][:, :, cols], op=ALU.subtract)
+            u, e0 = divmod(first, 2)
+            nc.vector.tensor_tensor(out=q[h][:, first:first + count, :], in0=bank[:],
+                                    in1=y_sb[u][:, e0:e0 + count, cols], op=ALU.subtract)
 
-        def damping(k):
-            sq = keep.tile([P, PACK, CH], F32, name=f"sq{k}")
-            rs = keep.tile([P, PACK, CH], F32, name=f"rs{k}")
-            pairs = [slice(2 * u, 2 * u + 2) for u in range(PAIRS)]
-            for js in pairs:
-                nc.scalar.activation(out=sq[:, js, :], in_=chunk_of(q, k)[:, js, :], func=ACT.Square)
-            for js in pairs:
-                nc.scalar.activation(out=rs[:, js, :], in_=sq[:, js, :], func=ACT.Abs_reciprocal_sqrt, bias=1.0)
-            for js in pairs:
-                nc.scalar.activation(out=damp[k][:, js, :], in_=rs[:, js, :], func=ACT.Square)
+        def square(h, js):
+            nc.scalar.activation(out=sq[h][:, js, :], in_=q[h][:, js, :], func=ACT.Square)
 
-        def weigh(h):
-            qw.append(keep.tile([P, PACK, NH], F32, name=f"qw{h}", tag="qw"))
-            for j in range(PACK):
-                nc.vector.tensor_scalar(out=qw[h][:, j, :], in0=q[h][:, j, :], scalar1=wt_sb[:, j:j + 1],
-                                        scalar2=None, op0=ALU.mult)
+        def inverse_root(h, js):
+            nc.scalar.activation(out=root[h][:, js, :], in_=sq[h][:, js, :], func=ACT.Abs_reciprocal_sqrt, bias=1.0)
+
+        def weigh(h, j):
+            nc.vector.scalar_tensor_tensor(out=part[h][:, j, :], in0=q[h][:, j, :], scalar=wt_sb[:, j:j + 1],
+                                           in1=root[h][:, j, :], op0=ALU.mult, op1=ALU.mult)
 
         g_grouped = keep.tile([P, N, PACK], BF16, name="g_grouped", align_bytes=64)
+        g_codes = keep.tile([P, N], U32, name="g_codes", align_bytes=64)
+        g_scales = keep.tile([P, N], U8, name="g_scales", align_bytes=64)
 
         def gradient(k):
+            h, c = divmod(k, NH // CH)
+            cols = slice(c * CH, (c + 1) * CH)
             nc.vector.tensor_tensor(
                 out=g_grouped[:, k * CH:(k + 1) * CH, :].rearrange("p (c i) j -> p c j i", i=2),
-                in0=chunk_of(qw, k).rearrange("p j (c i) -> p c j i", i=2),
-                in1=damp[k][:].rearrange("p j (c i) -> p c j i", i=2), op=ALU.mult)
+                in0=part[h][:, :, cols].rearrange("p j (c i) -> p c j i", i=2),
+                in1=root[h][:, :, cols].rearrange("p j (c i) -> p c j i", i=2), op=ALU.mult)
 
         def quantize_g(k):
             cols = slice(k * CH, (k + 1) * CH)
@@ -157,68 +146,90 @@ def tile_attend_gcau_w_kernel(tc, xT, wT, y, wt, xm, offs, out):
                                   in_=g_grouped[:, cols, :].rearrange("p n j -> p (n j)"))
 
         xm_scales = keep.tile([P, D], U8, name="xm_scales", align_bytes=64)
-        xm_codes = []
+        xm_codes = keep.tile([P, D], U32, name="xm_codes", align_bytes=64)
 
-        def weave_xm(copy, first, width):
-            grouped = keep.tile([P, width, PACK], BF16, name=f"xm_grouped{first}", align_bytes=64)
+        def weave_xm(copy, m, tag):
+            grouped = keep.tile([P, P, PACK], BF16, name=f"xm_grouped{m}", tag=tag, align_bytes=64)
             copy(out=grouped[:].rearrange("p (c i) j -> p c j i", i=4),
-                 in_=xm_raw[:, :, first:first + width].rearrange("p j (c i) -> p c j i", i=4))
+                 in_=xm_raw[:, :, m * P:(m + 1) * P].rearrange("p j (c i) -> p c j i", i=4))
             return grouped
 
-        def quantize_xm(grouped, first, width, codes_tag):
-            codes = keep.tile([P, width], U32, name=f"xm_codes{first}", tag=codes_tag, align_bytes=64)
-            nc.vector.quantize_mx(out=codes[:].bitcast(E4M3), scales=xm_scales[:, first:first + width],
+        def quantize_xm(grouped, m):
+            cols = slice(m * P, (m + 1) * P)
+            nc.vector.quantize_mx(out=xm_codes[:, cols].bitcast(E4M3), scales=xm_scales[:, cols],
                                   in_=grouped[:].rearrange("p d j -> p (d j)"))
-            xm_codes.extend(codes[:, c:c + P] for c in range(0, width, P))
 
-        def product(m, bank_tag):
-            acc = psum.tile([P, N], F32, name=f"acc_{bank_tag}", tag=bank_tag)
-            nc.tensor.matmul_mx(out=acc[:], lhsT=xm_codes[m].bitcast(E4M3), lhsT_scale=xm_scales[:, m * P:(m + 1) * P],
-                                rhs=g_codes[:].bitcast(E5M2), rhs_scale=g_scales[:], start=True, stop=True)
+        def product(m, cols, bank_tag):
+            rows = slice(m * P, (m + 1) * P)
+            acc = psum.tile([P, cols.stop - cols.start], F32, name=f"acc_{m}_{cols.start}", tag=bank_tag)
+            nc.tensor.matmul_mx(out=acc[:], lhsT=xm_codes[:, rows].bitcast(E4M3), lhsT_scale=xm_scales[:, rows],
+                                rhs=g_codes[:, cols].bitcast(E5M2), rhs_scale=g_scales[:, cols], start=True, stop=True)
             return acc
 
-        def place(acc, m, cols, where, dw_tag):
-            dw = keep.tile([P, cols.stop - cols.start], F32, name=f"dw_{dw_tag}", tag=dw_tag, align_bytes=64)
-            nc.scalar.copy(out=dw[:], in_=acc[:, cols])
-            nc.vector.tensor_copy(out=windows[m][:].indirect(where), in_=dw[:])
+        def copy_out(copy, acc, width, name, tag):
+            dw = keep.tile([P, width], F32, name=name, tag=tag, align_bytes=64)
+            copy(out=dw[:], in_=acc[:])
+            return dw
+
+        def scatter_vector(m, where, dw):
+            nc.vector.tensor_copy(out=windows[m][:].indirect(where), in_=dw)
+
+        def scatter_scalar(m, where, dw):
+            nc.scalar.activation(out=windows[m][:].indirect(where), in_=dw, func=ACT.Copy)
 
         def store(m):
             nc.sync.dma_start(out=out[m * P:(m + 1) * P, :], in_=windows[m][:])
 
-        for u in range(PAIRS):
-            for c in range(NH // CH):
-                residual(0, u, c * CH, CH, f"bank{2 * u + c}")
-        damping(0)
-        damping(1)
-        weigh(0)
-        residual(1, 0, 0, NH, "bank4")
-        gradient(0)
-        xm_first = weave_xm(nc.vector.tensor_copy, 0, P)
-        quantize_g(0)
-        gradient(1)
-        quantize_xm(xm_first, 0, P, "damp1")
-        quantize_g(1)
-        residual(1, 1, 0, NH, "bank5")
-        weigh(1)
-        place(product(0, "early0"), 0, slice(0, NH), half_offsets(0), "dw_a")
+        halves = [slice(h * NH, (h + 1) * NH) for h in range(HALVES)]
+        pairs = [slice(2 * u, 2 * u + 2) for u in range(PAIRS)]
+        tiles = [slice(j, j + 1) for j in range(PACK)]
 
-        damping(2)
+        for j in range(PACK):
+            residual(0, j, 1, f"bank{j}")
+        for u in range(PAIRS):
+            residual(1, 2 * u, 2, f"bank{4 + u}")
+        for u in range(PAIRS):
+            for j in (2 * u, 2 * u + 1):
+                square(0, tiles[j])
+            for j in (2 * u, 2 * u + 1):
+                inverse_root(0, tiles[j])
+        xm0 = weave_xm(nc.scalar.copy, 0, "xm_grouped0")
+        for js in pairs:
+            square(1, js)
+        for js in pairs:
+            inverse_root(1, js)
+        for j in range(PACK):
+            weigh(0, j)
+        gradient(0)
+        gradient(1)
+        quantize_g(0)
+        quantize_xm(xm0, 0)
+        quantize_g(1)
+        xm1 = weave_xm(nc.scalar.copy, 1, "sq1")
+        dw = copy_out(nc.scalar.copy, product(0, halves[0], "bank6"), NH, "dw00", "dw_s")
+        scatter_scalar(0, half_offsets(0), dw[:])
+        for j in range(PACK):
+            weigh(1, j)
         gradient(2)
-        xm_second = weave_xm(nc.scalar.copy, P, P)
-        damping(3)
-        quantize_xm(xm_second, P, P, "xm_codes1")
-        early_second = product(1, "early1")
         gradient(3)
         quantize_g(2)
+        quantize_xm(xm1, 1)
         quantize_g(3)
-        place(early_second, 1, slice(0, NH), half_offsets(0), "damp3")
-
-        xm_last = weave_xm(nc.scalar.copy, EARLY * P, D - EARLY * P)
-        place(product(0, "bank0"), 0, slice(NH, N), half_offsets(1), "dw_late0")
+        xm2 = weave_xm(nc.vector.tensor_copy, 2, "xm_grouped2")
+        dw01 = copy_out(nc.vector.tensor_copy, product(0, halves[1], "bank7"), NH, "dw01", "dw01")
+        quantize_xm(xm2, 2)
+        scatter_vector(0, half_offsets(1), dw01[:])
         store(0)
-        quantize_xm(xm_last, EARLY * P, D - EARLY * P, "xm_codes2")
-        place(product(1, "bank1"), 1, slice(NH, N), half_offsets(1), "dw_late1")
+        xm3 = weave_xm(nc.scalar.copy, 3, "dw_s")
+        for h in range(HALVES):
+            dw = copy_out(nc.scalar.copy, product(1, halves[h], f"bank{h}"), NH, f"dw1{h}", f"dw1{h}")
+            scatter_scalar(1, half_offsets(h), dw[:])
         store(1)
-        for m in range(EARLY, TILES):
-            place(product(m, f"bank{m}"), m, slice(0, N), offsets[:], f"dw{m}")
-            store(m)
+        quantize_xm(xm3, 3)
+        dw2 = copy_out(nc.vector.tensor_copy, product(2, slice(0, N), "bank2"), N, "dw2", "dw01")
+        scatter_vector(2, offsets[:], dw2[:])
+        store(2)
+        dw3 = copy_out(nc.scalar.copy, product(3, slice(0, N), "bank3"), N, "dw3", "dw3")
+        for h in range(HALVES):
+            scatter_scalar(3, half_offsets(h), dw3[:, halves[h]])
+        store(3)

@@ -74,21 +74,24 @@ def tile_attend_gcau_w_kernel(tc, xT, wT, y, wt, xm, offs, out):
         for t in range(2):
             nc.scalar.activation(out=pair_listed[:, t, :], in_=planes[t][:].indirect(offsets[:]), func=ACT.Copy)
         nc.scalar.copy(out=w_grouped[:, :, 0:2], in_=pair_listed[:].rearrange("p t n -> p n t"))
-        nc.vector.tensor_copy(out=w_grouped[:, :, 2], in_=planes[2][:].indirect(offsets[:]))
-        last_listed = keep.tile([P, NH], F32, name="last_listed")
-        nc.vector.tensor_copy(out=last_listed[:], in_=planes[3][:].indirect(half_offsets(0)))
-        nc.scalar.copy(out=w_grouped[:, 0:NH, 3], in_=last_listed[:])
-        nc.vector.tensor_copy(out=w_grouped[:, NH:N, 3], in_=planes[3][:].indirect(half_offsets(1)))
+        last_listed = keep.tile([P, 2, NH], F32, name="last_listed")
+        nc.vector.tensor_copy(out=w_grouped[:, 0:NH, 2], in_=planes[2][:].indirect(half_offsets(0)))
+        nc.vector.tensor_copy(out=last_listed[:, 0, :], in_=planes[2][:].indirect(half_offsets(1)))
+        nc.vector.tensor_copy(out=w_grouped[:, 0:NH, 3], in_=planes[3][:].indirect(half_offsets(0)))
+        nc.scalar.activation(out=last_listed[:, 1, :], in_=planes[3][:].indirect(half_offsets(1)), func=ACT.Copy)
+        nc.scalar.copy(out=w_grouped[:, NH:N, 2:4], in_=last_listed[:].rearrange("p t n -> p n t"))
         for h in range(HALVES):
             quantize_w(h)
 
         x_codes = keep.tile([P, R], U32, name="x_codes", align_bytes=64)
         x_scales = keep.tile([P, R], U8, name="x_scales", align_bytes=64)
 
-        def weave_x(copy, u):
+        def weave_x(u):
             grouped = keep.tile([P, 2, P, PACK], BF16, name=f"x_grouped{u}", align_bytes=64)
-            copy(out=grouped[:].rearrange("p e (c i) t -> p c t i e", i=2),
-                 in_=x_raw[:].rearrange("p t (c i j) -> p c t i j", i=2, j=PACK)[:, :, :, :, 2 * u:2 * u + 2])
+            woven = grouped[:].rearrange("p e (c i) t -> p c t i e", i=2)
+            source = x_raw[:].rearrange("p t (c i j) -> p c t i j", i=2, j=PACK)[:, :, :, :, 2 * u:2 * u + 2]
+            nc.vector.tensor_copy(out=woven[:, 0:P // 4], in_=source[:, 0:P // 4])
+            nc.scalar.copy(out=woven[:, P // 4:P // 2], in_=source[:, P // 4:P // 2])
             return grouped
 
         def quantize_x(grouped, u):
@@ -96,14 +99,14 @@ def tile_attend_gcau_w_kernel(tc, xT, wT, y, wt, xm, offs, out):
             nc.vector.quantize_mx(out=x_codes[:, cols].bitcast(E4M3), scales=x_scales[:, cols],
                                   in_=grouped[:].rearrange("p e s t -> p (e s t)"))
 
-        x_grouped = [weave_x(nc.vector.tensor_copy, 0), weave_x(nc.scalar.copy, 1)]
+        x_grouped = [weave_x(u) for u in range(PAIRS)]
         for u in range(PAIRS):
             quantize_x(x_grouped[u], u)
 
-        q = [keep.tile([P, PACK, NH], F32, name=f"q{h}") for h in range(HALVES)]
+        q = [keep.tile([P, PACK, NH], F32, name=f"q{h}", tag=f"q{h}", align_bytes=64) for h in range(HALVES)]
         sq = [keep.tile([P, PACK, NH], F32, name=f"sq{h}", tag=f"sq{h}", align_bytes=64) for h in range(HALVES)]
         root = [keep.tile([P, PACK, NH], F32, name=f"root{h}") for h in range(HALVES)]
-        part = [keep.tile([P, PACK, NH], F32, name=f"part{h}") for h in range(HALVES)]
+        part = [keep.tile([P, PACK, NH], F32, name=f"part{h}", tag=f"part{h}", align_bytes=64) for h in range(HALVES)]
 
         def residual(h, first, count, bank_tag):
             cols = slice(h * NH, (h + 1) * NH)
@@ -123,6 +126,15 @@ def tile_attend_gcau_w_kernel(tc, xT, wT, y, wt, xm, offs, out):
 
         def inverse_root(h, js):
             nc.scalar.activation(out=root[h][:, js, :], in_=sq[h][:, js, :], func=ACT.Abs_reciprocal_sqrt, bias=1.0)
+
+        def damping(h, js):
+            single = keep.tile([P, 2, NH], F32, name="single")
+            nc.scalar.activation(out=single[:], in_=sq[h][:, js, :], func=ACT.Abs_reciprocal_sqrt, bias=1.0)
+            return single
+
+        def weigh_only(h, j):
+            nc.vector.tensor_scalar(out=part[h][:, j, :], in0=q[h][:, j, :], scalar1=wt_sb[:, j:j + 1],
+                                    scalar2=None, op0=ALU.mult)
 
         def weigh(h, j):
             nc.vector.scalar_tensor_tensor(out=part[h][:, j, :], in0=q[h][:, j, :], scalar=wt_sb[:, j:j + 1],
@@ -146,24 +158,32 @@ def tile_attend_gcau_w_kernel(tc, xT, wT, y, wt, xm, offs, out):
                                   in_=g_grouped[:, cols, :].rearrange("p n j -> p (n j)"))
 
         xm_scales = keep.tile([P, D], U8, name="xm_scales", align_bytes=64)
-        xm_codes = keep.tile([P, D], U32, name="xm_codes", align_bytes=64)
+        xm_codes = []
 
-        def weave_xm(copy, m, tag):
-            grouped = keep.tile([P, P, PACK], BF16, name=f"xm_grouped{m}", tag=tag, align_bytes=64)
+        def weave_xm(copy, first, count, tag):
+            grouped = keep.tile([P, count * P, PACK], BF16, name=f"xm_grouped{first}", tag=tag, align_bytes=64)
             copy(out=grouped[:].rearrange("p (c i) j -> p c j i", i=4),
-                 in_=xm_raw[:, :, m * P:(m + 1) * P].rearrange("p j (c i) -> p c j i", i=4))
+                 in_=xm_raw[:, :, first * P:(first + count) * P].rearrange("p j (c i) -> p c j i", i=4))
             return grouped
 
-        def quantize_xm(grouped, m):
-            cols = slice(m * P, (m + 1) * P)
-            nc.vector.quantize_mx(out=xm_codes[:, cols].bitcast(E4M3), scales=xm_scales[:, cols],
+        def quantize_xm(grouped, first, count, tag):
+            codes = keep.tile([P, count * P], U32, name=f"xm_codes{first}", tag=tag, align_bytes=64)
+            nc.vector.quantize_mx(out=codes[:].bitcast(E4M3), scales=xm_scales[:, first * P:(first + count) * P],
                                   in_=grouped[:].rearrange("p d j -> p (d j)"))
+            xm_codes.extend(codes[:, e * P:(e + 1) * P] for e in range(count))
 
-        def product(m, cols, bank_tag):
+        def product(acc, m, cols):
             rows = slice(m * P, (m + 1) * P)
-            acc = psum.tile([P, cols.stop - cols.start], F32, name=f"acc_{m}_{cols.start}", tag=bank_tag)
-            nc.tensor.matmul_mx(out=acc[:], lhsT=xm_codes[:, rows].bitcast(E4M3), lhsT_scale=xm_scales[:, rows],
+            nc.tensor.matmul_mx(out=acc, lhsT=xm_codes[m].bitcast(E4M3), lhsT_scale=xm_scales[:, rows],
                                 rhs=g_codes[:, cols].bitcast(E5M2), rhs_scale=g_scales[:, cols], start=True, stop=True)
+
+        def products(parts, bank_tag):
+            width = sum(cols.stop - cols.start for m, cols in parts)
+            acc = psum.tile([P, width], F32, name=f"acc_{parts[0][0]}_{parts[0][1].start}", tag=bank_tag)
+            first = 0
+            for m, cols in parts:
+                product(acc[:, first:first + cols.stop - cols.start], m, cols)
+                first = first + cols.stop - cols.start
             return acc
 
         def copy_out(copy, acc, width, name, tag):
@@ -182,6 +202,7 @@ def tile_attend_gcau_w_kernel(tc, xT, wT, y, wt, xm, offs, out):
 
         halves = [slice(h * NH, (h + 1) * NH) for h in range(HALVES)]
         pairs = [slice(2 * u, 2 * u + 2) for u in range(PAIRS)]
+        chunks = [slice(k * CH, (k + 1) * CH) for k in range(CHUNKS)]
         tiles = [slice(j, j + 1) for j in range(PACK)]
 
         for j in range(PACK):
@@ -193,43 +214,47 @@ def tile_attend_gcau_w_kernel(tc, xT, wT, y, wt, xm, offs, out):
                 square(0, tiles[j])
             for j in (2 * u, 2 * u + 1):
                 inverse_root(0, tiles[j])
-        xm0 = weave_xm(nc.scalar.copy, 0, "xm_grouped0")
+        xm0 = weave_xm(nc.scalar.copy, 0, 1, "xm_grouped0")
         for js in pairs:
             square(1, js)
-        for js in pairs:
-            inverse_root(1, js)
+        single = damping(1, pairs[0])
+        inverse_root(1, pairs[1])
+        nc.scalar.activation(out=root[1][:, pairs[0], :], in_=single[:], func=ACT.Square)
         for j in range(PACK):
             weigh(0, j)
+        quantize_xm(xm0, 0, 1, "xm_codes0")
         gradient(0)
         gradient(1)
         quantize_g(0)
-        quantize_xm(xm0, 0)
         quantize_g(1)
-        xm1 = weave_xm(nc.scalar.copy, 1, "sq1")
-        dw = copy_out(nc.scalar.copy, product(0, halves[0], "bank6"), NH, "dw00", "dw_s")
-        scatter_scalar(0, half_offsets(0), dw[:])
-        for j in range(PACK):
+        xm1 = weave_xm(nc.scalar.copy, 1, 1, "sq1")
+        dw00 = copy_out(nc.scalar.copy, products([(0, halves[0])], "bank6"), NH, "dw00", "dw00")
+        scatter_scalar(0, half_offsets(0), dw00[:])
+        for j in (0, 1):
+            weigh_only(1, j)
+        for j in (2, 3):
             weigh(1, j)
         gradient(2)
         gradient(3)
         quantize_g(2)
-        quantize_xm(xm1, 1)
+        quantize_xm(xm1, 1, 1, "q1")
         quantize_g(3)
-        xm2 = weave_xm(nc.vector.tensor_copy, 2, "xm_grouped2")
-        dw01 = copy_out(nc.vector.tensor_copy, product(0, halves[1], "bank7"), NH, "dw01", "dw01")
-        quantize_xm(xm2, 2)
+        xm23 = weave_xm(nc.vector.tensor_copy, 2, 2, "part1")
+        dw01 = copy_out(nc.vector.tensor_copy, products([(0, halves[1])], "bank0"), NH, "dw01", "dw01")
+        quantize_xm(xm23, 2, 2, "xm_codes2")
         scatter_vector(0, half_offsets(1), dw01[:])
         store(0)
-        xm3 = weave_xm(nc.scalar.copy, 3, "dw_s")
-        for h in range(HALVES):
-            dw = copy_out(nc.scalar.copy, product(1, halves[h], f"bank{h}"), NH, f"dw1{h}", f"dw1{h}")
-            scatter_scalar(1, half_offsets(h), dw[:])
+        dw10 = copy_out(nc.scalar.copy, products([(1, halves[0])], "bank7"), NH, "dw10", "dw10")
+        scatter_scalar(1, half_offsets(0), dw10[:])
+        dw11 = copy_out(nc.scalar.copy, products([(1, halves[1])], "bank1"), NH, "dw11", "dw11")
+        scatter_vector(1, half_offsets(1), dw11[:])
         store(1)
-        quantize_xm(xm3, 3)
-        dw2 = copy_out(nc.vector.tensor_copy, product(2, slice(0, N), "bank2"), N, "dw2", "dw01")
-        scatter_vector(2, offsets[:], dw2[:])
+        dw2 = copy_out(nc.scalar.copy, products([(2, slice(0, N))], "bank2"), N, "dw2", "dw10")
+        dw30 = copy_out(nc.scalar.copy, products([(3, halves[0])], "bank3"), NH, "dw30", "dw30")
+        dw31 = copy_out(nc.vector.tensor_copy, products([(3, halves[1])], "bank4"), NH, "dw31", "dw11")
+        scatter_scalar(2, half_offsets(0), dw2[:, halves[0]])
+        scatter_vector(2, half_offsets(1), dw2[:, halves[1]])
         store(2)
-        dw3 = copy_out(nc.scalar.copy, product(3, slice(0, N), "bank3"), N, "dw3", "dw3")
-        for h in range(HALVES):
-            scatter_scalar(3, half_offsets(h), dw3[:, halves[h]])
+        scatter_scalar(3, half_offsets(0), dw30[:])
+        scatter_vector(3, half_offsets(1), dw31[:])
         store(3)

@@ -45,11 +45,14 @@ def tile_attend_gcau_w_kernel(tc, xT, wT, y, wt, xm, offs, out):
         y_view = y[0].rearrange("(p j) n -> p j n", j=PACK)
         y_sb = [keep.tile([P, 2, N], F32, name=f"y_sb{u}") for u in range(PAIRS)]
         wt_sb = keep.tile([P, PACK], F32, name="wt_sb")
+        nc.sync.dma_start(out=wt_sb[:], in_=wt[0].rearrange("(p j) o -> p (j o)", j=PACK))
         for u in range(PAIRS):
             nc.sync.dma_start(out=y_sb[u][:], in_=y_view[:, 2 * u:2 * u + 2, :])
-        nc.sync.dma_start(out=wt_sb[:], in_=wt[0].rearrange("(p j) o -> p (j o)", j=PACK))
-        xm_raw = keep.tile([P, PACK, D], F32, name="xm_raw")
-        nc.sync.dma_start(out=xm_raw[:], in_=xm[0].rearrange("(p j) d -> p j d", j=PACK))
+        xm_view = xm[0].rearrange("(p j) d -> p j d", j=PACK)
+        xm_first = keep.tile([P, PACK, P], F32, name="xm_first")
+        nc.sync.dma_start(out=xm_first[:], in_=xm_view[:, :, 0:P])
+        xm_rest = keep.tile([P, PACK, D - P], F32, name="xm_rest")
+        nc.sync.dma_start(out=xm_rest[:], in_=xm_view[:, :, P:])
 
         windows = [keep.tile([P, T], F32, name=f"window{m}") for m in range(TILES)]
         for win in windows:
@@ -106,7 +109,7 @@ def tile_attend_gcau_w_kernel(tc, xT, wT, y, wt, xm, offs, out):
         q = [keep.tile([P, PACK, NH], F32, name=f"q{h}", tag=f"q{h}", align_bytes=64) for h in range(HALVES)]
         sq = [keep.tile([P, PACK, NH], F32, name=f"sq{h}", tag=f"sq{h}", align_bytes=64) for h in range(HALVES)]
         root = [keep.tile([P, PACK, NH], F32, name=f"root{h}") for h in range(HALVES)]
-        part = [keep.tile([P, PACK, NH], F32, name=f"part{h}", tag=f"part{h}", align_bytes=64) for h in range(HALVES)]
+        part = [keep.tile([P, PACK, NH], F32, name="part0")]
 
         def residual(h, first, count, bank_tag):
             cols = slice(h * NH, (h + 1) * NH)
@@ -128,7 +131,7 @@ def tile_attend_gcau_w_kernel(tc, xT, wT, y, wt, xm, offs, out):
             nc.scalar.activation(out=root[h][:, js, :], in_=sq[h][:, js, :], func=ACT.Abs_reciprocal_sqrt, bias=1.0)
 
         def damping(h, js):
-            single = keep.tile([P, 2, NH], F32, name="single")
+            single = keep.tile([P, 2, NH], F32, name=f"single{js.start}")
             nc.scalar.activation(out=single[:], in_=sq[h][:, js, :], func=ACT.Abs_reciprocal_sqrt, bias=1.0)
             return single
 
@@ -160,10 +163,16 @@ def tile_attend_gcau_w_kernel(tc, xT, wT, y, wt, xm, offs, out):
         xm_scales = keep.tile([P, D], U8, name="xm_scales", align_bytes=64)
         xm_codes = []
 
+        def weave_xm_first():
+            grouped = keep.tile([P, P, PACK], BF16, name="xm_grouped0", tag="part1", align_bytes=64)
+            nc.gpsimd.tensor_scalar(out=grouped[:], in0=xm_first[:].rearrange("p j d -> p d j"),
+                                    scalar1=1.0, scalar2=0.0, op0=ALU.mult, op1=ALU.add)
+            return grouped
+
         def weave_xm(copy, first, count, tag):
             grouped = keep.tile([P, count * P, PACK], BF16, name=f"xm_grouped{first}", tag=tag, align_bytes=64)
             copy(out=grouped[:].rearrange("p (c i) j -> p c j i", i=4),
-                 in_=xm_raw[:, :, first * P:(first + count) * P].rearrange("p j (c i) -> p c j i", i=4))
+                 in_=xm_rest[:, :, (first - 1) * P:(first - 1 + count) * P].rearrange("p j (c i) -> p c j i", i=4))
             return grouped
 
         def quantize_xm(grouped, first, count, tag):
@@ -214,12 +223,12 @@ def tile_attend_gcau_w_kernel(tc, xT, wT, y, wt, xm, offs, out):
                 square(0, tiles[j])
             for j in (2 * u, 2 * u + 1):
                 inverse_root(0, tiles[j])
-        xm0 = weave_xm(nc.scalar.copy, 0, 1, "xm_grouped0")
+        xm0 = weave_xm_first()
         for js in pairs:
             square(1, js)
-        single = damping(1, pairs[0])
-        inverse_root(1, pairs[1])
-        nc.scalar.activation(out=root[1][:, pairs[0], :], in_=single[:], func=ACT.Square)
+        singles = [damping(1, js) for js in pairs]
+        for u in range(PAIRS):
+            nc.scalar.activation(out=root[1][:, pairs[u], :], in_=singles[u][:], func=ACT.Square)
         for j in range(PACK):
             weigh(0, j)
         quantize_xm(xm0, 0, 1, "xm_codes0")
@@ -230,10 +239,9 @@ def tile_attend_gcau_w_kernel(tc, xT, wT, y, wt, xm, offs, out):
         xm1 = weave_xm(nc.scalar.copy, 1, 1, "sq1")
         dw00 = copy_out(nc.scalar.copy, products([(0, halves[0])], "bank6"), NH, "dw00", "dw00")
         scatter_scalar(0, half_offsets(0), dw00[:])
-        for j in (0, 1):
+        part.append(keep.tile([P, PACK, NH], F32, name="part1", tag="part1", align_bytes=64))
+        for j in range(PACK):
             weigh_only(1, j)
-        for j in (2, 3):
-            weigh(1, j)
         gradient(2)
         gradient(3)
         quantize_g(2)

@@ -22,8 +22,6 @@ PAIRS = PACK // 2
 HALVES = 2
 NH = N // HALVES
 CH = 128
-CHUNKS = N // CH
-EARLY = 2
 TILES = D // P
 
 
@@ -45,12 +43,12 @@ def tile_attend_gcau_w_kernel(tc, xT, wT, y, wt, xm, offs, out):
         y_view = y[0].rearrange("(p j) n -> p j n", j=PACK)
         y_sb = [keep.tile([P, 2, N], F32, name=f"y_sb{u}") for u in range(PAIRS)]
         wt_sb = keep.tile([P, PACK], F32, name="wt_sb")
-        nc.sync.dma_start(out=wt_sb[:], in_=wt[0].rearrange("(p j) o -> p (j o)", j=PACK))
         for u in range(PAIRS):
             nc.sync.dma_start(out=y_sb[u][:], in_=y_view[:, 2 * u:2 * u + 2, :])
         xm_view = xm[0].rearrange("(p j) d -> p j d", j=PACK)
         xm_first = keep.tile([P, PACK, P], F32, name="xm_first")
         nc.sync.dma_start(out=xm_first[:], in_=xm_view[:, :, 0:P])
+        nc.sync.dma_start(out=wt_sb[:], in_=wt[0].rearrange("(p j) o -> p (j o)", j=PACK))
         xm_rest = keep.tile([P, PACK, D - P], F32, name="xm_rest")
         nc.sync.dma_start(out=xm_rest[:], in_=xm_view[:, :, P:])
 
@@ -58,33 +56,33 @@ def tile_attend_gcau_w_kernel(tc, xT, wT, y, wt, xm, offs, out):
         for win in windows:
             nc.vector.memset(win[:].bitcast(I32), 0)
 
+        warm_in = keep.tile([P, 1], F32, name="warm_in")
         warm_out = keep.tile([P, 1], F32, name="warm_out")
-        nc.scalar.activation(out=warm_out[:], in_=windows[0][:, 0:1], func=ACT.Abs_reciprocal_sqrt, bias=1.0)
+        nc.gpsimd.memset(warm_in[:], 0.0)
+        nc.scalar.activation(out=warm_out[:], in_=warm_in[:], func=ACT.Abs_reciprocal_sqrt, bias=1.0)
 
-        w_grouped = keep.tile([P, N, PACK], BF16, name="w_grouped", align_bytes=64)
-        w_codes = keep.tile([P, N], U32, name="w_codes", align_bytes=64)
-        w_scales = keep.tile([P, N], U8, name="w_scales", align_bytes=64)
+        halves = [slice(h * NH, (h + 1) * NH) for h in range(HALVES)]
+        pairs = [slice(2 * u, 2 * u + 2) for u in range(PAIRS)]
 
         def half_offsets(h):
             return offsets[:, h * NH // 16:(h + 1) * NH // 16]
 
-        def quantize_w(h):
-            cols = slice(h * NH, (h + 1) * NH)
+        w_grouped = keep.tile([P, N, PACK], BF16, name="w_grouped", align_bytes=64)
+        w_codes = keep.tile([P, N], U32, name="w_codes", align_bytes=64)
+        w_scales = keep.tile([P, N], U8, name="w_scales", align_bytes=64)
+        low_listed = keep.tile([P, 2, N], F32, name="low_listed")
+        for t in range(2):
+            nc.scalar.activation(out=low_listed[:, t, :], in_=planes[t][:].indirect(offsets[:]), func=ACT.Copy)
+        nc.scalar.copy(out=w_grouped[:, :, 0:2], in_=low_listed[:].rearrange("p t n -> p n t"))
+        high_listed = keep.tile([P, 2, NH], F32, name="high_listed")
+        nc.vector.tensor_copy(out=w_grouped[:, halves[0], 2], in_=planes[2][:].indirect(half_offsets(0)))
+        nc.vector.tensor_copy(out=high_listed[:, 0, :], in_=planes[2][:].indirect(half_offsets(1)))
+        nc.vector.tensor_copy(out=w_grouped[:, halves[0], 3], in_=planes[3][:].indirect(half_offsets(0)))
+        nc.scalar.activation(out=high_listed[:, 1, :], in_=planes[3][:].indirect(half_offsets(1)), func=ACT.Copy)
+        nc.scalar.copy(out=w_grouped[:, halves[1], 2:4], in_=high_listed[:].rearrange("p t n -> p n t"))
+        for cols in halves:
             nc.vector.quantize_mx(out=w_codes[:, cols].bitcast(E4M3), scales=w_scales[:, cols],
                                   in_=w_grouped[:, cols, :].rearrange("p n t -> p (n t)"))
-
-        pair_listed = keep.tile([P, 2, N], F32, name="pair_listed")
-        for t in range(2):
-            nc.scalar.activation(out=pair_listed[:, t, :], in_=planes[t][:].indirect(offsets[:]), func=ACT.Copy)
-        nc.scalar.copy(out=w_grouped[:, :, 0:2], in_=pair_listed[:].rearrange("p t n -> p n t"))
-        last_listed = keep.tile([P, 2, NH], F32, name="last_listed")
-        nc.vector.tensor_copy(out=w_grouped[:, 0:NH, 2], in_=planes[2][:].indirect(half_offsets(0)))
-        nc.vector.tensor_copy(out=last_listed[:, 0, :], in_=planes[2][:].indirect(half_offsets(1)))
-        nc.vector.tensor_copy(out=w_grouped[:, 0:NH, 3], in_=planes[3][:].indirect(half_offsets(0)))
-        nc.scalar.activation(out=last_listed[:, 1, :], in_=planes[3][:].indirect(half_offsets(1)), func=ACT.Copy)
-        nc.scalar.copy(out=w_grouped[:, NH:N, 2:4], in_=last_listed[:].rearrange("p t n -> p n t"))
-        for h in range(HALVES):
-            quantize_w(h)
 
         x_codes = keep.tile([P, R], U32, name="x_codes", align_bytes=64)
         x_scales = keep.tile([P, R], U8, name="x_scales", align_bytes=64)
@@ -92,27 +90,24 @@ def tile_attend_gcau_w_kernel(tc, xT, wT, y, wt, xm, offs, out):
         def weave_x(u):
             grouped = keep.tile([P, 2, P, PACK], BF16, name=f"x_grouped{u}", align_bytes=64)
             woven = grouped[:].rearrange("p e (c i) t -> p c t i e", i=2)
-            source = x_raw[:].rearrange("p t (c i j) -> p c t i j", i=2, j=PACK)[:, :, :, :, 2 * u:2 * u + 2]
+            source = x_raw[:].rearrange("p t (c i j) -> p c t i j", i=2, j=PACK)[:, :, :, :, pairs[u]]
             nc.vector.tensor_copy(out=woven[:, 0:P // 4], in_=source[:, 0:P // 4])
             nc.scalar.copy(out=woven[:, P // 4:P // 2], in_=source[:, P // 4:P // 2])
             return grouped
 
-        def quantize_x(grouped, u):
-            cols = slice(2 * u * P, (2 * u + 2) * P)
-            nc.vector.quantize_mx(out=x_codes[:, cols].bitcast(E4M3), scales=x_scales[:, cols],
-                                  in_=grouped[:].rearrange("p e s t -> p (e s t)"))
-
         x_grouped = [weave_x(u) for u in range(PAIRS)]
         for u in range(PAIRS):
-            quantize_x(x_grouped[u], u)
+            cols = slice(2 * u * P, (2 * u + 2) * P)
+            nc.vector.quantize_mx(out=x_codes[:, cols].bitcast(E4M3), scales=x_scales[:, cols],
+                                  in_=x_grouped[u][:].rearrange("p e s t -> p (e s t)"))
 
         q = [keep.tile([P, PACK, NH], F32, name=f"q{h}", tag=f"q{h}", align_bytes=64) for h in range(HALVES)]
         sq = [keep.tile([P, PACK, NH], F32, name=f"sq{h}", tag=f"sq{h}", align_bytes=64) for h in range(HALVES)]
-        root = [keep.tile([P, PACK, NH], F32, name=f"root{h}") for h in range(HALVES)]
-        part = [keep.tile([P, PACK, NH], F32, name="part0")]
+        right = [keep.tile([P, PACK, NH], F32, name=f"right{h}") for h in range(HALVES)]
+        left = [keep.tile([P, PACK, NH], F32, name="left0")]
 
         def residual(h, first, count, bank_tag):
-            cols = slice(h * NH, (h + 1) * NH)
+            cols = halves[h]
             bank = psum.tile([P, count, NH], F32, name=f"scores_{bank_tag}", tag=bank_tag)
             for e in range(count):
                 j = first + e
@@ -120,28 +115,15 @@ def tile_attend_gcau_w_kernel(tc, xT, wT, y, wt, xm, offs, out):
                     out=bank[:, e, :],
                     lhsT=x_codes[:, j * P:(j + 1) * P].bitcast(E4M3), lhsT_scale=x_scales[:, j * P:(j + 1) * P],
                     rhs=w_codes[:, cols].bitcast(E4M3), rhs_scale=w_scales[:, cols], start=True, stop=True)
-            u, e0 = divmod(first, 2)
+            u, in_pair = divmod(first, 2)
             nc.vector.tensor_tensor(out=q[h][:, first:first + count, :], in0=bank[:],
-                                    in1=y_sb[u][:, e0:e0 + count, cols], op=ALU.subtract)
+                                    in1=y_sb[u][:, in_pair:in_pair + count, cols], op=ALU.subtract)
 
-        def square(h, js):
-            nc.scalar.activation(out=sq[h][:, js, :], in_=q[h][:, js, :], func=ACT.Square)
+        def square(dst, src):
+            nc.scalar.activation(out=dst, in_=src, func=ACT.Square)
 
-        def inverse_root(h, js):
-            nc.scalar.activation(out=root[h][:, js, :], in_=sq[h][:, js, :], func=ACT.Abs_reciprocal_sqrt, bias=1.0)
-
-        def damping(h, js):
-            single = keep.tile([P, 2, NH], F32, name=f"single{js.start}")
-            nc.scalar.activation(out=single[:], in_=sq[h][:, js, :], func=ACT.Abs_reciprocal_sqrt, bias=1.0)
-            return single
-
-        def weigh_only(h, j):
-            nc.vector.tensor_scalar(out=part[h][:, j, :], in0=q[h][:, j, :], scalar1=wt_sb[:, j:j + 1],
-                                    scalar2=None, op0=ALU.mult)
-
-        def weigh(h, j):
-            nc.vector.scalar_tensor_tensor(out=part[h][:, j, :], in0=q[h][:, j, :], scalar=wt_sb[:, j:j + 1],
-                                           in1=root[h][:, j, :], op0=ALU.mult, op1=ALU.mult)
+        def inverse_root(dst, src):
+            nc.scalar.activation(out=dst, in_=src, func=ACT.Abs_reciprocal_sqrt, bias=1.0)
 
         g_grouped = keep.tile([P, N, PACK], BF16, name="g_grouped", align_bytes=64)
         g_codes = keep.tile([P, N], U32, name="g_codes", align_bytes=64)
@@ -152,8 +134,8 @@ def tile_attend_gcau_w_kernel(tc, xT, wT, y, wt, xm, offs, out):
             cols = slice(c * CH, (c + 1) * CH)
             nc.vector.tensor_tensor(
                 out=g_grouped[:, k * CH:(k + 1) * CH, :].rearrange("p (c i) j -> p c j i", i=2),
-                in0=part[h][:, :, cols].rearrange("p j (c i) -> p c j i", i=2),
-                in1=root[h][:, :, cols].rearrange("p j (c i) -> p c j i", i=2), op=ALU.mult)
+                in0=left[h][:, :, cols].rearrange("p j (c i) -> p c j i", i=2),
+                in1=right[h][:, :, cols].rearrange("p j (c i) -> p c j i", i=2), op=ALU.mult)
 
         def quantize_g(k):
             cols = slice(k * CH, (k + 1) * CH)
@@ -162,12 +144,6 @@ def tile_attend_gcau_w_kernel(tc, xT, wT, y, wt, xm, offs, out):
 
         xm_scales = keep.tile([P, D], U8, name="xm_scales", align_bytes=64)
         xm_codes = []
-
-        def weave_xm_first():
-            grouped = keep.tile([P, P, PACK], BF16, name="xm_grouped0", tag="part1", align_bytes=64)
-            nc.gpsimd.tensor_scalar(out=grouped[:], in0=xm_first[:].rearrange("p j d -> p d j"),
-                                    scalar1=1.0, scalar2=0.0, op0=ALU.mult, op1=ALU.add)
-            return grouped
 
         def weave_xm(copy, first, count, tag):
             grouped = keep.tile([P, count * P, PACK], BF16, name=f"xm_grouped{first}", tag=tag, align_bytes=64)
@@ -181,88 +157,85 @@ def tile_attend_gcau_w_kernel(tc, xT, wT, y, wt, xm, offs, out):
                                   in_=grouped[:].rearrange("p d j -> p (d j)"))
             xm_codes.extend(codes[:, e * P:(e + 1) * P] for e in range(count))
 
-        def product(acc, m, cols):
-            rows = slice(m * P, (m + 1) * P)
-            nc.tensor.matmul_mx(out=acc, lhsT=xm_codes[m].bitcast(E4M3), lhsT_scale=xm_scales[:, rows],
-                                rhs=g_codes[:, cols].bitcast(E5M2), rhs_scale=g_scales[:, cols], start=True, stop=True)
-
-        def products(parts, bank_tag):
-            width = sum(cols.stop - cols.start for m, cols in parts)
-            acc = psum.tile([P, width], F32, name=f"acc_{parts[0][0]}_{parts[0][1].start}", tag=bank_tag)
-            first = 0
-            for m, cols in parts:
-                product(acc[:, first:first + cols.stop - cols.start], m, cols)
-                first = first + cols.stop - cols.start
+        def product(m, h, bank_tag):
+            acc = psum.tile([P, NH], F32, name=f"acc{m}{h}", tag=bank_tag)
+            nc.tensor.matmul_mx(out=acc[:], lhsT=xm_codes[m].bitcast(E4M3), lhsT_scale=xm_scales[:, m * P:(m + 1) * P],
+                                rhs=g_codes[:, halves[h]].bitcast(E5M2), rhs_scale=g_scales[:, halves[h]],
+                                start=True, stop=True)
             return acc
 
-        def copy_out(copy, acc, width, name, tag):
-            dw = keep.tile([P, width], F32, name=name, tag=tag, align_bytes=64)
+        def copy_out(copy, m, h, bank_tag):
+            acc = product(m, h, bank_tag)
+            dw = keep.tile([P, NH], F32, name=f"dw{m}{h}", tag=f"dw{m}{h}", align_bytes=64)
             copy(out=dw[:], in_=acc[:])
             return dw
 
-        def scatter_vector(m, where, dw):
-            nc.vector.tensor_copy(out=windows[m][:].indirect(where), in_=dw)
+        def scatter_first_half(m, dw):
+            nc.scalar.activation(out=windows[m][:].indirect(half_offsets(0)), in_=dw, func=ACT.Copy)
 
-        def scatter_scalar(m, where, dw):
-            nc.scalar.activation(out=windows[m][:].indirect(where), in_=dw, func=ACT.Copy)
-
-        def store(m):
+        def scatter_second_half_and_store(m, dw):
+            nc.vector.tensor_copy(out=windows[m][:].indirect(half_offsets(1)), in_=dw)
             nc.sync.dma_start(out=out[m * P:(m + 1) * P, :], in_=windows[m][:])
-
-        halves = [slice(h * NH, (h + 1) * NH) for h in range(HALVES)]
-        pairs = [slice(2 * u, 2 * u + 2) for u in range(PAIRS)]
-        chunks = [slice(k * CH, (k + 1) * CH) for k in range(CHUNKS)]
-        tiles = [slice(j, j + 1) for j in range(PACK)]
 
         for j in range(PACK):
             residual(0, j, 1, f"bank{j}")
         for u in range(PAIRS):
-            residual(1, 2 * u, 2, f"bank{4 + u}")
+            residual(1, 2 * u, 2, f"bank{PACK + u}")
+
         for u in range(PAIRS):
             for j in (2 * u, 2 * u + 1):
-                square(0, tiles[j])
+                square(sq[0][:, j:j + 1, :], q[0][:, j:j + 1, :])
             for j in (2 * u, 2 * u + 1):
-                inverse_root(0, tiles[j])
-        xm0 = weave_xm_first()
+                inverse_root(right[0][:, j:j + 1, :], sq[0][:, j:j + 1, :])
+
+        xm0 = keep.tile([P, P, PACK], BF16, name="xm_grouped0", tag="left1", align_bytes=64)
+        nc.gpsimd.tensor_scalar(out=xm0[:], in0=xm_first[:].rearrange("p j d -> p d j"),
+                                scalar1=1.0, scalar2=0.0, op0=ALU.mult, op1=ALU.add)
+
         for js in pairs:
-            square(1, js)
-        singles = [damping(1, js) for js in pairs]
+            square(sq[1][:, js, :], q[1][:, js, :])
+        roots = []
         for u in range(PAIRS):
-            nc.scalar.activation(out=root[1][:, pairs[u], :], in_=singles[u][:], func=ACT.Square)
+            roots.append(keep.tile([P, 2, NH], F32, name=f"root{u}"))
+            inverse_root(roots[u][:], sq[1][:, pairs[u], :])
+        for u in range(PAIRS):
+            square(right[1][:, pairs[u], :], roots[u][:])
+
         for j in range(PACK):
-            weigh(0, j)
+            nc.vector.scalar_tensor_tensor(out=left[0][:, j, :], in0=q[0][:, j, :], scalar=wt_sb[:, j:j + 1],
+                                           in1=right[0][:, j, :], op0=ALU.mult, op1=ALU.mult)
         quantize_xm(xm0, 0, 1, "xm_codes0")
         gradient(0)
         gradient(1)
         quantize_g(0)
         quantize_g(1)
         xm1 = weave_xm(nc.scalar.copy, 1, 1, "sq1")
-        dw00 = copy_out(nc.scalar.copy, products([(0, halves[0])], "bank6"), NH, "dw00", "dw00")
-        scatter_scalar(0, half_offsets(0), dw00[:])
-        part.append(keep.tile([P, PACK, NH], F32, name="part1", tag="part1", align_bytes=64))
+        scatter_first_half(0, copy_out(nc.scalar.copy, 0, 0, "bank6")[:])
+
+        left.append(keep.tile([P, PACK, NH], F32, name="left1", tag="left1", align_bytes=64))
         for j in range(PACK):
-            weigh_only(1, j)
+            nc.vector.tensor_scalar(out=left[1][:, j, :], in0=q[1][:, j, :], scalar1=wt_sb[:, j:j + 1],
+                                    scalar2=None, op0=ALU.mult)
         gradient(2)
         gradient(3)
         quantize_g(2)
         quantize_xm(xm1, 1, 1, "q1")
         quantize_g(3)
-        xm23 = weave_xm(nc.vector.tensor_copy, 2, 2, "part1")
-        dw01 = copy_out(nc.vector.tensor_copy, products([(0, halves[1])], "bank0"), NH, "dw01", "dw01")
+
+        xm23 = weave_xm(nc.vector.tensor_copy, 2, 2, "left1")
+        dw01 = copy_out(nc.vector.tensor_copy, 0, 1, "bank0")
         quantize_xm(xm23, 2, 2, "xm_codes2")
-        scatter_vector(0, half_offsets(1), dw01[:])
-        store(0)
-        dw10 = copy_out(nc.scalar.copy, products([(1, halves[0])], "bank7"), NH, "dw10", "dw10")
-        scatter_scalar(1, half_offsets(0), dw10[:])
-        dw11 = copy_out(nc.scalar.copy, products([(1, halves[1])], "bank1"), NH, "dw11", "dw11")
-        scatter_vector(1, half_offsets(1), dw11[:])
-        store(1)
-        dw2 = copy_out(nc.scalar.copy, products([(2, slice(0, N))], "bank2"), N, "dw2", "dw10")
-        dw30 = copy_out(nc.scalar.copy, products([(3, halves[0])], "bank3"), NH, "dw30", "dw30")
-        dw31 = copy_out(nc.vector.tensor_copy, products([(3, halves[1])], "bank4"), NH, "dw31", "dw11")
-        scatter_scalar(2, half_offsets(0), dw2[:, halves[0]])
-        scatter_vector(2, half_offsets(1), dw2[:, halves[1]])
-        store(2)
-        scatter_scalar(3, half_offsets(0), dw30[:])
-        scatter_vector(3, half_offsets(1), dw31[:])
-        store(3)
+        scatter_second_half_and_store(0, dw01[:])
+
+        scatter_first_half(1, copy_out(nc.scalar.copy, 1, 0, "bank7")[:])
+        scatter_second_half_and_store(1, copy_out(nc.scalar.copy, 1, 1, "bank1")[:])
+
+        dw_first = keep.tile([P, 2, NH], F32, name="dw_first", tag="dw10", align_bytes=64)
+        dw_second = keep.tile([P, 2, NH], F32, name="dw_second", tag="dw11", align_bytes=64)
+        for e in range(2):
+            nc.scalar.copy(out=dw_first[:, e, :], in_=product(2 + e, 0, f"bank{2 + e}")[:])
+        for e in range(2):
+            nc.vector.tensor_copy(out=dw_second[:, e, :], in_=product(2 + e, 1, f"bank{PACK + e}")[:])
+        for e in range(2):
+            scatter_first_half(2 + e, dw_first[:, e, :])
+            scatter_second_half_and_store(2 + e, dw_second[:, e, :])

@@ -23,6 +23,7 @@ HALVES = 2
 NH = N // HALVES
 CH = 128
 TILES = D // P
+X_CUTS = (42, 22)
 
 
 def tile_attend_gcau_w_kernel(tc, xT, wT, y, wt, xm, offs, out):
@@ -36,21 +37,22 @@ def tile_attend_gcau_w_kernel(tc, xT, wT, y, wt, xm, offs, out):
         planes = [keep.tile([P, T], F32, name=f"plane{t}") for t in range(PACK)]
         nc.sync.dma_start(out=planes[0][:], in_=w_view[:, 0, :])
         nc.sync.dma_start(offsets[:], offs)
+        wt_sb = keep.tile([P, PACK], F32, name="wt_sb")
+        nc.sync.dma_start(out=wt_sb[:], in_=wt[0].rearrange("(p j) o -> p (j o)", j=PACK))
         for t in range(1, PACK):
             nc.sync.dma_start(out=planes[t][:], in_=w_view[:, t, :])
         x_raw = keep.tile([P, PACK, R], F32, name="x_raw")
         nc.sync.dma_start(out=x_raw[:], in_=xT[0].rearrange("(p t) r -> p t r", t=PACK))
         y_view = y[0].rearrange("(p j) n -> p j n", j=PACK)
         y_sb = [keep.tile([P, 2, N], F32, name=f"y_sb{u}") for u in range(PAIRS)]
-        wt_sb = keep.tile([P, PACK], F32, name="wt_sb")
         for u in range(PAIRS):
             nc.sync.dma_start(out=y_sb[u][:], in_=y_view[:, 2 * u:2 * u + 2, :])
         xm_view = xm[0].rearrange("(p j) d -> p j d", j=PACK)
-        xm_first = keep.tile([P, PACK, P], F32, name="xm_first")
-        nc.sync.dma_start(out=xm_first[:], in_=xm_view[:, :, 0:P])
-        nc.sync.dma_start(out=wt_sb[:], in_=wt[0].rearrange("(p j) o -> p (j o)", j=PACK))
-        xm_rest = keep.tile([P, PACK, D - P], F32, name="xm_rest")
-        nc.sync.dma_start(out=xm_rest[:], in_=xm_view[:, :, P:])
+        xm_early = [keep.tile([P, PACK, P], F32, name=f"xm_early{m}") for m in range(2)]
+        for m in range(2):
+            nc.sync.dma_start(out=xm_early[m][:], in_=xm_view[:, :, m * P:(m + 1) * P])
+        xm_late = keep.tile([P, PACK, 2 * P], F32, name="xm_late")
+        nc.sync.dma_start(out=xm_late[:], in_=xm_view[:, :, 2 * P:])
 
         windows = [keep.tile([P, T], F32, name=f"window{m}") for m in range(TILES)]
         for win in windows:
@@ -60,6 +62,12 @@ def tile_attend_gcau_w_kernel(tc, xT, wT, y, wt, xm, offs, out):
         warm_out = keep.tile([P, 1], F32, name="warm_out")
         nc.gpsimd.memset(warm_in[:], 0.0)
         nc.scalar.activation(out=warm_out[:], in_=warm_in[:], func=ACT.Abs_reciprocal_sqrt, bias=1.0)
+
+        wt_safe = keep.tile([P, PACK], F32, name="wt_safe")
+        wt_inv = keep.tile([P, PACK], F32, name="wt_inv")
+        nc.vector.scalar_tensor_tensor(out=wt_safe[:], in0=wt_sb[:], scalar=0.0, in1=wt_sb[:],
+                                       op0=ALU.is_equal, op1=ALU.add)
+        nc.vector.reciprocal(out=wt_inv[:], in_=wt_safe[:])
 
         halves = [slice(h * NH, (h + 1) * NH) for h in range(HALVES)]
         pairs = [slice(2 * u, 2 * u + 2) for u in range(PAIRS)]
@@ -87,26 +95,39 @@ def tile_attend_gcau_w_kernel(tc, xT, wT, y, wt, xm, offs, out):
         x_codes = keep.tile([P, R], U32, name="x_codes", align_bytes=64)
         x_scales = keep.tile([P, R], U8, name="x_scales", align_bytes=64)
 
-        def weave_x(u):
+        def weave_x(u, cut):
             grouped = keep.tile([P, 2, P, PACK], BF16, name=f"x_grouped{u}", align_bytes=64)
             woven = grouped[:].rearrange("p e (c i) t -> p c t i e", i=2)
             source = x_raw[:].rearrange("p t (c i j) -> p c t i j", i=2, j=PACK)[:, :, :, :, pairs[u]]
-            nc.vector.tensor_copy(out=woven[:, 0:P // 4], in_=source[:, 0:P // 4])
-            nc.scalar.copy(out=woven[:, P // 4:P // 2], in_=source[:, P // 4:P // 2])
+            nc.vector.tensor_copy(out=woven[:, 0:cut], in_=source[:, 0:cut])
+            nc.scalar.copy(out=woven[:, cut:P // 2], in_=source[:, cut:P // 2])
             return grouped
 
-        x_grouped = [weave_x(u) for u in range(PAIRS)]
-        for u in range(PAIRS):
-            cols = slice(2 * u * P, (2 * u + 2) * P)
+        x_grouped = [weave_x(u, cut) for u, cut in enumerate(X_CUTS)]
+        for u, first, count in ((0, 0, 1), (0, 1, 1), (1, 0, 2)):
+            cols = slice((2 * u + first) * P, (2 * u + first + count) * P)
             nc.vector.quantize_mx(out=x_codes[:, cols].bitcast(E4M3), scales=x_scales[:, cols],
-                                  in_=x_grouped[u][:].rearrange("p e s t -> p (e s t)"))
+                                  in_=x_grouped[u][:, first:first + count].rearrange("p e s t -> p (e s t)"))
 
-        q = [keep.tile([P, PACK, NH], F32, name=f"q{h}", tag=f"q{h}", align_bytes=64) for h in range(HALVES)]
-        sq = [keep.tile([P, PACK, NH], F32, name=f"sq{h}", tag=f"sq{h}", align_bytes=64) for h in range(HALVES)]
+        y_weighed = [keep.tile([P, NH], F32, name=f"y_weighed{j}") for j in range(PACK)]
+        for j in range(2):
+            nc.scalar.activation(out=y_weighed[j][:], in_=y_sb[0][:, j, halves[1]], func=ACT.Copy,
+                                 scale=wt_sb[:, j:j + 1])
+        for j in range(2, PACK):
+            nc.gpsimd.tensor_scalar(out=y_weighed[j][:], in0=y_sb[1][:, j - 2, halves[1]],
+                                    scalar1=wt_sb[:, j:j + 1], scalar2=0.0, op0=ALU.mult, op1=ALU.add)
+        xm_grouped = []
+        for m in range(2):
+            xm_grouped.append(keep.tile([P, P, PACK], BF16, name=f"xm_grouped{m}", align_bytes=64))
+            nc.gpsimd.tensor_scalar(out=xm_grouped[m][:], in0=xm_early[m][:].rearrange("p j d -> p d j"),
+                                    scalar1=1.0, scalar2=0.0, op0=ALU.mult, op1=ALU.add)
+
+        q0 = keep.tile([P, PACK, NH], F32, name="q0")
+        left = [keep.tile([P, PACK, NH], F32, name=f"left{h}", tag=f"left{h}", align_bytes=64) for h in range(HALVES)]
+        sq = [keep.tile([P, PACK, NH], F32, name=f"sq{h}", tag=f"sq{h}") for h in range(HALVES)]
         right = [keep.tile([P, PACK, NH], F32, name=f"right{h}") for h in range(HALVES)]
-        left = [keep.tile([P, PACK, NH], F32, name="left0")]
 
-        def residual(h, first, count, bank_tag):
+        def scores(h, first, count, bank_tag):
             cols = halves[h]
             bank = psum.tile([P, count, NH], F32, name=f"scores_{bank_tag}", tag=bank_tag)
             for e in range(count):
@@ -115,17 +136,16 @@ def tile_attend_gcau_w_kernel(tc, xT, wT, y, wt, xm, offs, out):
                     out=bank[:, e, :],
                     lhsT=x_codes[:, j * P:(j + 1) * P].bitcast(E4M3), lhsT_scale=x_scales[:, j * P:(j + 1) * P],
                     rhs=w_codes[:, cols].bitcast(E4M3), rhs_scale=w_scales[:, cols], start=True, stop=True)
-            u, in_pair = divmod(first, 2)
-            nc.vector.tensor_tensor(out=q[h][:, first:first + count, :], in0=bank[:],
-                                    in1=y_sb[u][:, in_pair:in_pair + count, cols], op=ALU.subtract)
+            return bank
 
-        def square(dst, src):
-            nc.scalar.activation(out=dst, in_=src, func=ACT.Square)
+        def square(dst, src, scale=1.0):
+            nc.scalar.activation(out=dst, in_=src, func=ACT.Square, scale=scale)
 
         def inverse_root(dst, src):
             nc.scalar.activation(out=dst, in_=src, func=ACT.Abs_reciprocal_sqrt, bias=1.0)
 
-        g_grouped = keep.tile([P, N, PACK], BF16, name="g_grouped", align_bytes=64)
+        g_grouped = [keep.tile([P, CH, PACK], BF16, name=f"g_grouped{k}", tag=f"g_grouped{k}", align_bytes=64)
+                     for k in range(N // CH)]
         g_codes = keep.tile([P, N], U32, name="g_codes", align_bytes=64)
         g_scales = keep.tile([P, N], U8, name="g_scales", align_bytes=64)
 
@@ -133,107 +153,119 @@ def tile_attend_gcau_w_kernel(tc, xT, wT, y, wt, xm, offs, out):
             h, c = divmod(k, NH // CH)
             cols = slice(c * CH, (c + 1) * CH)
             nc.vector.tensor_tensor(
-                out=g_grouped[:, k * CH:(k + 1) * CH, :].rearrange("p (c i) j -> p c j i", i=2),
+                out=g_grouped[k][:].rearrange("p (c i) j -> p c j i", i=2),
                 in0=left[h][:, :, cols].rearrange("p j (c i) -> p c j i", i=2),
                 in1=right[h][:, :, cols].rearrange("p j (c i) -> p c j i", i=2), op=ALU.mult)
 
         def quantize_g(k):
             cols = slice(k * CH, (k + 1) * CH)
             nc.vector.quantize_mx(out=g_codes[:, cols].bitcast(E5M2), scales=g_scales[:, cols],
-                                  in_=g_grouped[:, cols, :].rearrange("p n j -> p (n j)"))
+                                  in_=g_grouped[k][:].rearrange("p n j -> p (n j)"))
 
         xm_scales = keep.tile([P, D], U8, name="xm_scales", align_bytes=64)
-        xm_codes = []
+        xm_codes = keep.tile([P, D], U32, name="xm_codes", align_bytes=64)
 
-        def weave_xm(copy, first, count, tag):
-            grouped = keep.tile([P, count * P, PACK], BF16, name=f"xm_grouped{first}", tag=tag, align_bytes=64)
-            copy(out=grouped[:].rearrange("p (c i) j -> p c j i", i=4),
-                 in_=xm_rest[:, :, (first - 1) * P:(first - 1 + count) * P].rearrange("p j (c i) -> p c j i", i=4))
+        def weave_xm(m, tag):
+            grouped = keep.tile([P, P, PACK], BF16, name=f"xm_grouped{m}", tag=tag, align_bytes=64)
+            nc.vector.tensor_copy(out=grouped[:].rearrange("p (c i) j -> p c j i", i=4),
+                                  in_=xm_late[:, :, (m - 2) * P:(m - 1) * P].rearrange("p j (c i) -> p c j i", i=4))
             return grouped
 
-        def quantize_xm(grouped, first, count, tag):
-            codes = keep.tile([P, count * P], U32, name=f"xm_codes{first}", tag=tag, align_bytes=64)
-            nc.vector.quantize_mx(out=codes[:].bitcast(E4M3), scales=xm_scales[:, first * P:(first + count) * P],
+        def quantize_xm(grouped, first, count):
+            cols = slice(first * P, (first + count) * P)
+            nc.vector.quantize_mx(out=xm_codes[:, cols].bitcast(E4M3), scales=xm_scales[:, cols],
                                   in_=grouped[:].rearrange("p d j -> p (d j)"))
-            xm_codes.extend(codes[:, e * P:(e + 1) * P] for e in range(count))
 
         def product(m, h, bank_tag):
             acc = psum.tile([P, NH], F32, name=f"acc{m}{h}", tag=bank_tag)
-            nc.tensor.matmul_mx(out=acc[:], lhsT=xm_codes[m].bitcast(E4M3), lhsT_scale=xm_scales[:, m * P:(m + 1) * P],
-                                rhs=g_codes[:, halves[h]].bitcast(E5M2), rhs_scale=g_scales[:, halves[h]],
-                                start=True, stop=True)
+            product_in(acc[:], m, h)
             return acc
 
-        def copy_out(copy, m, h, bank_tag):
+        def product_in(acc, m, h):
+            cols = slice(m * P, (m + 1) * P)
+            nc.tensor.matmul_mx(out=acc, lhsT=xm_codes[:, cols].bitcast(E4M3), lhsT_scale=xm_scales[:, cols],
+                                rhs=g_codes[:, halves[h]].bitcast(E5M2), rhs_scale=g_scales[:, halves[h]],
+                                start=True, stop=True)
+
+        def copy_out(copy, m, h, bank_tag, tag):
             acc = product(m, h, bank_tag)
-            dw = keep.tile([P, NH], F32, name=f"dw{m}{h}", tag=f"dw{m}{h}", align_bytes=64)
+            dw = keep.tile([P, NH], F32, name=f"dw{m}{h}", tag=tag)
             copy(out=dw[:], in_=acc[:])
             return dw
 
         def scatter_first_half(m, dw):
-            nc.scalar.activation(out=windows[m][:].indirect(half_offsets(0)), in_=dw, func=ACT.Copy)
+            nc.scalar.activation(out=windows[m][:].indirect(half_offsets(0)), in_=dw[:], func=ACT.Copy)
 
         def scatter_second_half_and_store(m, dw):
-            nc.vector.tensor_copy(out=windows[m][:].indirect(half_offsets(1)), in_=dw)
+            nc.vector.tensor_copy(out=windows[m][:].indirect(half_offsets(1)), in_=dw[:])
             nc.sync.dma_start(out=out[m * P:(m + 1) * P, :], in_=windows[m][:])
 
         for j in range(PACK):
-            residual(0, j, 1, f"bank{j}")
+            bank = scores(0, j, 1, f"bank{j}")
+            nc.vector.tensor_tensor(out=q0[:, j, :], in0=bank[:, 0, :], in1=y_sb[j // 2][:, j % 2, halves[0]],
+                                    op=ALU.subtract)
         for u in range(PAIRS):
-            residual(1, 2 * u, 2, f"bank{PACK + u}")
+            bank = scores(1, 2 * u, 2, f"bank{PACK + u}")
+            for e in range(2):
+                j = 2 * u + e
+                nc.vector.scalar_tensor_tensor(out=left[1][:, j, :], in0=bank[:, e, :], scalar=wt_sb[:, j:j + 1],
+                                               in1=y_weighed[j][:], op0=ALU.mult, op1=ALU.subtract)
 
         for u in range(PAIRS):
             for j in (2 * u, 2 * u + 1):
-                square(sq[0][:, j:j + 1, :], q[0][:, j:j + 1, :])
+                square(sq[0][:, j, :], q0[:, j, :])
             for j in (2 * u, 2 * u + 1):
-                inverse_root(right[0][:, j:j + 1, :], sq[0][:, j:j + 1, :])
-
-        xm0 = keep.tile([P, P, PACK], BF16, name="xm_grouped0", tag="left1", align_bytes=64)
-        nc.gpsimd.tensor_scalar(out=xm0[:], in0=xm_first[:].rearrange("p j d -> p d j"),
-                                scalar1=1.0, scalar2=0.0, op0=ALU.mult, op1=ALU.add)
-
-        for js in pairs:
-            square(sq[1][:, js, :], q[1][:, js, :])
+                inverse_root(right[0][:, j, :], sq[0][:, j, :])
+        for j in range(PACK):
+            square(sq[1][:, j, :], left[1][:, j, :], wt_inv[:, j:j + 1])
+        chunks = [slice(c * CH, (c + 1) * CH) for c in range(NH // CH)]
         roots = []
-        for u in range(PAIRS):
-            roots.append(keep.tile([P, 2, NH], F32, name=f"root{u}"))
-            inverse_root(roots[u][:], sq[1][:, pairs[u], :])
-        for u in range(PAIRS):
-            square(right[1][:, pairs[u], :], roots[u][:])
+        for c, cols in enumerate(chunks):
+            roots.append(keep.tile([P, PACK, CH], F32, name=f"root{c}", tag=f"root{c}"))
+            inverse_root(roots[c][:], sq[1][:, :, cols])
+        for c, cols in enumerate(chunks):
+            square(right[1][:, :, cols], roots[c][:])
 
         for j in range(PACK):
-            nc.vector.scalar_tensor_tensor(out=left[0][:, j, :], in0=q[0][:, j, :], scalar=wt_sb[:, j:j + 1],
+            nc.vector.scalar_tensor_tensor(out=left[0][:, j, :], in0=q0[:, j, :], scalar=wt_sb[:, j:j + 1],
                                            in1=right[0][:, j, :], op0=ALU.mult, op1=ALU.mult)
-        quantize_xm(xm0, 0, 1, "xm_codes0")
+        quantize_xm(xm_grouped[0], 0, 1)
         gradient(0)
         gradient(1)
         quantize_g(0)
         quantize_g(1)
-        xm1 = weave_xm(nc.scalar.copy, 1, 1, "sq1")
-        scatter_first_half(0, copy_out(nc.scalar.copy, 0, 0, "bank6")[:])
-
-        left.append(keep.tile([P, PACK, NH], F32, name="left1", tag="left1", align_bytes=64))
-        for j in range(PACK):
-            nc.vector.tensor_scalar(out=left[1][:, j, :], in0=q[1][:, j, :], scalar1=wt_sb[:, j:j + 1],
-                                    scalar2=None, op0=ALU.mult)
+        quantize_xm(xm_grouped[1], 1, 1)
+        joint = psum.tile([P, 2, NH], F32, name="joint", tag="bank6")
+        dw_early = keep.tile([P, 2, NH], F32, name="dw_early", tag="sq1")
+        for m in range(2):
+            product_in(joint[:, m, :], m, 0)
+        for m in range(2):
+            nc.scalar.copy(out=dw_early[:, m, :], in_=joint[:, m, :])
+        for m in range(2):
+            scatter_first_half(m, dw_early[:, m, :])
+        xm2 = weave_xm(2, "g_grouped0")
         gradient(2)
         gradient(3)
         quantize_g(2)
-        quantize_xm(xm1, 1, 1, "q1")
         quantize_g(3)
 
-        xm23 = weave_xm(nc.vector.tensor_copy, 2, 2, "left1")
-        dw01 = copy_out(nc.vector.tensor_copy, 0, 1, "bank0")
-        quantize_xm(xm23, 2, 2, "xm_codes2")
-        scatter_second_half_and_store(0, dw01[:])
+        quantize_xm(xm2, 2, 1)
+        xm3 = weave_xm(3, "left1")
+        dw01 = copy_out(nc.vector.tensor_copy, 0, 1, "bank0", "dw01")
+        quantize_xm(xm3, 3, 1)
+        scatter_second_half_and_store(0, dw01)
 
-        scatter_first_half(1, copy_out(nc.scalar.copy, 1, 0, "bank7")[:])
-        scatter_second_half_and_store(1, copy_out(nc.scalar.copy, 1, 1, "bank1")[:])
+        joint = psum.tile([P, 2, NH], F32, name="joint_late", tag="bank1")
+        product_in(joint[:, 0, :], 1, 1)
+        product_in(joint[:, 1, :], 2, 0)
+        dw11 = keep.tile([P, NH], F32, name="dw11", tag="dw11")
+        nc.scalar.copy(out=dw11[:], in_=joint[:, 0, :])
+        scatter_second_half_and_store(1, dw11)
 
-        dw_first = keep.tile([P, 2, NH], F32, name="dw_first", tag="dw10", align_bytes=64)
-        dw_second = keep.tile([P, 2, NH], F32, name="dw_second", tag="dw11", align_bytes=64)
-        for e in range(2):
-            nc.scalar.copy(out=dw_first[:, e, :], in_=product(2 + e, 0, f"bank{2 + e}")[:])
+        dw_first = keep.tile([P, 2, NH], F32, name="dw_first", tag="sq1")
+        dw_second = keep.tile([P, 2, NH], F32, name="dw_second", tag="dw11")
+        nc.scalar.copy(out=dw_first[:, 0, :], in_=joint[:, 1, :])
+        nc.scalar.copy(out=dw_first[:, 1, :], in_=product(3, 0, "bank3")[:])
         for e in range(2):
             nc.vector.tensor_copy(out=dw_second[:, e, :], in_=product(2 + e, 1, f"bank{PACK + e}")[:])
         for e in range(2):

@@ -48,11 +48,10 @@ def tile_attend_gcau_w_kernel(tc, xT, wT, y, wt, xm, offs, out):
         for u in range(PAIRS):
             nc.sync.dma_start(out=y_sb[u][:], in_=y_view[:, 2 * u:2 * u + 2, :])
         xm_view = xm[0].rearrange("(p j) d -> p j d", j=PACK)
-        xm_early = [keep.tile([P, PACK, P], F32, name=f"xm_early{m}") for m in range(2)]
-        for m in range(2):
-            nc.sync.dma_start(out=xm_early[m][:], in_=xm_view[:, :, m * P:(m + 1) * P])
-        xm_late = keep.tile([P, PACK, 2 * P], F32, name="xm_late")
-        nc.sync.dma_start(out=xm_late[:], in_=xm_view[:, :, 2 * P:])
+        xm_first = keep.tile([P, PACK, P], F32, name="xm_first")
+        nc.sync.dma_start(out=xm_first[:], in_=xm_view[:, :, 0:P])
+        xm_rest = keep.tile([P, PACK, D - P], F32, name="xm_rest")
+        nc.sync.dma_start(out=xm_rest[:], in_=xm_view[:, :, P:])
 
         windows = [keep.tile([P, T], F32, name=f"window{m}") for m in range(TILES)]
         for win in windows:
@@ -116,11 +115,9 @@ def tile_attend_gcau_w_kernel(tc, xT, wT, y, wt, xm, offs, out):
         for j in range(2, PACK):
             nc.gpsimd.tensor_scalar(out=y_weighed[j][:], in0=y_sb[1][:, j - 2, halves[1]],
                                     scalar1=wt_sb[:, j:j + 1], scalar2=0.0, op0=ALU.mult, op1=ALU.add)
-        xm_grouped = []
-        for m in range(2):
-            xm_grouped.append(keep.tile([P, P, PACK], BF16, name=f"xm_grouped{m}", align_bytes=64))
-            nc.gpsimd.tensor_scalar(out=xm_grouped[m][:], in0=xm_early[m][:].rearrange("p j d -> p d j"),
-                                    scalar1=1.0, scalar2=0.0, op0=ALU.mult, op1=ALU.add)
+        xm0 = keep.tile([P, P, PACK], BF16, name="xm_grouped0", align_bytes=64)
+        nc.gpsimd.tensor_scalar(out=xm0[:], in0=xm_first[:].rearrange("p j d -> p d j"),
+                                scalar1=1.0, scalar2=0.0, op0=ALU.mult, op1=ALU.add)
 
         q0 = keep.tile([P, PACK, NH], F32, name="q0")
         left = [keep.tile([P, PACK, NH], F32, name=f"left{h}", tag=f"left{h}", align_bytes=64) for h in range(HALVES)]
@@ -165,10 +162,10 @@ def tile_attend_gcau_w_kernel(tc, xT, wT, y, wt, xm, offs, out):
         xm_scales = keep.tile([P, D], U8, name="xm_scales", align_bytes=64)
         xm_codes = keep.tile([P, D], U32, name="xm_codes", align_bytes=64)
 
-        def weave_xm(m, tag):
-            grouped = keep.tile([P, P, PACK], BF16, name=f"xm_grouped{m}", tag=tag, align_bytes=64)
+        def weave_xm(m, count, tag):
+            grouped = keep.tile([P, count * P, PACK], BF16, name=f"xm_grouped{m}", tag=tag, align_bytes=64)
             nc.vector.tensor_copy(out=grouped[:].rearrange("p (c i) j -> p c j i", i=4),
-                                  in_=xm_late[:, :, (m - 2) * P:(m - 1) * P].rearrange("p j (c i) -> p c j i", i=4))
+                                  in_=xm_rest[:, :, (m - 1) * P:(m - 1 + count) * P].rearrange("p j (c i) -> p c j i", i=4))
             return grouped
 
         def quantize_xm(grouped, first, count):
@@ -229,30 +226,25 @@ def tile_attend_gcau_w_kernel(tc, xT, wT, y, wt, xm, offs, out):
         for j in range(PACK):
             nc.vector.scalar_tensor_tensor(out=left[0][:, j, :], in0=q0[:, j, :], scalar=wt_sb[:, j:j + 1],
                                            in1=right[0][:, j, :], op0=ALU.mult, op1=ALU.mult)
-        quantize_xm(xm_grouped[0], 0, 1)
+        quantize_xm(xm0, 0, 1)
         gradient(0)
         gradient(1)
         quantize_g(0)
         quantize_g(1)
-        quantize_xm(xm_grouped[1], 1, 1)
-        joint = psum.tile([P, 2, NH], F32, name="joint", tag="bank6")
+        quantize_xm(weave_xm(1, 1, "g_grouped0"), 1, 1)
         dw_early = keep.tile([P, 2, NH], F32, name="dw_early", tag="sq1")
         for m in range(2):
-            product_in(joint[:, m, :], m, 0)
-        for m in range(2):
-            nc.scalar.copy(out=dw_early[:, m, :], in_=joint[:, m, :])
+            nc.scalar.copy(out=dw_early[:, m, :], in_=product(m, 0, f"bank{6 + m}")[:])
         for m in range(2):
             scatter_first_half(m, dw_early[:, m, :])
-        xm2 = weave_xm(2, "g_grouped0")
         gradient(2)
         gradient(3)
         quantize_g(2)
         quantize_g(3)
 
-        quantize_xm(xm2, 2, 1)
-        xm3 = weave_xm(3, "left1")
+        xm23 = weave_xm(2, 2, "left1")
         dw01 = copy_out(nc.vector.tensor_copy, 0, 1, "bank0", "dw01")
-        quantize_xm(xm3, 3, 1)
+        quantize_xm(xm23, 2, 2)
         scatter_second_half_and_store(0, dw01)
 
         joint = psum.tile([P, 2, NH], F32, name="joint_late", tag="bank1")

@@ -119,7 +119,7 @@ def tile_attend_gcau_w_kernel(tc, xT, wT, y, wt, xm, offs, out):
         nc.gpsimd.tensor_scalar(out=xm0[:], in0=xm_first[:].rearrange("p j d -> p d j"),
                                 scalar1=1.0, scalar2=0.0, op0=ALU.mult, op1=ALU.add)
 
-        q0 = keep.tile([P, PACK, NH], F32, name="q0")
+        q0 = keep.tile([P, PACK, NH], F32, name="q0", tag="q0", align_bytes=64)
         left = [keep.tile([P, PACK, NH], F32, name=f"left{h}", tag=f"left{h}", align_bytes=64) for h in range(HALVES)]
         sq = [keep.tile([P, PACK, NH], F32, name=f"sq{h}", tag=f"sq{h}") for h in range(HALVES)]
         right = [keep.tile([P, PACK, NH], F32, name=f"right{h}") for h in range(HALVES)]
@@ -141,23 +141,22 @@ def tile_attend_gcau_w_kernel(tc, xT, wT, y, wt, xm, offs, out):
         def inverse_root(dst, src):
             nc.scalar.activation(out=dst, in_=src, func=ACT.Abs_reciprocal_sqrt, bias=1.0)
 
-        g_grouped = [keep.tile([P, CH, PACK], BF16, name=f"g_grouped{k}", tag=f"g_grouped{k}", align_bytes=64)
-                     for k in range(N // CH)]
+        g_grouped = keep.tile([P, N, PACK], BF16, name="g_grouped", align_bytes=64)
         g_codes = keep.tile([P, N], U32, name="g_codes", align_bytes=64)
         g_scales = keep.tile([P, N], U8, name="g_scales", align_bytes=64)
 
-        def gradient(k):
-            h, c = divmod(k, NH // CH)
-            cols = slice(c * CH, (c + 1) * CH)
+        def gradient(first, count):
+            h, c = divmod(first, NH)
+            cols = slice(c, c + count)
             nc.vector.tensor_tensor(
-                out=g_grouped[k][:].rearrange("p (c i) j -> p c j i", i=2),
+                out=g_grouped[:, first:first + count, :].rearrange("p (c i) j -> p c j i", i=2),
                 in0=left[h][:, :, cols].rearrange("p j (c i) -> p c j i", i=2),
                 in1=right[h][:, :, cols].rearrange("p j (c i) -> p c j i", i=2), op=ALU.mult)
 
-        def quantize_g(k):
-            cols = slice(k * CH, (k + 1) * CH)
+        def quantize_g(first, count):
+            cols = slice(first, first + count)
             nc.vector.quantize_mx(out=g_codes[:, cols].bitcast(E5M2), scales=g_scales[:, cols],
-                                  in_=g_grouped[k][:].rearrange("p n j -> p (n j)"))
+                                  in_=g_grouped[:, cols, :].rearrange("p n j -> p (n j)"))
 
         xm_scales = keep.tile([P, D], U8, name="xm_scales", align_bytes=64)
         xm_codes = keep.tile([P, D], U32, name="xm_codes", align_bytes=64)
@@ -197,7 +196,13 @@ def tile_attend_gcau_w_kernel(tc, xT, wT, y, wt, xm, offs, out):
             nc.vector.tensor_copy(out=windows[m][:].indirect(half_offsets(1)), in_=dw[:])
             nc.sync.dma_start(out=out[m * P:(m + 1) * P, :], in_=windows[m][:])
 
-        for j in range(PACK):
+        chunks = [slice(c * CH, (c + 1) * CH) for c in range(NH // CH)]
+        for c, cols in enumerate(chunks):
+            bank = psum.tile([P, CH], F32, name=f"scores_first{c}", tag=f"bank{6 * c}")
+            nc.tensor.matmul_mx(out=bank[:], lhsT=x_codes[:, 0:P].bitcast(E4M3), lhsT_scale=x_scales[:, 0:P],
+                                rhs=w_codes[:, cols].bitcast(E4M3), rhs_scale=w_scales[:, cols], start=True, stop=True)
+            nc.vector.tensor_tensor(out=q0[:, 0, cols], in0=bank[:], in1=y_sb[0][:, 0, cols], op=ALU.subtract)
+        for j in range(1, PACK):
             bank = scores(0, j, 1, f"bank{j}")
             nc.vector.tensor_tensor(out=q0[:, j, :], in0=bank[:, 0, :], in1=y_sb[j // 2][:, j % 2, halves[0]],
                                     op=ALU.subtract)
@@ -208,14 +213,17 @@ def tile_attend_gcau_w_kernel(tc, xT, wT, y, wt, xm, offs, out):
                 nc.vector.scalar_tensor_tensor(out=left[1][:, j, :], in0=bank[:, e, :], scalar=wt_sb[:, j:j + 1],
                                                in1=y_weighed[j][:], op0=ALU.mult, op1=ALU.subtract)
 
-        for u in range(PAIRS):
-            for j in (2 * u, 2 * u + 1):
-                square(sq[0][:, j, :], q0[:, j, :])
-            for j in (2 * u, 2 * u + 1):
-                inverse_root(right[0][:, j, :], sq[0][:, j, :])
+        for cols in chunks:
+            square(sq[0][:, 0, cols], q0[:, 0, cols])
+        square(sq[0][:, 1, :], q0[:, 1, :])
+        for j in range(2):
+            inverse_root(right[0][:, j, :], sq[0][:, j, :])
+        for j in range(2, PACK):
+            square(sq[0][:, j, :], q0[:, j, :])
+        for j in range(2, PACK):
+            inverse_root(right[0][:, j, :], sq[0][:, j, :])
         for j in range(PACK):
             square(sq[1][:, j, :], left[1][:, j, :], wt_inv[:, j:j + 1])
-        chunks = [slice(c * CH, (c + 1) * CH) for c in range(NH // CH)]
         roots = []
         for c, cols in enumerate(chunks):
             roots.append(keep.tile([P, PACK, CH], F32, name=f"root{c}", tag=f"root{c}"))
@@ -227,23 +235,29 @@ def tile_attend_gcau_w_kernel(tc, xT, wT, y, wt, xm, offs, out):
             nc.vector.scalar_tensor_tensor(out=left[0][:, j, :], in0=q0[:, j, :], scalar=wt_sb[:, j:j + 1],
                                            in1=right[0][:, j, :], op0=ALU.mult, op1=ALU.mult)
         quantize_xm(xm0, 0, 1)
-        gradient(0)
-        gradient(1)
-        quantize_g(0)
-        quantize_g(1)
-        quantize_xm(weave_xm(1, 1, "g_grouped0"), 1, 1)
+        gradient(0, NH)
+        xm1 = weave_xm(1, 1, "q0")
+        quantize_g(0, NH)
+        quantize_xm(xm1, 1, 1)
         dw_early = keep.tile([P, 2, NH], F32, name="dw_early", tag="sq1")
         for m in range(2):
             nc.scalar.copy(out=dw_early[:, m, :], in_=product(m, 0, f"bank{6 + m}")[:])
         for m in range(2):
             scatter_first_half(m, dw_early[:, m, :])
-        gradient(2)
-        gradient(3)
-        quantize_g(2)
-        quantize_g(3)
+        for first in (NH, NH + CH):
+            gradient(first, CH)
+        for first in (NH, NH + CH):
+            quantize_g(first, CH)
 
         xm23 = weave_xm(2, 2, "left1")
-        dw01 = copy_out(nc.vector.tensor_copy, 0, 1, "bank0", "dw01")
+        dw01 = keep.tile([P, NH], F32, name="dw01")
+        for c, cols in enumerate(chunks):
+            acc = psum.tile([P, CH], F32, name=f"acc_chunk{c}", tag=f"bank{2 * c}")
+            slots = slice(NH + c * CH, NH + (c + 1) * CH)
+            nc.tensor.matmul_mx(out=acc[:], lhsT=xm_codes[:, 0:P].bitcast(E4M3), lhsT_scale=xm_scales[:, 0:P],
+                                rhs=g_codes[:, slots].bitcast(E5M2), rhs_scale=g_scales[:, slots],
+                                start=True, stop=True)
+            nc.vector.tensor_copy(out=dw01[:, cols], in_=acc[:])
         quantize_xm(xm23, 2, 2)
         scatter_second_half_and_store(0, dw01)
 

@@ -23,7 +23,7 @@ HALVES = 2
 NH = N // HALVES
 CH = 128
 TILES = D // P
-X_CUTS = (42, 22)
+X_CUTS = (42, 36)
 
 
 def tile_attend_gcau_w_kernel(tc, xT, wT, y, wt, xm, offs, out):
@@ -38,7 +38,7 @@ def tile_attend_gcau_w_kernel(tc, xT, wT, y, wt, xm, offs, out):
         nc.sync.dma_start(out=planes[0][:], in_=w_view[:, 0, :])
         nc.sync.dma_start(offsets[:], offs)
         wt_sb = keep.tile([P, PACK], F32, name="wt_sb")
-        nc.sync.dma_start(out=wt_sb[:], in_=wt[0].rearrange("(p j) o -> p (j o)", j=PACK))
+        nc.scalar.dma_start(out=wt_sb[:], in_=wt[0].rearrange("(p j) o -> p (j o)", j=PACK))
         for t in range(1, PACK):
             nc.sync.dma_start(out=planes[t][:], in_=w_view[:, t, :])
         x_raw = keep.tile([P, PACK, R], F32, name="x_raw")

@@ -119,21 +119,10 @@ def tile_attend_gcau_w_kernel(tc, xT, wT, y, wt, xm, offs, out):
         nc.gpsimd.tensor_scalar(out=xm0[:], in0=xm_first[:].rearrange("p j d -> p d j"),
                                 scalar1=1.0, scalar2=0.0, op0=ALU.mult, op1=ALU.add)
 
-        q0 = keep.tile([P, PACK, NH], F32, name="q0", tag="q0", align_bytes=64)
-        left = [keep.tile([P, PACK, NH], F32, name=f"left{h}", tag=f"left{h}", align_bytes=64) for h in range(HALVES)]
-        sq = [keep.tile([P, PACK, NH], F32, name=f"sq{h}", tag=f"sq{h}") for h in range(HALVES)]
-        right = [keep.tile([P, PACK, NH], F32, name=f"right{h}") for h in range(HALVES)]
-
-        def scores(h, first, count, bank_tag):
-            cols = halves[h]
-            bank = psum.tile([P, count, NH], F32, name=f"scores_{bank_tag}", tag=bank_tag)
-            for e in range(count):
-                j = first + e
-                nc.tensor.matmul_mx(
-                    out=bank[:, e, :],
-                    lhsT=x_codes[:, j * P:(j + 1) * P].bitcast(E4M3), lhsT_scale=x_scales[:, j * P:(j + 1) * P],
-                    rhs=w_codes[:, cols].bitcast(E4M3), rhs_scale=w_scales[:, cols], start=True, stop=True)
-            return bank
+        def scores(bank, j, cols):
+            rows = slice(j * P, (j + 1) * P)
+            nc.tensor.matmul_mx(out=bank, lhsT=x_codes[:, rows].bitcast(E4M3), lhsT_scale=x_scales[:, rows],
+                                rhs=w_codes[:, cols].bitcast(E4M3), rhs_scale=w_scales[:, cols], start=True, stop=True)
 
         def square(dst, src, scale=1.0):
             nc.scalar.activation(out=dst, in_=src, func=ACT.Square, scale=scale)
@@ -144,27 +133,26 @@ def tile_attend_gcau_w_kernel(tc, xT, wT, y, wt, xm, offs, out):
         g_grouped = keep.tile([P, N, PACK], BF16, name="g_grouped", align_bytes=64)
         g_codes = keep.tile([P, N], U32, name="g_codes", align_bytes=64)
         g_scales = keep.tile([P, N], U8, name="g_scales", align_bytes=64)
+        xm_scales = keep.tile([P, D], U8, name="xm_scales", align_bytes=64)
+        xm_codes = keep.tile([P, D], U32, name="xm_codes", align_bytes=64)
 
-        def gradient(first, count):
-            h, c = divmod(first, NH)
-            cols = slice(c, c + count)
+        def gradient(first, count, left, right):
+            cols = slice(first % NH, first % NH + count)
             nc.vector.tensor_tensor(
                 out=g_grouped[:, first:first + count, :].rearrange("p (c i) j -> p c j i", i=2),
-                in0=left[h][:, :, cols].rearrange("p j (c i) -> p c j i", i=2),
-                in1=right[h][:, :, cols].rearrange("p j (c i) -> p c j i", i=2), op=ALU.mult)
+                in0=left[:, :, cols].rearrange("p j (c i) -> p c j i", i=2),
+                in1=right[:, :, cols].rearrange("p j (c i) -> p c j i", i=2), op=ALU.mult)
 
         def quantize_g(first, count):
             cols = slice(first, first + count)
             nc.vector.quantize_mx(out=g_codes[:, cols].bitcast(E5M2), scales=g_scales[:, cols],
                                   in_=g_grouped[:, cols, :].rearrange("p n j -> p (n j)"))
 
-        xm_scales = keep.tile([P, D], U8, name="xm_scales", align_bytes=64)
-        xm_codes = keep.tile([P, D], U32, name="xm_codes", align_bytes=64)
-
         def weave_xm(m, count, tag):
             grouped = keep.tile([P, count * P, PACK], BF16, name=f"xm_grouped{m}", tag=tag, align_bytes=64)
+            source = xm_rest[:, :, (m - 1) * P:(m - 1 + count) * P]
             nc.vector.tensor_copy(out=grouped[:].rearrange("p (c i) j -> p c j i", i=4),
-                                  in_=xm_rest[:, :, (m - 1) * P:(m - 1 + count) * P].rearrange("p j (c i) -> p c j i", i=4))
+                                  in_=source.rearrange("p j (c i) -> p c j i", i=4))
             return grouped
 
         def quantize_xm(grouped, first, count):
@@ -172,108 +160,111 @@ def tile_attend_gcau_w_kernel(tc, xT, wT, y, wt, xm, offs, out):
             nc.vector.quantize_mx(out=xm_codes[:, cols].bitcast(E4M3), scales=xm_scales[:, cols],
                                   in_=grouped[:].rearrange("p d j -> p (d j)"))
 
-        def product(m, h, bank_tag):
-            acc = psum.tile([P, NH], F32, name=f"acc{m}{h}", tag=bank_tag)
-            product_in(acc[:], m, h)
-            return acc
-
-        def product_in(acc, m, h):
-            cols = slice(m * P, (m + 1) * P)
-            nc.tensor.matmul_mx(out=acc, lhsT=xm_codes[:, cols].bitcast(E4M3), lhsT_scale=xm_scales[:, cols],
-                                rhs=g_codes[:, halves[h]].bitcast(E5M2), rhs_scale=g_scales[:, halves[h]],
+        def product(acc, m, cols):
+            rows = slice(m * P, (m + 1) * P)
+            nc.tensor.matmul_mx(out=acc, lhsT=xm_codes[:, rows].bitcast(E4M3), lhsT_scale=xm_scales[:, rows],
+                                rhs=g_codes[:, cols].bitcast(E5M2), rhs_scale=g_scales[:, cols],
                                 start=True, stop=True)
 
-        def copy_out(copy, m, h, bank_tag, tag):
-            acc = product(m, h, bank_tag)
-            dw = keep.tile([P, NH], F32, name=f"dw{m}{h}", tag=tag)
-            copy(out=dw[:], in_=acc[:])
-            return dw
+        def lone_product(m, cols, bank_tag):
+            acc = psum.tile([P, cols.stop - cols.start], F32, name=f"acc{m}_{cols.start}", tag=bank_tag)
+            product(acc[:], m, cols)
+            return acc
 
-        def scatter_first_half(m, dw):
-            nc.scalar.activation(out=windows[m][:].indirect(half_offsets(0)), in_=dw[:], func=ACT.Copy)
+        def scatter_on_scalar(m, h, dw):
+            nc.scalar.activation(out=windows[m][:].indirect(half_offsets(h)), in_=dw, func=ACT.Copy)
 
-        def scatter_second_half_and_store(m, dw):
-            nc.vector.tensor_copy(out=windows[m][:].indirect(half_offsets(1)), in_=dw[:])
+        def store(m):
             nc.sync.dma_start(out=out[m * P:(m + 1) * P, :], in_=windows[m][:])
 
         chunks = [slice(c * CH, (c + 1) * CH) for c in range(NH // CH)]
+        q = [keep.tile([P, NH], F32, name=f"q{j}", tag=f"q{j}", align_bytes=64) for j in range(PACK)]
         for c, cols in enumerate(chunks):
             bank = psum.tile([P, CH], F32, name=f"scores_first{c}", tag=f"bank{6 * c}")
-            nc.tensor.matmul_mx(out=bank[:], lhsT=x_codes[:, 0:P].bitcast(E4M3), lhsT_scale=x_scales[:, 0:P],
-                                rhs=w_codes[:, cols].bitcast(E4M3), rhs_scale=w_scales[:, cols], start=True, stop=True)
-            nc.vector.tensor_tensor(out=q0[:, 0, cols], in0=bank[:], in1=y_sb[0][:, 0, cols], op=ALU.subtract)
+            scores(bank[:], 0, cols)
+            nc.vector.tensor_tensor(out=q[0][:, cols], in0=bank[:], in1=y_sb[0][:, 0, cols], op=ALU.subtract)
         for j in range(1, PACK):
-            bank = scores(0, j, 1, f"bank{j}")
-            nc.vector.tensor_tensor(out=q0[:, j, :], in0=bank[:, 0, :], in1=y_sb[j // 2][:, j % 2, halves[0]],
-                                    op=ALU.subtract)
+            bank = psum.tile([P, NH], F32, name=f"scores_first_tile{j}", tag=f"bank{j}")
+            scores(bank[:], j, halves[0])
+            nc.vector.tensor_tensor(out=q[j][:], in0=bank[:], in1=y_sb[j // 2][:, j % 2, halves[0]], op=ALU.subtract)
+        second_scores = []
         for u in range(PAIRS):
-            bank = scores(1, 2 * u, 2, f"bank{PACK + u}")
+            second_scores.append(psum.tile([P, 2, NH], F32, name=f"scores_second{u}", tag=f"bank{PACK + u}"))
             for e in range(2):
-                j = 2 * u + e
-                nc.vector.scalar_tensor_tensor(out=left[1][:, j, :], in0=bank[:, e, :], scalar=wt_sb[:, j:j + 1],
-                                               in1=y_weighed[j][:], op0=ALU.mult, op1=ALU.subtract)
+                scores(second_scores[u][:, e, :], 2 * u + e, halves[1])
 
+        sq0 = keep.tile([P, PACK, NH], F32, name="sq0")
+        root0 = keep.tile([P, PACK, NH], F32, name="root0")
+        left0 = keep.tile([P, PACK, NH], F32, name="left0")
         for cols in chunks:
-            square(sq[0][:, 0, cols], q0[:, 0, cols])
-        square(sq[0][:, 1, :], q0[:, 1, :])
+            square(sq0[:, 0, cols], q[0][:, cols])
+        square(sq0[:, 1, :], q[1][:])
         for j in range(2):
-            inverse_root(right[0][:, j, :], sq[0][:, j, :])
+            inverse_root(root0[:, j, :], sq0[:, j, :])
         for j in range(2, PACK):
-            square(sq[0][:, j, :], q0[:, j, :])
+            square(sq0[:, j, :], q[j][:])
         for j in range(2, PACK):
-            inverse_root(right[0][:, j, :], sq[0][:, j, :])
+            inverse_root(root0[:, j, :], sq0[:, j, :])
+
+        def weigh(j):
+            nc.vector.scalar_tensor_tensor(out=left0[:, j, :], in0=q[j][:], scalar=wt_sb[:, j:j + 1],
+                                           in1=root0[:, j, :], op0=ALU.mult, op1=ALU.mult)
+
+        left1 = keep.tile([P, PACK, NH], F32, name="left1", tag="left1", align_bytes=64)
         for j in range(PACK):
-            square(sq[1][:, j, :], left[1][:, j, :], wt_inv[:, j:j + 1])
+            nc.vector.scalar_tensor_tensor(out=left1[:, j, :], in0=second_scores[j // 2][:, j % 2, :],
+                                           scalar=wt_sb[:, j:j + 1], in1=y_weighed[j][:],
+                                           op0=ALU.mult, op1=ALU.subtract)
+
+        sq1 = keep.tile([P, PACK, NH], F32, name="sq1", tag="sq1")
+        damping1 = keep.tile([P, PACK, NH], F32, name="damping1")
+        for j in range(PACK):
+            square(sq1[:, j, :], left1[:, j, :], wt_inv[:, j:j + 1])
         roots = []
         for c, cols in enumerate(chunks):
-            roots.append(keep.tile([P, PACK, CH], F32, name=f"root{c}", tag=f"root{c}"))
-            inverse_root(roots[c][:], sq[1][:, :, cols])
+            roots.append(keep.tile([P, PACK, CH], F32, name=f"root1_{c}"))
+            inverse_root(roots[c][:], sq1[:, :, cols])
         for c, cols in enumerate(chunks):
-            square(right[1][:, :, cols], roots[c][:])
+            square(damping1[:, :, cols], roots[c][:])
 
         for j in range(PACK):
-            nc.vector.scalar_tensor_tensor(out=left[0][:, j, :], in0=q0[:, j, :], scalar=wt_sb[:, j:j + 1],
-                                           in1=right[0][:, j, :], op0=ALU.mult, op1=ALU.mult)
+            weigh(j)
         quantize_xm(xm0, 0, 1)
-        gradient(0, NH)
-        xm1 = weave_xm(1, 1, "q0")
+        gradient(0, NH, left0, root0)
+        xm1 = weave_xm(1, 1, "q3")
         quantize_g(0, NH)
         quantize_xm(xm1, 1, 1)
-        dw_early = keep.tile([P, 2, NH], F32, name="dw_early", tag="sq1")
-        for m in range(2):
-            nc.scalar.copy(out=dw_early[:, m, :], in_=product(m, 0, f"bank{6 + m}")[:])
-        for m in range(2):
-            scatter_first_half(m, dw_early[:, m, :])
+
+        dw0 = keep.tile([P, NH], F32, name="dw0_first", tag="sq1")
+        dw1 = keep.tile([P, N], F32, name="dw1")
+        nc.scalar.copy(out=dw0[:], in_=lone_product(0, halves[0], "bank7")[:])
+        nc.scalar.copy(out=dw1[:, halves[0]], in_=lone_product(1, halves[0], "bank6")[:])
+        scatter_on_scalar(0, 0, dw0[:])
+
         for first in (NH, NH + CH):
-            gradient(first, CH)
+            gradient(first, CH, left1, damping1)
         for first in (NH, NH + CH):
             quantize_g(first, CH)
-
         xm23 = weave_xm(2, 2, "left1")
-        dw01 = keep.tile([P, NH], F32, name="dw01")
-        for c, cols in enumerate(chunks):
-            acc = psum.tile([P, CH], F32, name=f"acc_chunk{c}", tag=f"bank{2 * c}")
-            slots = slice(NH + c * CH, NH + (c + 1) * CH)
-            nc.tensor.matmul_mx(out=acc[:], lhsT=xm_codes[:, 0:P].bitcast(E4M3), lhsT_scale=xm_scales[:, 0:P],
-                                rhs=g_codes[:, slots].bitcast(E5M2), rhs_scale=g_scales[:, slots],
-                                start=True, stop=True)
-            nc.vector.tensor_copy(out=dw01[:, cols], in_=acc[:])
+        dw0_second = keep.tile([P, NH], F32, name="dw0_second")
+        dw2 = [keep.tile([P, NH], F32, name=f"dw2_{h}") for h in range(HALVES)]
+        late = psum.tile([P, NH], F32, name="late", tag="bank0")
+        for cols in chunks:
+            product(late[:, cols], 0, slice(NH + cols.start, NH + cols.stop))
+        nc.vector.tensor_copy(out=dw0_second[:], in_=late[:])
+        scatter_on_scalar(0, 1, dw0_second[:])
+        store(0)
+        nc.vector.tensor_copy(out=dw1[:, halves[1]], in_=lone_product(1, halves[1], "bank1")[:])
         quantize_xm(xm23, 2, 2)
-        scatter_second_half_and_store(0, dw01)
+        nc.vector.tensor_copy(out=windows[1][:].indirect(offsets[:]), in_=dw1[:])
+        store(1)
 
-        joint = psum.tile([P, 2, NH], F32, name="joint_late", tag="bank1")
-        product_in(joint[:, 0, :], 1, 1)
-        product_in(joint[:, 1, :], 2, 0)
-        dw11 = keep.tile([P, NH], F32, name="dw11", tag="dw11")
-        nc.scalar.copy(out=dw11[:], in_=joint[:, 0, :])
-        scatter_second_half_and_store(1, dw11)
-
-        dw_first = keep.tile([P, 2, NH], F32, name="dw_first", tag="sq1")
-        dw_second = keep.tile([P, 2, NH], F32, name="dw_second", tag="dw11")
-        nc.scalar.copy(out=dw_first[:, 0, :], in_=joint[:, 1, :])
-        nc.scalar.copy(out=dw_first[:, 1, :], in_=product(3, 0, "bank3")[:])
-        for e in range(2):
-            nc.vector.tensor_copy(out=dw_second[:, e, :], in_=product(2 + e, 1, f"bank{PACK + e}")[:])
-        for e in range(2):
-            scatter_first_half(2 + e, dw_first[:, e, :])
-            scatter_second_half_and_store(2 + e, dw_second[:, e, :])
+        for h in range(HALVES):
+            nc.scalar.copy(out=dw2[h][:], in_=lone_product(2, halves[h], f"bank{2 + h}")[:])
+        scatter_on_scalar(2, 0, dw2[0][:])
+        dw3 = keep.tile([P, N], F32, name="dw3")
+        nc.scalar.copy(out=dw3[:], in_=lone_product(3, slice(0, N), "bank0")[:])
+        scatter_on_scalar(2, 1, dw2[1][:])
+        store(2)
+        nc.vector.tensor_copy(out=windows[3][:].indirect(offsets[:]), in_=dw3[:])
+        store(3)

@@ -38,11 +38,11 @@ def tile_attend_gcau_w_kernel(tc, xT, wT, y, wt, xm, offs, out):
         nc.sync.dma_start(out=planes[0][:], in_=w_view[:, 0, :])
         nc.sync.dma_start(offsets[:], offs)
         wt_sb = keep.tile([P, PACK], F32, name="wt_sb")
-        nc.scalar.dma_start(out=wt_sb[:], in_=wt[0].rearrange("(p j) o -> p (j o)", j=PACK))
         for t in range(1, PACK):
             nc.sync.dma_start(out=planes[t][:], in_=w_view[:, t, :])
         x_raw = keep.tile([P, PACK, R], F32, name="x_raw")
         nc.sync.dma_start(out=x_raw[:], in_=xT[0].rearrange("(p t) r -> p t r", t=PACK))
+        nc.sync.dma_start(out=wt_sb[:], in_=wt[0].rearrange("(p j) o -> p (j o)", j=PACK))
         y_view = y[0].rearrange("(p j) n -> p j n", j=PACK)
         y_sb = [keep.tile([P, 2, N], F32, name=f"y_sb{u}") for u in range(PAIRS)]
         for u in range(PAIRS):
@@ -61,12 +61,6 @@ def tile_attend_gcau_w_kernel(tc, xT, wT, y, wt, xm, offs, out):
         warm_out = keep.tile([P, 1], F32, name="warm_out")
         nc.gpsimd.memset(warm_in[:], 0.0)
         nc.scalar.activation(out=warm_out[:], in_=warm_in[:], func=ACT.Abs_reciprocal_sqrt, bias=1.0)
-
-        wt_safe = keep.tile([P, PACK], F32, name="wt_safe")
-        wt_inv = keep.tile([P, PACK], F32, name="wt_inv")
-        nc.vector.scalar_tensor_tensor(out=wt_safe[:], in0=wt_sb[:], scalar=0.0, in1=wt_sb[:],
-                                       op0=ALU.is_equal, op1=ALU.add)
-        nc.vector.reciprocal(out=wt_inv[:], in_=wt_safe[:])
 
         halves = [slice(h * NH, (h + 1) * NH) for h in range(HALVES)]
         pairs = [slice(2 * u, 2 * u + 2) for u in range(PAIRS)]
@@ -107,6 +101,12 @@ def tile_attend_gcau_w_kernel(tc, xT, wT, y, wt, xm, offs, out):
             cols = slice((2 * u + first) * P, (2 * u + first + count) * P)
             nc.vector.quantize_mx(out=x_codes[:, cols].bitcast(E4M3), scales=x_scales[:, cols],
                                   in_=x_grouped[u][:, first:first + count].rearrange("p e s t -> p (e s t)"))
+
+        wt_safe = keep.tile([P, PACK], F32, name="wt_safe")
+        wt_inv = keep.tile([P, PACK], F32, name="wt_inv")
+        nc.vector.scalar_tensor_tensor(out=wt_safe[:], in0=wt_sb[:], scalar=0.0, in1=wt_sb[:],
+                                       op0=ALU.is_equal, op1=ALU.add)
+        nc.vector.reciprocal(out=wt_inv[:], in_=wt_safe[:])
 
         y_weighed = [keep.tile([P, NH], F32, name=f"y_weighed{j}") for j in range(PACK)]
         for j in range(2):
@@ -195,7 +195,7 @@ def tile_attend_gcau_w_kernel(tc, xT, wT, y, wt, xm, offs, out):
 
         sq0 = keep.tile([P, PACK, NH], F32, name="sq0")
         root0 = keep.tile([P, PACK, NH], F32, name="root0")
-        left0 = keep.tile([P, PACK, NH], F32, name="left0")
+        left0 = keep.tile([P, PACK, NH], F32, name="left0", tag="left0", align_bytes=64)
         for cols in chunks:
             square(sq0[:, 0, cols], q[0][:, cols])
         square(sq0[:, 1, :], q[1][:])
@@ -217,7 +217,7 @@ def tile_attend_gcau_w_kernel(tc, xT, wT, y, wt, xm, offs, out):
                                            op0=ALU.mult, op1=ALU.subtract)
 
         sq1 = keep.tile([P, PACK, NH], F32, name="sq1", tag="sq1")
-        damping1 = keep.tile([P, PACK, NH], F32, name="damping1")
+        damping1 = keep.tile([P, PACK, NH], F32, name="damping1", tag="damping1")
         for j in range(PACK):
             square(sq1[:, j, :], left1[:, j, :], wt_inv[:, j:j + 1])
         roots = []
@@ -235,36 +235,38 @@ def tile_attend_gcau_w_kernel(tc, xT, wT, y, wt, xm, offs, out):
         quantize_g(0, NH)
         quantize_xm(xm1, 1, 1)
 
+        xm2 = weave_xm(2, 1, "left0")
         dw0 = keep.tile([P, NH], F32, name="dw0_first", tag="sq1")
-        dw1 = keep.tile([P, N], F32, name="dw1")
         nc.scalar.copy(out=dw0[:], in_=lone_product(0, halves[0], "bank7")[:])
-        nc.scalar.copy(out=dw1[:, halves[0]], in_=lone_product(1, halves[0], "bank6")[:])
+        early1 = lone_product(1, halves[0], "bank6")
         scatter_on_scalar(0, 0, dw0[:])
 
         for first in (NH, NH + CH):
             gradient(first, CH, left1, damping1)
         for first in (NH, NH + CH):
             quantize_g(first, CH)
-        xm23 = weave_xm(2, 2, "left1")
+        dw1 = keep.tile([P, N], F32, name="dw1", tag="damping1")
+        nc.vector.tensor_copy(out=dw1[:, halves[0]], in_=early1[:])
+        xm3 = weave_xm(3, 1, "left1")
         dw0_second = keep.tile([P, NH], F32, name="dw0_second")
         dw2 = [keep.tile([P, NH], F32, name=f"dw2_{h}") for h in range(HALVES)]
-        late = psum.tile([P, NH], F32, name="late", tag="bank0")
-        for cols in chunks:
-            product(late[:, cols], 0, slice(NH + cols.start, NH + cols.stop))
-        nc.vector.tensor_copy(out=dw0_second[:], in_=late[:])
+        late = [lone_product(0, slice(NH + cols.start, NH + cols.stop), f"bank{c}") for c, cols in enumerate(chunks)]
+        nc.vector.tensor_copy(out=dw0_second[:, chunks[0]], in_=late[0][:])
+        quantize_xm(xm2, 2, 1)
+        nc.vector.tensor_copy(out=dw0_second[:, chunks[1]], in_=late[1][:])
         scatter_on_scalar(0, 1, dw0_second[:])
         store(0)
-        nc.vector.tensor_copy(out=dw1[:, halves[1]], in_=lone_product(1, halves[1], "bank1")[:])
-        quantize_xm(xm23, 2, 2)
+        nc.vector.tensor_copy(out=dw1[:, halves[1]], in_=lone_product(1, halves[1], "bank4")[:])
+        quantize_xm(xm3, 3, 1)
         nc.vector.tensor_copy(out=windows[1][:].indirect(offsets[:]), in_=dw1[:])
         store(1)
 
         for h in range(HALVES):
-            nc.scalar.copy(out=dw2[h][:], in_=lone_product(2, halves[h], f"bank{2 + h}")[:])
-        scatter_on_scalar(2, 0, dw2[0][:])
-        dw3 = keep.tile([P, N], F32, name="dw3")
-        nc.scalar.copy(out=dw3[:], in_=lone_product(3, slice(0, N), "bank0")[:])
-        scatter_on_scalar(2, 1, dw2[1][:])
+            nc.scalar.copy(out=dw2[h][:], in_=lone_product(2, halves[h], f"bank{1 + 3 * h}")[:])
+        for h in range(HALVES):
+            scatter_on_scalar(2, h, dw2[h][:])
         store(2)
+        dw3 = keep.tile([P, N], F32, name="dw3")
+        nc.vector.tensor_copy(out=dw3[:], in_=lone_product(3, slice(0, N), "bank0")[:])
         nc.vector.tensor_copy(out=windows[3][:].indirect(offsets[:]), in_=dw3[:])
         store(3)

@@ -108,10 +108,8 @@ def tile_attend_gcau_w_kernel(tc, xT, wT, y, wt, xm, offs, out):
                                        op0=ALU.is_equal, op1=ALU.add)
         nc.vector.reciprocal(out=wt_inv[:], in_=wt_safe[:])
 
-        y_weighed = [keep.tile([P, NH], F32, name=f"y_weighed{j}") for j in range(PACK)]
-        for j in range(2):
-            nc.scalar.activation(out=y_weighed[j][:], in_=y_sb[0][:, j, halves[1]], func=ACT.Copy,
-                                 scale=wt_sb[:, j:j + 1])
+        y_weighed = {j: keep.tile([P, NH], F32, name=f"y_weighed{j}") for j in range(1, PACK)}
+        nc.scalar.activation(out=y_weighed[1][:], in_=y_sb[0][:, 1, halves[1]], func=ACT.Copy, scale=wt_sb[:, 1:2])
         for j in range(2, PACK):
             nc.gpsimd.tensor_scalar(out=y_weighed[j][:], in0=y_sb[1][:, j - 2, halves[1]],
                                     scalar1=wt_sb[:, j:j + 1], scalar2=0.0, op0=ALU.mult, op1=ALU.add)
@@ -134,7 +132,7 @@ def tile_attend_gcau_w_kernel(tc, xT, wT, y, wt, xm, offs, out):
         g_codes = keep.tile([P, N], U32, name="g_codes", align_bytes=64)
         g_scales = keep.tile([P, N], U8, name="g_scales", align_bytes=64)
         xm_scales = keep.tile([P, D], U8, name="xm_scales", align_bytes=64)
-        xm_codes = keep.tile([P, D], U32, name="xm_codes", align_bytes=64)
+        xm_codes = {m: keep.tile([P, P], U32, name=f"xm_codes{m}", align_bytes=64) for m in (0, 1, 3)}
 
         def gradient(first, count, left, right):
             cols = slice(first % NH, first % NH + count)
@@ -155,14 +153,13 @@ def tile_attend_gcau_w_kernel(tc, xT, wT, y, wt, xm, offs, out):
                                   in_=source.rearrange("p j (c i) -> p c j i", i=4))
             return grouped
 
-        def quantize_xm(grouped, first, count):
-            cols = slice(first * P, (first + count) * P)
-            nc.vector.quantize_mx(out=xm_codes[:, cols].bitcast(E4M3), scales=xm_scales[:, cols],
+        def quantize_xm(grouped, m):
+            nc.vector.quantize_mx(out=xm_codes[m][:].bitcast(E4M3), scales=xm_scales[:, m * P:(m + 1) * P],
                                   in_=grouped[:].rearrange("p d j -> p (d j)"))
 
         def product(acc, m, cols):
             rows = slice(m * P, (m + 1) * P)
-            nc.tensor.matmul_mx(out=acc, lhsT=xm_codes[:, rows].bitcast(E4M3), lhsT_scale=xm_scales[:, rows],
+            nc.tensor.matmul_mx(out=acc, lhsT=xm_codes[m][:].bitcast(E4M3), lhsT_scale=xm_scales[:, rows],
                                 rhs=g_codes[:, cols].bitcast(E5M2), rhs_scale=g_scales[:, cols],
                                 start=True, stop=True)
 
@@ -188,52 +185,59 @@ def tile_attend_gcau_w_kernel(tc, xT, wT, y, wt, xm, offs, out):
             scores(bank[:], j, halves[0])
             nc.vector.tensor_tensor(out=q[j][:], in0=bank[:], in1=y_sb[j // 2][:, j % 2, halves[0]], op=ALU.subtract)
         second_scores = []
-        for u in range(PAIRS):
-            second_scores.append(psum.tile([P, 2, NH], F32, name=f"scores_second{u}", tag=f"bank{PACK + u}"))
-            for e in range(2):
-                scores(second_scores[u][:, e, :], 2 * u + e, halves[1])
+        for j, number in enumerate((4, 7, 5, 0)):
+            second_scores.append(psum.tile([P, NH], F32, name=f"scores_second{j}", tag=f"bank{number}"))
+            scores(second_scores[j][:], j, halves[1])
 
-        sq0 = keep.tile([P, PACK, NH], F32, name="sq0")
+        sq0 = [keep.tile([P, NH], F32, name=f"sq0_{j}", tag="sq1" if j == 2 else f"sq0_{j}") for j in range(PACK)]
         root0 = keep.tile([P, PACK, NH], F32, name="root0")
         left0 = keep.tile([P, PACK, NH], F32, name="left0", tag="left0", align_bytes=64)
         for cols in chunks:
-            square(sq0[:, 0, cols], q[0][:, cols])
-        square(sq0[:, 1, :], q[1][:])
+            square(sq0[0][:, cols], q[0][:, cols])
+        square(sq0[1][:], q[1][:])
         for j in range(2):
-            inverse_root(root0[:, j, :], sq0[:, j, :])
+            inverse_root(root0[:, j, :], sq0[j][:])
         for j in range(2, PACK):
-            square(sq0[:, j, :], q[j][:])
+            square(sq0[j][:], q[j][:])
         for j in range(2, PACK):
-            inverse_root(root0[:, j, :], sq0[:, j, :])
+            inverse_root(root0[:, j, :], sq0[j][:])
 
         def weigh(j):
             nc.vector.scalar_tensor_tensor(out=left0[:, j, :], in0=q[j][:], scalar=wt_sb[:, j:j + 1],
                                            in1=root0[:, j, :], op0=ALU.mult, op1=ALU.mult)
 
         left1 = keep.tile([P, PACK, NH], F32, name="left1", tag="left1", align_bytes=64)
-        for j in range(PACK):
-            nc.vector.scalar_tensor_tensor(out=left1[:, j, :], in0=second_scores[j // 2][:, j % 2, :],
+        q_second = keep.tile([P, NH], F32, name="q_second")
+        nc.vector.tensor_tensor(out=q_second[:], in0=second_scores[0][:], in1=y_sb[0][:, 0, halves[1]],
+                                op=ALU.subtract)
+        for j in range(1, PACK):
+            nc.vector.scalar_tensor_tensor(out=left1[:, j, :], in0=second_scores[j][:],
                                            scalar=wt_sb[:, j:j + 1], in1=y_weighed[j][:],
                                            op0=ALU.mult, op1=ALU.subtract)
 
         sq1 = keep.tile([P, PACK, NH], F32, name="sq1", tag="sq1")
         damping1 = keep.tile([P, PACK, NH], F32, name="damping1", tag="damping1")
-        for j in range(PACK):
+        square(sq1[:, 0, :], q_second[:])
+        square(sq1[:, 1, :], left1[:, 1, :], wt_inv[:, 1:2])
+        for j in range(2, PACK):
             square(sq1[:, j, :], left1[:, j, :], wt_inv[:, j:j + 1])
+        inverse_root(damping1[:, 0, :], sq1[:, 0, :])
         roots = []
         for c, cols in enumerate(chunks):
-            roots.append(keep.tile([P, PACK, CH], F32, name=f"root1_{c}"))
-            inverse_root(roots[c][:], sq1[:, :, cols])
+            roots.append(keep.tile([P, PACK - 1, CH], F32, name=f"root1_{c}"))
+            inverse_root(roots[c][:], sq1[:, 1:, cols])
         for c, cols in enumerate(chunks):
-            square(damping1[:, :, cols], roots[c][:])
+            square(damping1[:, 1:, cols], roots[c][:])
 
         for j in range(PACK):
             weigh(j)
-        quantize_xm(xm0, 0, 1)
+        quantize_xm(xm0, 0)
         gradient(0, NH, left0, root0)
         xm1 = weave_xm(1, 1, "q3")
         quantize_g(0, NH)
-        quantize_xm(xm1, 1, 1)
+        nc.vector.scalar_tensor_tensor(out=left1[:, 0, :], in0=q_second[:], scalar=wt_sb[:, 0:1],
+                                       in1=damping1[:, 0, :], op0=ALU.mult, op1=ALU.mult)
+        quantize_xm(xm1, 1)
 
         xm2 = weave_xm(2, 1, "left0")
         dw0 = keep.tile([P, NH], F32, name="dw0_first", tag="sq1")
@@ -245,24 +249,28 @@ def tile_attend_gcau_w_kernel(tc, xT, wT, y, wt, xm, offs, out):
             gradient(first, CH, left1, damping1)
         for first in (NH, NH + CH):
             quantize_g(first, CH)
+        xm_codes[2] = keep.tile([P, P], U32, name="xm_codes2", tag="left1", align_bytes=64)
+        quantize_xm(xm2, 2)
+        xm3 = keep.tile([P, P, PACK], BF16, name="xm_grouped3", tag="left0", align_bytes=64)
+        nc.gpsimd.tensor_scalar(out=xm3[:], in0=xm_rest[:, :, 2 * P:].rearrange("p j d -> p d j"),
+                                scalar1=1.0, scalar2=0.0, op0=ALU.mult, op1=ALU.add)
         dw1 = keep.tile([P, N], F32, name="dw1", tag="damping1")
         nc.vector.tensor_copy(out=dw1[:, halves[0]], in_=early1[:])
-        xm3 = weave_xm(3, 1, "left1")
         dw0_second = keep.tile([P, NH], F32, name="dw0_second")
         dw2 = [keep.tile([P, NH], F32, name=f"dw2_{h}") for h in range(HALVES)]
         late = [lone_product(0, slice(NH + cols.start, NH + cols.stop), f"bank{c}") for c, cols in enumerate(chunks)]
-        nc.vector.tensor_copy(out=dw0_second[:, chunks[0]], in_=late[0][:])
-        quantize_xm(xm2, 2, 1)
-        nc.vector.tensor_copy(out=dw0_second[:, chunks[1]], in_=late[1][:])
+        for c, cols in enumerate(chunks):
+            nc.vector.tensor_copy(out=dw0_second[:, cols], in_=late[c][:])
         scatter_on_scalar(0, 1, dw0_second[:])
         store(0)
         nc.vector.tensor_copy(out=dw1[:, halves[1]], in_=lone_product(1, halves[1], "bank4")[:])
-        quantize_xm(xm3, 3, 1)
+        quantize_xm(xm3, 3)
         nc.vector.tensor_copy(out=windows[1][:].indirect(offsets[:]), in_=dw1[:])
         store(1)
 
+        whole2 = lone_product(2, slice(0, N), "bank1")
         for h in range(HALVES):
-            nc.scalar.copy(out=dw2[h][:], in_=lone_product(2, halves[h], f"bank{1 + 3 * h}")[:])
+            nc.scalar.copy(out=dw2[h][:], in_=whole2[:, halves[h]])
         for h in range(HALVES):
             scatter_on_scalar(2, h, dw2[h][:])
         store(2)

@@ -23,7 +23,7 @@ HALVES = 2
 NH = N // HALVES
 CH = 128
 TILES = D // P
-X_CUTS = (42, 36)
+X_CUTS = (32, 28)
 
 
 def tile_attend_gcau_w_kernel(tc, xT, wT, y, wt, xm, offs, out):
@@ -50,7 +50,7 @@ def tile_attend_gcau_w_kernel(tc, xT, wT, y, wt, xm, offs, out):
         xm_view = xm[0].rearrange("(p j) d -> p j d", j=PACK)
         xm_first = keep.tile([P, PACK, P], F32, name="xm_first")
         nc.sync.dma_start(out=xm_first[:], in_=xm_view[:, :, 0:P])
-        xm_rest = keep.tile([P, PACK, D - P], F32, name="xm_rest")
+        xm_rest = keep.tile([P, PACK, D - P], F32, name="xm_rest", tag="xm_rest", align_bytes=64)
         nc.sync.dma_start(out=xm_rest[:], in_=xm_view[:, :, P:])
 
         windows = [keep.tile([P, T], F32, name=f"window{m}") for m in range(TILES)]
@@ -128,23 +128,24 @@ def tile_attend_gcau_w_kernel(tc, xT, wT, y, wt, xm, offs, out):
         def inverse_root(dst, src):
             nc.scalar.activation(out=dst, in_=src, func=ACT.Abs_reciprocal_sqrt, bias=1.0)
 
-        g_grouped = keep.tile([P, N, PACK], BF16, name="g_grouped", align_bytes=64)
         g_codes = keep.tile([P, N], U32, name="g_codes", align_bytes=64)
         g_scales = keep.tile([P, N], U8, name="g_scales", align_bytes=64)
         xm_scales = keep.tile([P, D], U8, name="xm_scales", align_bytes=64)
         xm_codes = {m: keep.tile([P, P], U32, name=f"xm_codes{m}", align_bytes=64) for m in (0, 1, 3)}
 
         def gradient(first, count, left, right):
-            cols = slice(first % NH, first % NH + count)
+            grouped = keep.tile([P, count, PACK], BF16, name=f"g_grouped{first}", tag=f"g_grouped{first}",
+                                align_bytes=64)
             nc.vector.tensor_tensor(
-                out=g_grouped[:, first:first + count, :].rearrange("p (c i) j -> p c j i", i=2),
-                in0=left[:, :, cols].rearrange("p j (c i) -> p c j i", i=2),
-                in1=right[:, :, cols].rearrange("p j (c i) -> p c j i", i=2), op=ALU.mult)
+                out=grouped[:].rearrange("p (c i) j -> p c j i", i=2),
+                in0=left.rearrange("p j (c i) -> p c j i", i=2),
+                in1=right.rearrange("p j (c i) -> p c j i", i=2), op=ALU.mult)
+            return grouped
 
-        def quantize_g(first, count):
+        def quantize_g(grouped, first, count):
             cols = slice(first, first + count)
             nc.vector.quantize_mx(out=g_codes[:, cols].bitcast(E5M2), scales=g_scales[:, cols],
-                                  in_=g_grouped[:, cols, :].rearrange("p n j -> p (n j)"))
+                                  in_=grouped[:].rearrange("p n j -> p (n j)"))
 
         def weave_xm(m, count, tag):
             grouped = keep.tile([P, count * P, PACK], BF16, name=f"xm_grouped{m}", tag=tag, align_bytes=64)
@@ -190,7 +191,7 @@ def tile_attend_gcau_w_kernel(tc, xT, wT, y, wt, xm, offs, out):
             scores(second_scores[j][:], j, halves[1])
 
         sq0 = [keep.tile([P, NH], F32, name=f"sq0_{j}", tag="sq1" if j == 2 else f"sq0_{j}") for j in range(PACK)]
-        root0 = keep.tile([P, PACK, NH], F32, name="root0")
+        root0 = keep.tile([P, PACK, NH], F32, name="root0", tag="root0", align_bytes=64)
         left0 = keep.tile([P, PACK, NH], F32, name="left0", tag="left0", align_bytes=64)
         for cols in chunks:
             square(sq0[0][:, cols], q[0][:, cols])
@@ -216,42 +217,41 @@ def tile_attend_gcau_w_kernel(tc, xT, wT, y, wt, xm, offs, out):
                                            op0=ALU.mult, op1=ALU.subtract)
 
         sq1 = keep.tile([P, PACK, NH], F32, name="sq1", tag="sq1")
-        damping1 = keep.tile([P, PACK, NH], F32, name="damping1", tag="damping1")
+        damping1 = keep.tile([P, NH // CH, PACK, CH], F32, name="damping1", tag="damping1")
         square(sq1[:, 0, :], q_second[:])
         square(sq1[:, 1, :], left1[:, 1, :], wt_inv[:, 1:2])
         for j in range(2, PACK):
             square(sq1[:, j, :], left1[:, j, :], wt_inv[:, j:j + 1])
-        inverse_root(damping1[:, 0, :], sq1[:, 0, :])
+        inverse_root(damping1[:, :, 0, :], sq1[:, 0, :].rearrange("p (c n) -> p c n", n=CH))
         roots = []
         for c, cols in enumerate(chunks):
             roots.append(keep.tile([P, PACK - 1, CH], F32, name=f"root1_{c}"))
             inverse_root(roots[c][:], sq1[:, 1:, cols])
         for c, cols in enumerate(chunks):
-            square(damping1[:, 1:, cols], roots[c][:])
+            square(damping1[:, c, 1:, :], roots[c][:])
 
         for j in range(PACK):
             weigh(j)
         quantize_xm(xm0, 0)
-        gradient(0, NH, left0, root0)
-        xm1 = weave_xm(1, 1, "q3")
-        quantize_g(0, NH)
-        nc.vector.scalar_tensor_tensor(out=left1[:, 0, :], in0=q_second[:], scalar=wt_sb[:, 0:1],
-                                       in1=damping1[:, 0, :], op0=ALU.mult, op1=ALU.mult)
-        quantize_xm(xm1, 1)
+        g_first = gradient(0, NH, left0[:], root0[:])
+        nc.vector.scalar_tensor_tensor(out=left1[:, 0, :].rearrange("p (c n) -> p c n", n=CH),
+                                       in0=q_second[:].rearrange("p (c n) -> p c n", n=CH), scalar=wt_sb[:, 0:1],
+                                       in1=damping1[:, :, 0, :], op0=ALU.mult, op1=ALU.mult)
+        quantize_g(g_first, 0, NH)
+        xm1 = weave_xm(1, 1, "root0")
 
-        xm2 = weave_xm(2, 1, "left0")
         dw0 = keep.tile([P, NH], F32, name="dw0_first", tag="sq1")
         nc.scalar.copy(out=dw0[:], in_=lone_product(0, halves[0], "bank7")[:])
-        early1 = lone_product(1, halves[0], "bank6")
         scatter_on_scalar(0, 0, dw0[:])
 
+        g_second = {NH: gradient(NH, CH, left1[:, :, chunks[0]], damping1[:, 0])}
+        quantize_xm(xm1, 1)
+        early1 = lone_product(1, halves[0], "bank6")
+        g_second[NH + CH] = gradient(NH + CH, CH, left1[:, :, chunks[1]], damping1[:, 1])
         for first in (NH, NH + CH):
-            gradient(first, CH, left1, damping1)
-        for first in (NH, NH + CH):
-            quantize_g(first, CH)
-        xm_codes[2] = keep.tile([P, P], U32, name="xm_codes2", tag="left1", align_bytes=64)
-        quantize_xm(xm2, 2)
-        xm3 = keep.tile([P, P, PACK], BF16, name="xm_grouped3", tag="left0", align_bytes=64)
+            quantize_g(g_second[first], first, CH)
+        xm2 = weave_xm(2, 1, f"g_grouped{NH}")
+        xm3 = keep.tile([P, P, PACK], BF16, name="xm_grouped3", tag=f"g_grouped{NH + CH}", align_bytes=64)
         nc.gpsimd.tensor_scalar(out=xm3[:], in0=xm_rest[:, :, 2 * P:].rearrange("p j d -> p d j"),
                                 scalar1=1.0, scalar2=0.0, op0=ALU.mult, op1=ALU.add)
         dw1 = keep.tile([P, N], F32, name="dw1", tag="damping1")
@@ -264,6 +264,8 @@ def tile_attend_gcau_w_kernel(tc, xT, wT, y, wt, xm, offs, out):
         scatter_on_scalar(0, 1, dw0_second[:])
         store(0)
         nc.vector.tensor_copy(out=dw1[:, halves[1]], in_=lone_product(1, halves[1], "bank4")[:])
+        xm_codes[2] = keep.tile([P, P], U32, name="xm_codes2", tag="xm_rest", align_bytes=64)
+        quantize_xm(xm2, 2)
         quantize_xm(xm3, 3)
         nc.vector.tensor_copy(out=windows[1][:].indirect(offsets[:]), in_=dw1[:])
         store(1)

from contextlib import ExitStack

import concourse.mybir as mybir

N, T, D, R = 512, 2048, 512, 512
FLOPS = 2 * R * D * N * 2

F32 = mybir.dt.float32
BF16 = mybir.dt.bfloat16
I32 = mybir.dt.int32
U32 = mybir.dt.uint32
U16 = mybir.dt.uint16
U8 = mybir.dt.uint8
E4M3 = mybir.dt.float8_e4m3fn_x4
E5M2 = mybir.dt.float8_e5m2_x4
ACT = mybir.ActivationFunctionType
ALU = mybir.AluOpType

P = 128
PACK = 4
PAIRS = PACK // 2
HALVES = 2
NH = N // HALVES
CH = 128
TILES = D // P
X_CUTS = (32, 28)


def tile_attend_gcau_w_kernel(tc, xT, wT, y, wt, xm, offs, out):
    nc = tc.nc
    with ExitStack() as ctx:
        keep = ctx.enter_context(tc.tile_pool(name="keep", bufs=1))
        psum = ctx.enter_context(tc.psum_pool(name="psum", bufs=1))

        offsets = keep.tile([P, N // 16], U16, name="offsets")
        w_view = wT.rearrange("(p t) c -> p t c", t=PACK)
        planes = [keep.tile([P, T], F32, name=f"plane{t}") for t in range(PACK)]
        nc.sync.dma_start(out=planes[0][:], in_=w_view[:, 0, :])
        nc.sync.dma_start(offsets[:], offs)
        wt_sb = keep.tile([P, PACK], F32, name="wt_sb")
        for t in range(1, PACK):
            nc.sync.dma_start(out=planes[t][:], in_=w_view[:, t, :])
        x_raw = keep.tile([P, PACK, R], F32, name="x_raw")
        nc.sync.dma_start(out=x_raw[:], in_=xT[0].rearrange("(p t) r -> p t r", t=PACK))
        nc.sync.dma_start(out=wt_sb[:], in_=wt[0].rearrange("(p j) o -> p (j o)", j=PACK))
        y_view = y[0].rearrange("(p j) n -> p j n", j=PACK)
        y_sb = [keep.tile([P, 2, N], F32, name=f"y_sb{u}") for u in range(PAIRS)]
        for u in range(PAIRS):
            nc.sync.dma_start(out=y_sb[u][:], in_=y_view[:, 2 * u:2 * u + 2, :])
        xm_view = xm[0].rearrange("(p j) d -> p j d", j=PACK)
        xm_first = keep.tile([P, PACK, P], F32, name="xm_first")
        nc.sync.dma_start(out=xm_first[:], in_=xm_view[:, :, 0:P])
        xm_rest = keep.tile([P, PACK, D - P], F32, name="xm_rest", tag="xm_rest", align_bytes=64)
        nc.sync.dma_start(out=xm_rest[:], in_=xm_view[:, :, P:])

        windows = [keep.tile([P, T], F32, name=f"window{m}") for m in range(TILES)]
        for win in windows:
            nc.vector.memset(win[:].bitcast(I32), 0)

        warm_in = keep.tile([P, 1], F32, name="warm_in")
        warm_out = keep.tile([P, 1], F32, name="warm_out")
        nc.gpsimd.memset(warm_in[:], 0.0)
        nc.scalar.activation(out=warm_out[:], in_=warm_in[:], func=ACT.Abs_reciprocal_sqrt, bias=1.0)

        halves = [slice(h * NH, (h + 1) * NH) for h in range(HALVES)]
        pairs = [slice(2 * u, 2 * u + 2) for u in range(PAIRS)]

        def half_offsets(h):
            return offsets[:, h * NH // 16:(h + 1) * NH // 16]

        w_grouped = keep.tile([P, N, PACK], BF16, name="w_grouped", align_bytes=64)
        w_codes = keep.tile([P, N], U32, name="w_codes", align_bytes=64)
        w_scales = keep.tile([P, N], U8, name="w_scales", align_bytes=64)
        low_listed = keep.tile([P, 2, N], F32, name="low_listed")
        for t in range(2):
            nc.scalar.activation(out=low_listed[:, t, :], in_=planes[t][:].indirect(offsets[:]), func=ACT.Copy)
        nc.scalar.copy(out=w_grouped[:, :, 0:2], in_=low_listed[:].rearrange("p t n -> p n t"))
        high_listed = keep.tile([P, 2, NH], F32, name="high_listed")
        nc.vector.tensor_copy(out=w_grouped[:, halves[0], 2], in_=planes[2][:].indirect(half_offsets(0)))
        nc.vector.tensor_copy(out=high_listed[:, 0, :], in_=planes[2][:].indirect(half_offsets(1)))
        nc.vector.tensor_copy(out=w_grouped[:, halves[0], 3], in_=planes[3][:].indirect(half_offsets(0)))
        nc.scalar.activation(out=high_listed[:, 1, :], in_=planes[3][:].indirect(half_offsets(1)), func=ACT.Copy)
        nc.scalar.copy(out=w_grouped[:, halves[1], 2:4], in_=high_listed[:].rearrange("p t n -> p n t"))
        for cols in halves:
            nc.vector.quantize_mx(out=w_codes[:, cols].bitcast(E4M3), scales=w_scales[:, cols],
                                  in_=w_grouped[:, cols, :].rearrange("p n t -> p (n t)"))

        x_codes = keep.tile([P, R], U32, name="x_codes", align_bytes=64)
        x_scales = keep.tile([P, R], U8, name="x_scales", align_bytes=64)

        def weave_x(u, cut):
            grouped = keep.tile([P, 2, P, PACK], BF16, name=f"x_grouped{u}", align_bytes=64)
            woven = grouped[:].rearrange("p e (c i) t -> p c t i e", i=2)
            source = x_raw[:].rearrange("p t (c i j) -> p c t i j", i=2, j=PACK)[:, :, :, :, pairs[u]]
            nc.vector.tensor_copy(out=woven[:, 0:cut], in_=source[:, 0:cut])
            nc.scalar.copy(out=woven[:, cut:P // 2], in_=source[:, cut:P // 2])
            return grouped

        x_grouped = [weave_x(u, cut) for u, cut in enumerate(X_CUTS)]
        for u, first, count in ((0, 0, 1), (0, 1, 1), (1, 0, 2)):
            cols = slice((2 * u + first) * P, (2 * u + first + count) * P)
            nc.vector.quantize_mx(out=x_codes[:, cols].bitcast(E4M3), scales=x_scales[:, cols],
                                  in_=x_grouped[u][:, first:first + count].rearrange("p e s t -> p (e s t)"))

        wt_safe = keep.tile([P, PACK], F32, name="wt_safe")
        wt_inv = keep.tile([P, PACK], F32, name="wt_inv")
        nc.vector.scalar_tensor_tensor(out=wt_safe[:], in0=wt_sb[:], scalar=0.0, in1=wt_sb[:],
                                       op0=ALU.is_equal, op1=ALU.add)
        nc.vector.reciprocal(out=wt_inv[:], in_=wt_safe[:])

        y_weighed = {j: keep.tile([P, NH], F32, name=f"y_weighed{j}") for j in range(1, PACK)}
        nc.scalar.activation(out=y_weighed[1][:], in_=y_sb[0][:, 1, halves[1]], func=ACT.Copy, scale=wt_sb[:, 1:2])
        for j in range(2, PACK):
            nc.gpsimd.tensor_scalar(out=y_weighed[j][:], in0=y_sb[1][:, j - 2, halves[1]],
                                    scalar1=wt_sb[:, j:j + 1], scalar2=0.0, op0=ALU.mult, op1=ALU.add)
        xm0 = keep.tile([P, P, PACK], BF16, name="xm_grouped0", align_bytes=64)
        nc.gpsimd.tensor_scalar(out=xm0[:], in0=xm_first[:].rearrange("p j d -> p d j"),
                                scalar1=1.0, scalar2=0.0, op0=ALU.mult, op1=ALU.add)

        def scores(bank, j, cols):
            rows = slice(j * P, (j + 1) * P)
            nc.tensor.matmul_mx(out=bank, lhsT=x_codes[:, rows].bitcast(E4M3), lhsT_scale=x_scales[:, rows],
                                rhs=w_codes[:, cols].bitcast(E4M3), rhs_scale=w_scales[:, cols], start=True, stop=True)

        def square(dst, src, scale=1.0):
            nc.scalar.activation(out=dst, in_=src, func=ACT.Square, scale=scale)

        def inverse_root(dst, src):
            nc.scalar.activation(out=dst, in_=src, func=ACT.Abs_reciprocal_sqrt, bias=1.0)

        g_codes = keep.tile([P, N], U32, name="g_codes", align_bytes=64)
        g_scales = keep.tile([P, N], U8, name="g_scales", align_bytes=64)
        xm_scales = keep.tile([P, D], U8, name="xm_scales", align_bytes=64)
        xm_codes = {m: keep.tile([P, P], U32, name=f"xm_codes{m}", align_bytes=64) for m in (0, 1, 3)}

        def gradient(first, count, left, right):
            grouped = keep.tile([P, count, PACK], BF16, name=f"g_grouped{first}", tag=f"g_grouped{first}",
                                align_bytes=64)
            nc.vector.tensor_tensor(
                out=grouped[:].rearrange("p (c i) j -> p c j i", i=2),
                in0=left.rearrange("p j (c i) -> p c j i", i=2),
                in1=right.rearrange("p j (c i) -> p c j i", i=2), op=ALU.mult)
            return grouped

        def quantize_g(grouped, first, count):
            cols = slice(first, first + count)
            nc.vector.quantize_mx(out=g_codes[:, cols].bitcast(E5M2), scales=g_scales[:, cols],
                                  in_=grouped[:].rearrange("p n j -> p (n j)"))

        def weave_xm(m, count, tag):
            grouped = keep.tile([P, count * P, PACK], BF16, name=f"xm_grouped{m}", tag=tag, align_bytes=64)
            source = xm_rest[:, :, (m - 1) * P:(m - 1 + count) * P]
            nc.vector.tensor_copy(out=grouped[:].rearrange("p (c i) j -> p c j i", i=4),
                                  in_=source.rearrange("p j (c i) -> p c j i", i=4))
            return grouped

        def quantize_xm(grouped, m):
            nc.vector.quantize_mx(out=xm_codes[m][:].bitcast(E4M3), scales=xm_scales[:, m * P:(m + 1) * P],
                                  in_=grouped[:].rearrange("p d j -> p (d j)"))

        def product(acc, m, cols):
            rows = slice(m * P, (m + 1) * P)
            nc.tensor.matmul_mx(out=acc, lhsT=xm_codes[m][:].bitcast(E4M3), lhsT_scale=xm_scales[:, rows],
                                rhs=g_codes[:, cols].bitcast(E5M2), rhs_scale=g_scales[:, cols],
                                start=True, stop=True)

        def lone_product(m, cols, bank_tag):
            acc = psum.tile([P, cols.stop - cols.start], F32, name=f"acc{m}_{cols.start}", tag=bank_tag)
            product(acc[:], m, cols)
            return acc

        def scatter_on_scalar(m, h, dw):
            nc.scalar.activation(out=windows[m][:].indirect(half_offsets(h)), in_=dw, func=ACT.Copy)

        def store(m):
            nc.sync.dma_start(out=out[m * P:(m + 1) * P, :], in_=windows[m][:])

        chunks = [slice(c * CH, (c + 1) * CH) for c in range(NH // CH)]
        q = [keep.tile([P, NH], F32, name=f"q{j}", tag=f"q{j}", align_bytes=64) for j in range(PACK)]
        for c, cols in enumerate(chunks):
            bank = psum.tile([P, CH], F32, name=f"scores_first{c}", tag=f"bank{6 * c}")
            scores(bank[:], 0, cols)
            nc.vector.tensor_tensor(out=q[0][:, cols], in0=bank[:], in1=y_sb[0][:, 0, cols], op=ALU.subtract)
        for j in range(1, PACK):
            bank = psum.tile([P, NH], F32, name=f"scores_first_tile{j}", tag=f"bank{j}")
            scores(bank[:], j, halves[0])
            nc.vector.tensor_tensor(out=q[j][:], in0=bank[:], in1=y_sb[j // 2][:, j % 2, halves[0]], op=ALU.subtract)
        second_scores = []
        for j, number in enumerate((4, 7, 5, 0)):
            second_scores.append(psum.tile([P, NH], F32, name=f"scores_second{j}", tag=f"bank{number}"))
            scores(second_scores[j][:], j, halves[1])

        sq0 = [keep.tile([P, NH], F32, name=f"sq0_{j}", tag="sq1" if j == 2 else f"sq0_{j}") for j in range(PACK)]
        root0 = keep.tile([P, PACK, NH], F32, name="root0", tag="root0", align_bytes=64)
        left0 = keep.tile([P, PACK, NH], F32, name="left0", tag="left0", align_bytes=64)
        for cols in chunks:
            square(sq0[0][:, cols], q[0][:, cols])
        square(sq0[1][:], q[1][:])
        for j in range(2):
            inverse_root(root0[:, j, :], sq0[j][:])
        for j in range(2, PACK):
            square(sq0[j][:], q[j][:])
        for j in range(2, PACK):
            inverse_root(root0[:, j, :], sq0[j][:])

        def weigh(j):
            nc.vector.scalar_tensor_tensor(out=left0[:, j, :], in0=q[j][:], scalar=wt_sb[:, j:j + 1],
                                           in1=root0[:, j, :], op0=ALU.mult, op1=ALU.mult)

        left1 = keep.tile([P, PACK, NH], F32, name="left1", tag="left1", align_bytes=64)
        q_second = keep.tile([P, NH], F32, name="q_second")
        nc.vector.tensor_tensor(out=q_second[:], in0=second_scores[0][:], in1=y_sb[0][:, 0, halves[1]],
                                op=ALU.subtract)
        for j in range(1, PACK):
            nc.vector.scalar_tensor_tensor(out=left1[:, j, :], in0=second_scores[j][:],
                                           scalar=wt_sb[:, j:j + 1], in1=y_weighed[j][:],
                                           op0=ALU.mult, op1=ALU.subtract)

        sq1 = keep.tile([P, PACK, NH], F32, name="sq1", tag="sq1")
        damping1 = keep.tile([P, NH // CH, PACK, CH], F32, name="damping1", tag="damping1")
        square(sq1[:, 0, :], q_second[:])
        square(sq1[:, 1, :], left1[:, 1, :], wt_inv[:, 1:2])
        for j in range(2, PACK):
            square(sq1[:, j, :], left1[:, j, :], wt_inv[:, j:j + 1])
        inverse_root(damping1[:, :, 0, :], sq1[:, 0, :].rearrange("p (c n) -> p c n", n=CH))
        roots = []
        for c, cols in enumerate(chunks):
            roots.append(keep.tile([P, PACK - 1, CH], F32, name=f"root1_{c}"))
            inverse_root(roots[c][:], sq1[:, 1:, cols])
        for c, cols in enumerate(chunks):
            square(damping1[:, c, 1:, :], roots[c][:])

        for j in range(PACK):
            weigh(j)
        quantize_xm(xm0, 0)
        g_first = gradient(0, NH, left0[:], root0[:])
        nc.vector.scalar_tensor_tensor(out=left1[:, 0, :].rearrange("p (c n) -> p c n", n=CH),
                                       in0=q_second[:].rearrange("p (c n) -> p c n", n=CH), scalar=wt_sb[:, 0:1],
                                       in1=damping1[:, :, 0, :], op0=ALU.mult, op1=ALU.mult)
        quantize_g(g_first, 0, NH)
        xm1 = weave_xm(1, 1, "root0")

        dw0 = keep.tile([P, NH], F32, name="dw0_first", tag="sq1")
        nc.scalar.copy(out=dw0[:], in_=lone_product(0, halves[0], "bank7")[:])
        scatter_on_scalar(0, 0, dw0[:])

        g_second = {NH: gradient(NH, CH, left1[:, :, chunks[0]], damping1[:, 0])}
        quantize_xm(xm1, 1)
        early1 = lone_product(1, halves[0], "bank6")
        g_second[NH + CH] = gradient(NH + CH, CH, left1[:, :, chunks[1]], damping1[:, 1])
        for first in (NH, NH + CH):
            quantize_g(g_second[first], first, CH)
        xm2 = weave_xm(2, 1, f"g_grouped{NH}")
        xm3 = keep.tile([P, P, PACK], BF16, name="xm_grouped3", tag=f"g_grouped{NH + CH}", align_bytes=64)
        nc.gpsimd.tensor_scalar(out=xm3[:], in0=xm_rest[:, :, 2 * P:].rearrange("p j d -> p d j"),
                                scalar1=1.0, scalar2=0.0, op0=ALU.mult, op1=ALU.add)
        dw1 = keep.tile([P, N], F32, name="dw1", tag="damping1")
        nc.vector.tensor_copy(out=dw1[:, halves[0]], in_=early1[:])
        dw0_second = keep.tile([P, NH], F32, name="dw0_second")
        dw2 = [keep.tile([P, NH], F32, name=f"dw2_{h}") for h in range(HALVES)]
        late = [lone_product(0, slice(NH + cols.start, NH + cols.stop), f"bank{c}") for c, cols in enumerate(chunks)]
        for c, cols in enumerate(chunks):
            nc.vector.tensor_copy(out=dw0_second[:, cols], in_=late[c][:])
        scatter_on_scalar(0, 1, dw0_second[:])
        store(0)
        nc.vector.tensor_copy(out=dw1[:, halves[1]], in_=lone_product(1, halves[1], "bank4")[:])
        xm_codes[2] = keep.tile([P, P], U32, name="xm_codes2", tag="xm_rest", align_bytes=64)
        quantize_xm(xm2, 2)
        quantize_xm(xm3, 3)
        nc.vector.tensor_copy(out=windows[1][:].indirect(offsets[:]), in_=dw1[:])
        store(1)

        whole2 = lone_product(2, slice(0, N), "bank1")
        for h in range(HALVES):
            nc.scalar.copy(out=dw2[h][:], in_=whole2[:, halves[h]])
        for h in range(HALVES):
            scatter_on_scalar(2, h, dw2[h][:])
        store(2)
        dw3 = keep.tile([P, N], F32, name="dw3")
        nc.vector.tensor_copy(out=dw3[:], in_=lone_product(3, slice(0, N), "bank0")[:])
        nc.vector.tensor_copy(out=windows[3][:].indirect(offsets[:]), in_=dw3[:])
        store(3)
